import numpy as np
import ml_dtypes


def mxq(x, axis, fmt="e4m3"):
    dtype, down = {"e4m3": (ml_dtypes.float8_e4m3fn, 7), "e5m2": (ml_dtypes.float8_e5m2, 14)}[fmt]
    v = np.moveaxis(np.asarray(x, np.float32).astype(ml_dtypes.bfloat16).astype(np.float64), axis, -1)
    blocks = v.reshape(v.shape[:-1] + (-1, 32))
    amax = np.abs(blocks).max(-1, keepdims=True)
    byte = np.maximum(np.where(amax > 0, np.frexp(amax)[1] - 1 + 127, 0) - down, 1)
    scale = np.exp2(byte - 127.0)
    codes = (blocks / scale).astype(np.float32).astype(dtype).astype(np.float64)
    return np.moveaxis((codes * scale).reshape(v.shape), -1, axis)


WIDE = False


def mx_kscale(k):
    if not WIDE:
        return np.ones(k)
    levels = np.array([10, -10, 5, -5, 0])
    if k % 512:
        return np.exp2(np.random.permutation(np.resize(levels, k // 32))).repeat(32)
    a = np.empty((k // 512, 16))
    for p in range(k // 512):
        a[p, :8] = np.random.permutation(np.resize(levels, 8))
        for g in range(8):
            far = levels[np.abs(levels - a[p, g]) >= 10]
            a[p, g + 8] = far[np.random.randint(len(far))]
    return np.exp2(a.ravel()).repeat(32)


def f64(x):
    return np.asarray(x).astype(np.float64)


def striped(idx):
    return np.tile(idx.reshape(-1, 16).T, (8, 1)).astype(np.uint16)


def unstriped(offs):
    return offs[:16].T.reshape(-1).astype(np.int64)


def striped8(idx):
    return np.concatenate([x.reshape(-1, 16).T for x in idx]).astype(np.uint16)


def runs(offs, k):
    lists = np.stack([offs[16 * r : 16 * r + 16].T.reshape(-1) for r in range(8)]).astype(np.int64)
    return lists[np.arange(k) % 512 // 64]


def pack_weight(w):
    k, n = w.shape
    w = f64(np.asarray(w, np.float32).astype(ml_dtypes.bfloat16)).reshape(k // 32, 32, n)
    amax = np.abs(w).max(1)
    byte = np.clip(np.where(amax > 0, np.frexp(amax)[1] - 1 + 127 - 7, 1), 1, 254)
    scaled = (w * np.exp2(127.0 - byte)[:, None, :]).reshape(k, n).astype(np.float32)
    words = np.ascontiguousarray(scaled.reshape(k // 512, 128, 4, n).transpose(0, 1, 3, 2)).astype(ml_dtypes.float8_e4m3fn).view(np.uint8)
    return words, np.ascontiguousarray(byte.astype(np.uint8).reshape(k // 512, 16, n))


def unpack_weight(words, scales):
    g, p, n, _ = words.shape
    vals = np.ascontiguousarray(words).view(ml_dtypes.float8_e4m3fn).astype(np.float64) * np.repeat(np.exp2(scales.astype(np.float64) - 127.0), 8, axis=1)[..., None]
    return vals.transpose(0, 1, 3, 2).reshape(g * 512, n)


def silu(v):
    return v / (1.0 + np.exp(-np.maximum(v, -700.0)))


K, T, S, N, H, U = 512, 2048, 512, 512, 512, 512


def setup_inputs():
    n = np.random.standard_normal
    s = mx_kscale(K)[:, None]
    u = mx_kscale(H)
    packed_xT = pack_weight(n((K, T)) * s)
    return {
        "x_words": packed_xT[0],
        "x_scales": packed_xT[1],
        "w1": (n((K, H)) / np.sqrt(K) / s * u).astype(np.float32),
        "w2": (n((K, H)) / np.sqrt(K) / s * u).astype(np.float32),
        "w3": (n((H, N)) / np.sqrt(H) / u[:, None]).astype(np.float32),
        "w4": (n((H, N)) / np.sqrt(H) / u[:, None]).astype(np.float32),
        "mix": np.random.uniform(0.0, 1.0, (N, U)).astype(np.float32),
        "offs": striped(np.random.permutation(T)[:S]),
        "task": striped8(np.random.randint(0, U, (8, S))),
    }


def reference(x_words, x_scales, w1, w2, w3, w4, mix, offs, task):
    xq = unpack_weight(x_words, x_scales)[:, unstriped(offs)]
    z2 = silu(mxq(f64(w2), 0, "e4m3").T @ xq)
    b = mxq(f64(w4), 0, "e4m3").T @ mxq(z2, 0, "e4m3")
    q = f64(mix)[np.arange(N)[:, None], runs(task, N)]
    z = silu(mxq(f64(w1), 0, "e4m3").T @ xq)
    a = mxq(f64(w3), 0, "e4m3").T @ mxq(z, 0, "e4m3")
    return b + q * (a - b)

@@ -1,0 +1,194 @@
+from contextlib import ExitStack
+
+import concourse.mybir as mybir
+
+K, T, S, N, H, U = 512, 2048, 512, 512, 512, 512
+FLOPS = 4 * 2 * 512 * 512 * 512
+
+F32 = mybir.dt.float32
+BF16 = mybir.dt.bfloat16
+I32 = mybir.dt.int32
+U32 = mybir.dt.uint32
+U16 = mybir.dt.uint16
+U8 = mybir.dt.uint8
+FP8X4 = mybir.dt.float8_e4m3fn_x4
+ACT = mybir.ActivationFunctionType
+ALU = mybir.AluOpType
+
+P = 128
+PACK = 4
+HALF = 256
+
+
+def tile_picked_expertpair_silu_p_kernel(
+    tc, x_words, x_scales, w1, w2, w3, w4, mix, offs, task, out
+):
+    nc = tc.nc
+    with ExitStack() as ctx:
+        keep = ctx.enter_context(tc.tile_pool(name="keep", bufs=1))
+        psum = ctx.enter_context(tc.psum_pool(name="psum", bufs=1))
+
+        def sb(name, shape, dtype):
+            return keep.tile(shape, dtype, name=name, align_bytes=64)
+
+        task_sb = sb("task_sb", [P, S // 16], U16)
+        offs_sb = sb("offs_sb", [P, S // 16], U16)
+        xw = sb("xw", [P, T], U32)
+        xs = sb("xs", [P, T], U8)
+        mix_rows = mix.rearrange("(p t) u -> p t u", t=PACK)
+        out_rows = out.rearrange("(p t) j -> p t j", t=PACK)
+        mix_sb = [sb("mix%d" % t, [P, U], F32) for t in range(PACK)]
+        share = [sb("share%d" % t, [P, S], F32) for t in range(PACK - 1)]
+        raw = {}
+        wbf = {}
+        wcodes = {}
+        wscales = {}
+        for name in ("w1", "w2", "w3", "w4"):
+            raw[name] = [sb("%s_raw%d" % (name, h), [P, PACK, HALF], F32) for h in range(2)]
+            wbf[name] = sb("%s_bf" % name, [P, PACK * 512], BF16)
+            wcodes[name] = sb("%s_codes" % name, [P, 512], U32)
+            wscales[name] = sb("%s_scales" % name, [P, 512], U8)
+        dram = {"w1": w1, "w2": w2, "w3": w3, "w4": w4}
+
+        def load_mix(t):
+            nc.sync.dma_start(out=mix_sb[t][:], in_=mix_rows[:, t, :])
+
+        def load_w(name):
+            rows = dram[name].rearrange("(p j) c -> p j c", j=PACK)
+            for h in range(2):
+                nc.sync.dma_start(out=raw[name][h][:], in_=rows[:, :, h * HALF : (h + 1) * HALF])
+
+        def cast_views(name, h):
+            dst = wbf[name][:].rearrange("p (t m j) -> p m t j", t=PACK, j=PACK)[:, h * 64 : (h + 1) * 64]
+            src = raw[name][h][:].rearrange("p j (m t) -> p m t j", t=PACK)
+            return dst, src
+
+        def cast_v(name, h, sign):
+            dst, src = cast_views(name, h)
+            nc.vector.tensor_scalar(dst, src, sign, None, ALU.mult)
+
+        def cast_s(name, h, sign):
+            dst, src = cast_views(name, h)
+            nc.scalar.activation(dst, src, ACT.Copy, scale=sign)
+
+        def quantize(codes, scales, src, lo, hi):
+            nc.vector.quantize_mx(
+                out=codes[:, lo:hi].bitcast(FP8X4), scales=scales[:, lo:hi], in_=src[:, PACK * lo : PACK * hi]
+            )
+
+        def quant_w(name, lo=0, hi=512):
+            quantize(wcodes[name], wscales[name], wbf[name], lo, hi)
+
+        def gather_share(t):
+            for h in range(2):
+                nc.vector.tensor_copy(
+                    share[t][:, h * HALF : (h + 1) * HALF], mix_sb[t][:].indirect(task_sb[:, h * 16 : (h + 1) * 16])
+                )
+
+        warm = sb("warm", [P, 8], F32)
+        nc.vector.memset(warm[:], 0.0)
+        nc.vector.memset(xs[:].bitcast(I32), 0)
+        nc.sync.dma_start(task_sb[:], task)
+        load_mix(0)
+        nc.sync.dma_start(offs_sb[:], offs)
+        for q in range(4):
+            nc.scalar.dma_start(out=xs[32 * q : 32 * q + 4, :].bitcast(I32), in_=x_scales[0, 4 * q : 4 * q + 4, :].bitcast(I32))
+        warm_out = sb("warm_out", [P, 8], F32)
+        nc.scalar.activation(warm_out[:], warm[:], ACT.Silu)
+        load_mix(1)
+        load_mix(2)
+        nc.sync.dma_start(out=xw[:].bitcast(I32), in_=x_words[0].rearrange("p n t -> p (n t)").bitcast(I32))
+        load_w("w2")
+        load_w("w1")
+        load_w("w4")
+        load_mix(3)
+        load_w("w3")
+
+        for t in range(3):
+            gather_share(t)
+        xg = sb("xg", [P, S], U32)
+        sg = sb("sg", [P, S], U8)
+        nc.vector.tensor_copy(xg[:], xw[:].indirect(offs_sb[:]))
+        nc.vector.tensor_copy(sg[:], xs[:].indirect(offs_sb[:]))
+
+        zbf = {}
+        zcodes = {}
+        zscales = {}
+        for name in ("w2", "w1"):
+            zbf[name] = sb("z_bf_" + name, [P, PACK * S], BF16)
+            zcodes[name] = sb("z_codes_" + name, [P, S], U32)
+            zscales[name] = sb("z_scales_" + name, [P, S], U8)
+
+        def hidden(name, tag):
+            for c in range(4):
+                cols = slice(c * P, (c + 1) * P)
+                bank = psum.tile([P, PACK, P], F32, name="h_%s_%d" % (name, c), tag="%s%d" % (tag, c))
+                for t in range(PACK):
+                    wc = slice(t * P, (t + 1) * P)
+                    nc.tensor.matmul_mx(
+                        out=bank[:, t, :],
+                        lhsT=wcodes[name][:, wc].bitcast(FP8X4),
+                        lhsT_scale=wscales[name][:, wc],
+                        rhs=xg[:, cols].bitcast(FP8X4),
+                        rhs_scale=sg[:, cols],
+                        start=True,
+                        stop=True,
+                    )
+                nc.scalar.activation(
+                    zbf[name][:, PACK * c * P : PACK * (c + 1) * P].rearrange("p (n t) -> p n t", t=PACK),
+                    bank[:].rearrange("p t n -> p n t"),
+                    ACT.Silu,
+                )
+
+        def second(bank, wname, zname, t, start, stop):
+            wc = slice(t * P, (t + 1) * P)
+            nc.tensor.matmul_mx(
+                out=bank[:],
+                lhsT=wcodes[wname][:, wc].bitcast(FP8X4),
+                lhsT_scale=wscales[wname][:, wc],
+                rhs=zcodes[zname][:].bitcast(FP8X4),
+                rhs_scale=zscales[zname][:],
+                start=start,
+                stop=stop,
+            )
+
+        cast_s("w2", 0, 1.0)
+        cast_v("w2", 1, 1.0)
+        quant_w("w2")
+        cast_s("w1", 0, 1.0)
+        hidden("w2", "A")
+        cast_v("w1", 1, 1.0)
+        quant_w("w1")
+        hidden("w1", "B")
+        cast_v("w4", 0, 1.0)
+        cast_v("w4", 1, 1.0)
+        quant_w("w4")
+        quantize(zcodes["w2"], zscales["w2"], zbf["w2"], 0, S)
+        b_bank = [psum.tile([P, S], F32, name="b%d" % t, tag="B%d" % t) for t in range(PACK)]
+        d_bank = [psum.tile([P, S], F32, name="d%d" % t, tag="A%d" % t) for t in range(PACK)]
+        for t in range(PACK):
+            second(d_bank[t], "w4", "w2", t, True, False)
+        for t in range(PACK):
+            second(b_bank[t], "w4", "w2", t, True, True)
+        share.append(keep.tile([P, S], F32, name="share3", tag="z_bf_w2", align_bytes=64))
+        gather_share(3)
+        cast_s("w3", 0, -1.0)
+        cast_s("w3", 1, -1.0)
+        quantize(zcodes["w1"], zscales["w1"], zbf["w1"], 0, S)
+        for t in range(PACK):
+            quant_w("w3", t * P, (t + 1) * P)
+            second(d_bank[t], "w3", "w1", t, False, True)
+
+        e = [sb("e%d" % t, [P, S], F32) for t in range(PACK)]
+        res = [sb("res%d" % t, [P, S], F32) for t in range(PACK)]
+        b_sb = [sb("b_sb%d" % t, [P, S], F32) for t in range(2)]
+        for t in range(2):
+            nc.scalar.copy(b_sb[t][:], b_bank[t][:])
+        for t in range(PACK):
+            nc.vector.tensor_tensor(e[t][:], d_bank[t][:], share[t][:], ALU.mult)
+        for t in range(2):
+            nc.gpsimd.tensor_tensor(res[t][:], b_sb[t][:], e[t][:], ALU.subtract)
+            nc.scalar.dma_start(out=out_rows[:, t, :], in_=res[t][:])
+        for t in range(2, PACK):
+            nc.vector.tensor_tensor(res[t][:], b_bank[t][:], e[t][:], ALU.subtract)
+            nc.sync.dma_start(out=out_rows[:, t, :], in_=res[t][:])

@@ -44,7 +44,7 @@ def tile_picked_expertpair_silu_p_kernel(
         wcodes = {}
         wscales = {}
         for name in ("w1", "w2", "w3", "w4"):
-            raw[name] = [sb("%s_raw%d" % (name, h), [P, PACK, HALF], F32) for h in range(2)]
+            raw[name] = sb("%s_raw" % name, [P, PACK, 512], F32)
             wbf[name] = sb("%s_bf" % name, [P, PACK * 512], BF16)
             wcodes[name] = sb("%s_codes" % name, [P, 512], U32)
             wscales[name] = sb("%s_scales" % name, [P, 512], U8)
@@ -55,12 +55,11 @@ def tile_picked_expertpair_silu_p_kernel(
 
         def load_w(name):
             rows = dram[name].rearrange("(p j) c -> p j c", j=PACK)
-            for h in range(2):
-                nc.sync.dma_start(out=raw[name][h][:], in_=rows[:, :, h * HALF : (h + 1) * HALF])
+            nc.sync.dma_start(out=raw[name][:], in_=rows)
 
         def cast_views(name, h):
-            dst = wbf[name][:].rearrange("p (t m j) -> p m t j", t=PACK, j=PACK)[:, h * 64 : (h + 1) * 64]
-            src = raw[name][h][:].rearrange("p j (m t) -> p m t j", t=PACK)
+            dst = wbf[name][:].rearrange("p (t m j) -> p m t j", t=PACK, j=PACK)[:, h[0] : h[1]]
+            src = raw[name][:].rearrange("p j (m t) -> p m t j", t=PACK)[:, h[0] : h[1]]
             return dst, src
 
         def cast_v(name, h, sign):
@@ -101,8 +100,8 @@ def tile_picked_expertpair_silu_p_kernel(
         load_w("w2")
         load_w("w1")
         load_w("w4")
-        load_mix(3)
         load_w("w3")
+        load_mix(3)
 
         for t in range(3):
             gather_share(t)
@@ -116,7 +115,6 @@ def tile_picked_expertpair_silu_p_kernel(
         zscales = {}
         for name in ("w2", "w1"):
             zbf[name] = sb("z_bf_" + name, [P, PACK * S], BF16)
-            zcodes[name] = sb("z_codes_" + name, [P, S], U32)
             zscales[name] = sb("z_scales_" + name, [P, S], U8)
 
         def hidden(name, tag):
@@ -152,43 +150,57 @@ def tile_picked_expertpair_silu_p_kernel(
                 stop=stop,
             )
 
-        cast_s("w2", 0, 1.0)
-        cast_v("w2", 1, 1.0)
+        cast_s("w2", (0, 84), 1.0)
+        cast_v("w2", (84, 128), 1.0)
         quant_w("w2")
-        cast_s("w1", 0, 1.0)
+        cast_s("w1", (0, 40), 1.0)
         hidden("w2", "A")
-        cast_v("w1", 1, 1.0)
+        cast_v("w1", (40, 128), 1.0)
         quant_w("w1")
         hidden("w1", "B")
-        cast_v("w4", 0, 1.0)
-        cast_v("w4", 1, 1.0)
-        quant_w("w4")
+        cast_v("w4", (0, 128), 1.0)
+        zcodes["w2"] = sb("z_codes_w2", [P, S], U32)
         quantize(zcodes["w2"], zscales["w2"], zbf["w2"], 0, S)
-        b_bank = [psum.tile([P, S], F32, name="b%d" % t, tag="B%d" % t) for t in range(PACK)]
+        quant_w("w4")
+        b_bank = [psum.tile([P, S], F32, name="b%d" % t, tag="B%d" % t) for t in range(2)]
         d_bank = [psum.tile([P, S], F32, name="d%d" % t, tag="A%d" % t) for t in range(PACK)]
         for t in range(PACK):
             second(d_bank[t], "w4", "w2", t, True, False)
-        for t in range(PACK):
+        for t in range(2):
             second(b_bank[t], "w4", "w2", t, True, True)
-        share.append(keep.tile([P, S], F32, name="share3", tag="z_bf_w2", align_bytes=64))
-        gather_share(3)
-        cast_s("w3", 0, -1.0)
-        cast_s("w3", 1, -1.0)
+        cast_v("w3", (56, 128), -1.0)
+        cast_s("w3", (0, 56), -1.0)
+        last_share = [sb("share3a", [P, HALF], F32)]
+        nc.vector.tensor_copy(last_share[0][:], mix_sb[3][:].indirect(task_sb[:, 0:16]))
+        zcodes["w1"] = sb("z_codes_w1", [P, S], U32)
         quantize(zcodes["w1"], zscales["w1"], zbf["w1"], 0, S)
         for t in range(PACK):
-            quant_w("w3", t * P, (t + 1) * P)
+            if t % 2 == 0:
+                quant_w("w3", t * P, (t + 2) * P)
             second(d_bank[t], "w3", "w1", t, False, True)
 
+        last_share.append(keep.tile([P, HALF], F32, name="share3b", tag="z_bf_w1", align_bytes=64))
+        nc.vector.tensor_copy(last_share[1][:], mix_sb[3][:].indirect(task_sb[:, 16:32]))
         e = [sb("e%d" % t, [P, S], F32) for t in range(PACK)]
-        res = [sb("res%d" % t, [P, S], F32) for t in range(PACK)]
+        res = [sb("res%d" % t, [P, S], F32) for t in range(PACK - 1)]
         b_sb = [sb("b_sb%d" % t, [P, S], F32) for t in range(2)]
         for t in range(2):
             nc.scalar.copy(b_sb[t][:], b_bank[t][:])
-        for t in range(PACK):
+        for t in range(PACK - 1):
             nc.vector.tensor_tensor(e[t][:], d_bank[t][:], share[t][:], ALU.mult)
+            if t < 2:
+                b_bank.append(psum.tile([P, S], F32, name="b%d" % (t + 2), tag="A%d" % t))
+                second(b_bank[t + 2], "w4", "w2", t + 2, True, True)
+        for h in range(2):
+            cols = slice(h * HALF, (h + 1) * HALF)
+            nc.vector.tensor_tensor(e[3][:, cols], d_bank[3][:, cols], last_share[h][:], ALU.mult)
         for t in range(2):
             nc.gpsimd.tensor_tensor(res[t][:], b_sb[t][:], e[t][:], ALU.subtract)
             nc.scalar.dma_start(out=out_rows[:, t, :], in_=res[t][:])
-        for t in range(2, PACK):
-            nc.vector.tensor_tensor(res[t][:], b_bank[t][:], e[t][:], ALU.subtract)
-            nc.sync.dma_start(out=out_rows[:, t, :], in_=res[t][:])
+        nc.vector.tensor_tensor(res[2][:], b_bank[2][:], e[2][:], ALU.subtract)
+        nc.sync.dma_start(out=out_rows[:, 2, :], in_=res[2][:])
+        for h in range(2):
+            cols = slice(h * HALF, (h + 1) * HALF)
+            last_res = sb("res3_%d" % h, [P, HALF], F32)
+            nc.vector.tensor_tensor(last_res[:], b_bank[3][:, cols], e[3][:, cols], ALU.subtract)
+            nc.sync.dma_start(out=out_rows[:, 3, cols], in_=last_res[:])

@@ -58,8 +58,8 @@ def tile_picked_expertpair_silu_p_kernel(
             nc.sync.dma_start(out=raw[name][:], in_=rows)
 
         def cast_views(name, h):
-            dst = wbf[name][:].rearrange("p (t m j) -> p m t j", t=PACK, j=PACK)[:, h[0] : h[1]]
-            src = raw[name][:].rearrange("p j (m t) -> p m t j", t=PACK)[:, h[0] : h[1]]
+            dst = wbf[name][:].rearrange("p (t m j) -> p m j t", t=PACK, j=PACK)[:, h[0] : h[1]]
+            src = raw[name][:].rearrange("p j (m t) -> p m j t", t=PACK)[:, h[0] : h[1]]
             return dst, src
 
         def cast_v(name, h, sign):

@@ -3,7 +3,7 @@ from contextlib import ExitStack
 import concourse.mybir as mybir
 
 K, T, S, N, H, U = 512, 2048, 512, 512, 512, 512
-FLOPS = 4 * 2 * 512 * 512 * 512
+FLOPS = 2 * (2 * K * H * S + 2 * H * N * S)
 
 F32 = mybir.dt.float32
 BF16 = mybir.dt.bfloat16
@@ -17,7 +17,12 @@ ALU = mybir.AluOpType
 
 P = 128
 PACK = 4
-HALF = 256
+GROUP = 16
+QUADRANT = 32
+ALL = slice(0, S)
+HALVES = (slice(0, S // 2), slice(S // 2, S))
+W3_ON_SCALAR = 56
+GPSIMD_SLOTS = 2
 
 
 def tile_picked_expertpair_silu_p_kernel(
@@ -28,179 +33,171 @@ def tile_picked_expertpair_silu_p_kernel(
         keep = ctx.enter_context(tc.tile_pool(name="keep", bufs=1))
         psum = ctx.enter_context(tc.psum_pool(name="psum", bufs=1))
 
-        def sb(name, shape, dtype):
-            return keep.tile(shape, dtype, name=name, align_bytes=64)
+        def sbuf(name, shape, dtype, tag=None):
+            return keep.tile(shape, dtype, name=name, tag=tag or name, align_bytes=64)
 
-        task_sb = sb("task_sb", [P, S // 16], U16)
-        offs_sb = sb("offs_sb", [P, S // 16], U16)
-        xw = sb("xw", [P, T], U32)
-        xs = sb("xs", [P, T], U8)
+        def entries(list_tile, cols):
+            return list_tile[:, cols.start // GROUP : cols.stop // GROUP]
+
+        task_sb = sbuf("task_sb", [P, S // GROUP], U16)
+        offs_sb = sbuf("offs_sb", [P, S // GROUP], U16)
+        table_words = sbuf("table_words", [P, T], U32)
+        table_scales = sbuf("table_scales", [P, T], U8)
         mix_rows = mix.rearrange("(p t) u -> p t u", t=PACK)
         out_rows = out.rearrange("(p t) j -> p t j", t=PACK)
-        mix_sb = [sb("mix%d" % t, [P, U], F32) for t in range(PACK)]
-        share = [sb("share%d" % t, [P, S], F32) for t in range(PACK - 1)]
-        raw = {}
-        wbf = {}
-        wcodes = {}
-        wscales = {}
-        for name in ("w1", "w2", "w3", "w4"):
-            raw[name] = sb("%s_raw" % name, [P, PACK, 512], F32)
-            wbf[name] = sb("%s_bf" % name, [P, PACK * 512], BF16)
-            wcodes[name] = sb("%s_codes" % name, [P, 512], U32)
-            wscales[name] = sb("%s_scales" % name, [P, 512], U8)
-        dram = {"w1": w1, "w2": w2, "w3": w3, "w4": w4}
+        mix_sb = [sbuf("mix%d" % t, [P, U], F32) for t in range(PACK)]
+        share = [sbuf("share%d" % t, [P, S], F32) for t in range(PACK - 1)]
+        weights = {"w1": w1, "w2": w2, "w3": w3, "w4": w4}
+        w_raw, w_bf16, w_codes, w_scales = {}, {}, {}, {}
+        for name in weights:
+            w_raw[name] = sbuf(name + "_raw", [P, PACK, H], F32)
+            w_bf16[name] = sbuf(name + "_bf16", [P, PACK * H], BF16)
+            w_codes[name] = sbuf(name + "_codes", [P, H], U32)
+            w_scales[name] = sbuf(name + "_scales", [P, H], U8)
 
         def load_mix(t):
             nc.sync.dma_start(out=mix_sb[t][:], in_=mix_rows[:, t, :])
 
-        def load_w(name):
-            rows = dram[name].rearrange("(p j) c -> p j c", j=PACK)
-            nc.sync.dma_start(out=raw[name][:], in_=rows)
+        def load_weight(name):
+            nc.sync.dma_start(out=w_raw[name][:], in_=weights[name].rearrange("(p j) c -> p j c", j=PACK))
 
-        def cast_views(name, h):
-            dst = wbf[name][:].rearrange("p (t m j) -> p m j t", t=PACK, j=PACK)[:, h[0] : h[1]]
-            src = raw[name][:].rearrange("p j (m t) -> p m j t", t=PACK)[:, h[0] : h[1]]
+        def rounding_views(name, lo, hi):
+            dst = w_bf16[name][:].rearrange("p (t m j) -> p m j t", t=PACK, j=PACK)[:, lo:hi]
+            src = w_raw[name][:].rearrange("p j (m t) -> p m j t", t=PACK)[:, lo:hi]
             return dst, src
 
-        def cast_v(name, h, sign):
-            dst, src = cast_views(name, h)
+        def round_on_vector(name, lo, hi, sign):
+            dst, src = rounding_views(name, lo, hi)
             nc.vector.tensor_scalar(dst, src, sign, None, ALU.mult)
 
-        def cast_s(name, h, sign):
-            dst, src = cast_views(name, h)
+        def round_on_scalar(name, lo, hi, sign):
+            dst, src = rounding_views(name, lo, hi)
             nc.scalar.activation(dst, src, ACT.Copy, scale=sign)
 
-        def quantize(codes, scales, src, lo, hi):
+        def quantize(codes, scales, values, cols):
             nc.vector.quantize_mx(
-                out=codes[:, lo:hi].bitcast(FP8X4), scales=scales[:, lo:hi], in_=src[:, PACK * lo : PACK * hi]
+                out=codes[:, cols].bitcast(FP8X4),
+                scales=scales[:, cols],
+                in_=values[:, PACK * cols.start : PACK * cols.stop],
             )
 
-        def quant_w(name, lo=0, hi=512):
-            quantize(wcodes[name], wscales[name], wbf[name], lo, hi)
+        def quantize_weight(name, cols):
+            quantize(w_codes[name], w_scales[name], w_bf16[name], cols)
 
-        def gather_share(t):
-            for h in range(2):
-                nc.vector.tensor_copy(
-                    share[t][:, h * HALF : (h + 1) * HALF], mix_sb[t][:].indirect(task_sb[:, h * 16 : (h + 1) * 16])
-                )
-
-        warm = sb("warm", [P, 8], F32)
-        nc.vector.memset(warm[:], 0.0)
-        nc.vector.memset(xs[:].bitcast(I32), 0)
-        nc.sync.dma_start(task_sb[:], task)
-        load_mix(0)
-        nc.sync.dma_start(offs_sb[:], offs)
-        for q in range(4):
-            nc.scalar.dma_start(out=xs[32 * q : 32 * q + 4, :].bitcast(I32), in_=x_scales[0, 4 * q : 4 * q + 4, :].bitcast(I32))
-        warm_out = sb("warm_out", [P, 8], F32)
-        nc.scalar.activation(warm_out[:], warm[:], ACT.Silu)
-        load_mix(1)
-        load_mix(2)
-        nc.sync.dma_start(out=xw[:].bitcast(I32), in_=x_words[0].rearrange("p n t -> p (n t)").bitcast(I32))
-        load_w("w2")
-        load_w("w1")
-        load_w("w4")
-        load_w("w3")
-        load_mix(3)
-
-        for t in range(3):
-            gather_share(t)
-        xg = sb("xg", [P, S], U32)
-        sg = sb("sg", [P, S], U8)
-        nc.vector.tensor_copy(xg[:], xw[:].indirect(offs_sb[:]))
-        nc.vector.tensor_copy(sg[:], xs[:].indirect(offs_sb[:]))
-
-        zbf = {}
-        zcodes = {}
-        zscales = {}
-        for name in ("w2", "w1"):
-            zbf[name] = sb("z_bf_" + name, [P, PACK * S], BF16)
-            zscales[name] = sb("z_scales_" + name, [P, S], U8)
-
-        def hidden(name, tag):
-            for c in range(4):
-                cols = slice(c * P, (c + 1) * P)
-                bank = psum.tile([P, PACK, P], F32, name="h_%s_%d" % (name, c), tag="%s%d" % (tag, c))
-                for t in range(PACK):
-                    wc = slice(t * P, (t + 1) * P)
-                    nc.tensor.matmul_mx(
-                        out=bank[:, t, :],
-                        lhsT=wcodes[name][:, wc].bitcast(FP8X4),
-                        lhsT_scale=wscales[name][:, wc],
-                        rhs=xg[:, cols].bitcast(FP8X4),
-                        rhs_scale=sg[:, cols],
-                        start=True,
-                        stop=True,
-                    )
-                nc.scalar.activation(
-                    zbf[name][:, PACK * c * P : PACK * (c + 1) * P].rearrange("p (n t) -> p n t", t=PACK),
-                    bank[:].rearrange("p t n -> p n t"),
-                    ACT.Silu,
-                )
-
-        def second(bank, wname, zname, t, start, stop):
-            wc = slice(t * P, (t + 1) * P)
+        def product(dst, name, t, codes, scales, start, stop):
+            cols = slice(t * P, (t + 1) * P)
             nc.tensor.matmul_mx(
-                out=bank[:],
-                lhsT=wcodes[wname][:, wc].bitcast(FP8X4),
-                lhsT_scale=wscales[wname][:, wc],
-                rhs=zcodes[zname][:].bitcast(FP8X4),
-                rhs_scale=zscales[zname][:],
+                out=dst,
+                lhsT=w_codes[name][:, cols].bitcast(FP8X4),
+                lhsT_scale=w_scales[name][:, cols],
+                rhs=codes.bitcast(FP8X4),
+                rhs_scale=scales,
                 start=start,
                 stop=stop,
             )
 
-        cast_s("w2", (0, 84), 1.0)
-        cast_v("w2", (84, 128), 1.0)
-        quant_w("w2")
-        cast_s("w1", (0, 40), 1.0)
-        hidden("w2", "A")
-        cast_v("w1", (40, 128), 1.0)
-        quant_w("w1")
-        hidden("w1", "B")
-        cast_v("w4", (0, 128), 1.0)
-        zcodes["w2"] = sb("z_codes_w2", [P, S], U32)
-        quantize(zcodes["w2"], zscales["w2"], zbf["w2"], 0, S)
-        quant_w("w4")
-        b_bank = [psum.tile([P, S], F32, name="b%d" % t, tag="B%d" % t) for t in range(2)]
-        d_bank = [psum.tile([P, S], F32, name="d%d" % t, tag="A%d" % t) for t in range(PACK)]
-        for t in range(PACK):
-            second(d_bank[t], "w4", "w2", t, True, False)
-        for t in range(2):
-            second(b_bank[t], "w4", "w2", t, True, True)
-        cast_v("w3", (56, 128), -1.0)
-        cast_s("w3", (0, 56), -1.0)
-        last_share = [sb("share3a", [P, HALF], F32)]
-        nc.vector.tensor_copy(last_share[0][:], mix_sb[3][:].indirect(task_sb[:, 0:16]))
-        zcodes["w1"] = sb("z_codes_w1", [P, S], U32)
-        quantize(zcodes["w1"], zscales["w1"], zbf["w1"], 0, S)
-        for t in range(PACK):
-            if t % 2 == 0:
-                quant_w("w3", t * P, (t + 2) * P)
-            second(d_bank[t], "w3", "w1", t, False, True)
+        warm_in = sbuf("warm_in", [P, 8], F32)
+        nc.vector.memset(warm_in[:], 0.0)
+        nc.vector.memset(table_scales[:].bitcast(I32), 0)
+        nc.sync.dma_start(task_sb[:], task)
+        load_mix(0)
+        nc.sync.dma_start(offs_sb[:], offs)
+        for q in range(P // QUADRANT):
+            nc.scalar.dma_start(
+                out=table_scales[QUADRANT * q : QUADRANT * q + PACK, :].bitcast(I32),
+                in_=x_scales[0, PACK * q : PACK * (q + 1), :].bitcast(I32),
+            )
+        warm_out = sbuf("warm_out", [P, 8], F32)
+        nc.scalar.activation(warm_out[:], warm_in[:], ACT.Silu)
+        load_mix(1)
+        load_mix(2)
+        load_weight("w2")
+        nc.sync.dma_start(out=table_words[:].bitcast(I32), in_=x_words[0].rearrange("p n t -> p (n t)").bitcast(I32))
+        load_weight("w1")
+        load_weight("w4")
+        load_weight("w3")
+        load_mix(PACK - 1)
 
-        last_share.append(keep.tile([P, HALF], F32, name="share3b", tag="z_bf_w1", align_bytes=64))
-        nc.vector.tensor_copy(last_share[1][:], mix_sb[3][:].indirect(task_sb[:, 16:32]))
-        e = [sb("e%d" % t, [P, S], F32) for t in range(PACK)]
-        res = [sb("res%d" % t, [P, S], F32) for t in range(PACK - 1)]
-        b_sb = [sb("b_sb%d" % t, [P, S], F32) for t in range(2)]
-        for t in range(2):
-            nc.scalar.copy(b_sb[t][:], b_bank[t][:])
         for t in range(PACK - 1):
-            nc.vector.tensor_tensor(e[t][:], d_bank[t][:], share[t][:], ALU.mult)
-            if t < 2:
-                b_bank.append(psum.tile([P, S], F32, name="b%d" % (t + 2), tag="A%d" % t))
-                second(b_bank[t + 2], "w4", "w2", t + 2, True, True)
-        for h in range(2):
-            cols = slice(h * HALF, (h + 1) * HALF)
-            nc.vector.tensor_tensor(e[3][:, cols], d_bank[3][:, cols], last_share[h][:], ALU.mult)
-        for t in range(2):
-            nc.gpsimd.tensor_tensor(res[t][:], b_sb[t][:], e[t][:], ALU.subtract)
-            nc.scalar.dma_start(out=out_rows[:, t, :], in_=res[t][:])
-        nc.vector.tensor_tensor(res[2][:], b_bank[2][:], e[2][:], ALU.subtract)
-        nc.sync.dma_start(out=out_rows[:, 2, :], in_=res[2][:])
-        for h in range(2):
-            cols = slice(h * HALF, (h + 1) * HALF)
-            last_res = sb("res3_%d" % h, [P, HALF], F32)
-            nc.vector.tensor_tensor(last_res[:], b_bank[3][:, cols], e[3][:, cols], ALU.subtract)
-            nc.sync.dma_start(out=out_rows[:, 3, cols], in_=last_res[:])
+            for cols in HALVES:
+                nc.vector.tensor_copy(share[t][:, cols], mix_sb[t][:].indirect(entries(task_sb, cols)))
+        x_codes = sbuf("x_codes", [P, S], U32)
+        x_bytes = sbuf("x_bytes", [P, S], U8)
+        nc.vector.tensor_copy(x_bytes[:], table_scales[:].indirect(offs_sb[:]))
+
+        z_bf16 = {name: sbuf("z_bf16_" + name, [P, PACK * S], BF16) for name in ("w2", "w1")}
+        z_scales = {name: sbuf("z_scales_" + name, [P, S], U8) for name in ("w2", "w1")}
+
+        def hidden(name, banks):
+            for c in range(S // P):
+                cols = slice(c * P, (c + 1) * P)
+                bank = psum.tile([P, PACK, P], F32, name="hidden_%s_%d" % (name, c), tag=banks[c])
+                for t in range(PACK):
+                    product(bank[:, t, :], name, t, x_codes[:, cols], x_bytes[:, cols], True, True)
+                nc.scalar.activation(
+                    z_bf16[name][:, PACK * cols.start : PACK * cols.stop].rearrange("p (n t) -> p n t", t=PACK),
+                    bank[:].rearrange("p t n -> p n t"),
+                    ACT.Silu,
+                )
+
+        round_on_scalar("w2", 0, P, 1.0)
+        quantize_weight("w2", ALL)
+        for cols in HALVES:
+            nc.vector.tensor_copy(x_codes[:, cols], table_words[:].indirect(entries(offs_sb, cols)))
+        hidden("w2", ["A0", "A1", "A2", "A3"])
+        round_on_vector("w1", 0, P, 1.0)
+        quantize_weight("w1", ALL)
+        hidden("w1", ["B0", "B1", "B2", "B0"])
+
+        round_on_vector("w4", 0, P, 1.0)
+        z2_codes = sbuf("z2_codes", [P, S], U32, tag="w4_raw")
+        quantize(z2_codes, z_scales["w2"], z_bf16["w2"], ALL)
+        for cols in HALVES:
+            quantize_weight("w4", cols)
+        b_bank = [psum.tile([P, S], F32, name="b%d" % t, tag=bank) for t, bank in enumerate(("B3", "B1"))]
+        diff_bank = [psum.tile([P, S], F32, name="diff%d" % t, tag="A%d" % t) for t in range(PACK)]
+        for t in range(PACK):
+            product(diff_bank[t][:], "w4", t, z2_codes[:], z_scales["w2"][:], True, False)
+        for t in range(GPSIMD_SLOTS):
+            product(b_bank[t][:], "w4", t, z2_codes[:], z_scales["w2"][:], True, True)
+
+        round_on_vector("w3", W3_ON_SCALAR, P, -1.0)
+        round_on_scalar("w3", 0, W3_ON_SCALAR, -1.0)
+        last_share = [sbuf("last_share0", [P, S // 2], F32)]
+        nc.vector.tensor_copy(last_share[0][:], mix_sb[PACK - 1][:].indirect(entries(task_sb, HALVES[0])))
+        z_codes = sbuf("z_codes", [P, S], U32)
+        quantize(z_codes, z_scales["w1"], z_bf16["w1"], ALL)
+        for slots in ((0,), (1,), (2, 3)):
+            quantize_weight("w3", slice(slots[0] * P, (slots[-1] + 1) * P))
+            for t in slots:
+                product(diff_bank[t][:], "w3", t, z_codes[:], z_scales["w1"][:], False, True)
+        last_share.append(sbuf("last_share1", [P, S // 2], F32, tag="z_bf16_w1"))
+        nc.vector.tensor_copy(last_share[1][:], mix_sb[PACK - 1][:].indirect(entries(task_sb, HALVES[1])))
+
+        scaled = [sbuf("scaled%d" % t, [P, S], F32) for t in range(PACK)]
+        b_sb = [sbuf("b_sb%d" % t, [P, S], F32) for t in range(GPSIMD_SLOTS)]
+
+        def scale(t, cols, q):
+            nc.vector.tensor_tensor(scaled[t][:, cols], diff_bank[t][:, cols], q, ALU.mult)
+
+        def finish(engine, queue, b, t, cols):
+            result = sbuf("result%d_%d" % (t, cols.start), [P, cols.stop - cols.start], F32)
+            engine.tensor_tensor(result[:], b[:, cols], scaled[t][:, cols], ALU.subtract)
+            queue.dma_start(out=out_rows[:, t, cols], in_=result[:])
+
+        for t in range(GPSIMD_SLOTS):
+            nc.scalar.copy(b_sb[t][:], b_bank[t][:])
+        for t in range(GPSIMD_SLOTS):
+            scale(t, ALL, share[t][:])
+            late = GPSIMD_SLOTS + t
+            b_bank.append(psum.tile([P, S], F32, name="b%d" % late, tag="A%d" % t))
+            product(b_bank[late][:], "w4", late, z2_codes[:], z_scales["w2"][:], True, True)
+        finish(nc.gpsimd, nc.scalar, b_sb[0], 0, ALL)
+        for cols in HALVES:
+            finish(nc.gpsimd, nc.scalar, b_sb[1], 1, cols)
+        scale(2, ALL, share[2][:])
+        scale(3, HALVES[0], last_share[0][:])
+        finish(nc.vector, nc.sync, b_bank[2], 2, ALL)
+        scale(3, HALVES[1], last_share[1][:])
+        for cols in HALVES:
+            finish(nc.vector, nc.sync, b_bank[3], 3, cols)

@@ -96,8 +96,6 @@ def tile_picked_expertpair_silu_p_kernel(
                 stop=stop,
             )
 
-        warm_in = sbuf("warm_in", [P, 8], F32)
-        nc.vector.memset(warm_in[:], 0.0)
         nc.vector.memset(table_scales[:].bitcast(I32), 0)
         nc.sync.dma_start(task_sb[:], task)
         load_mix(0)
@@ -107,8 +105,6 @@ def tile_picked_expertpair_silu_p_kernel(
                 out=table_scales[QUADRANT * q : QUADRANT * q + PACK, :].bitcast(I32),
                 in_=x_scales[0, PACK * q : PACK * (q + 1), :].bitcast(I32),
             )
-        warm_out = sbuf("warm_out", [P, 8], F32)
-        nc.scalar.activation(warm_out[:], warm_in[:], ACT.Silu)
         load_mix(1)
         load_mix(2)
         load_weight("w2")

@@ -20,9 +20,12 @@ PACK = 4
 GROUP = 16
 QUADRANT = 32
 ALL = slice(0, S)
+ALL_QUADS = slice(0, P)
+ALL_SLOTS = slice(0, PACK)
+PAIRS = (slice(0, 2), slice(2, PACK))
 HALVES = (slice(0, S // 2), slice(S // 2, S))
-W3_ON_SCALAR = 56
-GPSIMD_SLOTS = 2
+RAW_OFFSET = {"w2": 0, "w1": PACK * H * 4}
+W3_ON_SCALAR = 64
 
 
 def tile_picked_expertpair_silu_p_kernel(
@@ -31,10 +34,14 @@ def tile_picked_expertpair_silu_p_kernel(
     nc = tc.nc
     with ExitStack() as ctx:
         keep = ctx.enter_context(tc.tile_pool(name="keep", bufs=1))
+        shared = ctx.enter_context(tc.tile_pool(name="shared", bufs=1))
         psum = ctx.enter_context(tc.psum_pool(name="psum", bufs=1))
 
         def sbuf(name, shape, dtype, tag=None):
             return keep.tile(shape, dtype, name=name, tag=tag or name, align_bytes=64)
+
+        def reused(name, shape, dtype, offset):
+            return shared.tile(shape, dtype, name=name, offset=offset, align_bytes=64)
 
         def entries(list_tile, cols):
             return list_tile[:, cols.start // GROUP : cols.stop // GROUP]
@@ -46,11 +53,14 @@ def tile_picked_expertpair_silu_p_kernel(
         mix_rows = mix.rearrange("(p t) u -> p t u", t=PACK)
         out_rows = out.rearrange("(p t) j -> p t j", t=PACK)
         mix_sb = [sbuf("mix%d" % t, [P, U], F32) for t in range(PACK)]
-        share = [sbuf("share%d" % t, [P, S], F32) for t in range(PACK - 1)]
+        share = [sbuf("share%d" % h, [P, PACK, S // 2], F32) for h in range(2)]
         weights = {"w1": w1, "w2": w2, "w3": w3, "w4": w4}
         w_raw, w_bf16, w_codes, w_scales = {}, {}, {}, {}
         for name in weights:
-            w_raw[name] = sbuf(name + "_raw", [P, PACK, H], F32)
+            if name in RAW_OFFSET:
+                w_raw[name] = reused(name + "_raw", [P, PACK, H], F32, RAW_OFFSET[name])
+            else:
+                w_raw[name] = sbuf(name + "_raw", [P, PACK, H], F32)
             w_bf16[name] = sbuf(name + "_bf16", [P, PACK * H], BF16)
             w_codes[name] = sbuf(name + "_codes", [P, H], U32)
             w_scales[name] = sbuf(name + "_scales", [P, H], U8)
@@ -61,18 +71,18 @@ def tile_picked_expertpair_silu_p_kernel(
         def load_weight(name):
             nc.sync.dma_start(out=w_raw[name][:], in_=weights[name].rearrange("(p j) c -> p j c", j=PACK))
 
-        def rounding_views(name, lo, hi):
-            dst = w_bf16[name][:].rearrange("p (t m j) -> p m j t", t=PACK, j=PACK)[:, lo:hi]
-            src = w_raw[name][:].rearrange("p j (m t) -> p m j t", t=PACK)[:, lo:hi]
+        def rounding_views(name, quads, slots):
+            dst = w_bf16[name][:].rearrange("p (t m j) -> p m j t", t=PACK, j=PACK)[:, quads, :, slots]
+            src = w_raw[name][:].rearrange("p j (m t) -> p m j t", t=PACK)[:, quads, :, slots]
             return dst, src
 
-        def round_on_vector(name, lo, hi, sign):
-            dst, src = rounding_views(name, lo, hi)
+        def round_on_vector(name, quads, slots, sign):
+            dst, src = rounding_views(name, quads, slots)
             nc.vector.tensor_scalar(dst, src, sign, None, ALU.mult)
 
-        def round_on_scalar(name, lo, hi, sign):
-            dst, src = rounding_views(name, lo, hi)
-            nc.scalar.activation(dst, src, ACT.Copy, scale=sign)
+        def round_on_scalar(name, quads, slots):
+            dst, src = rounding_views(name, quads, slots)
+            nc.scalar.copy(dst, src)
 
         def quantize(codes, scales, values, cols):
             nc.vector.quantize_mx(
@@ -81,8 +91,8 @@ def tile_picked_expertpair_silu_p_kernel(
                 in_=values[:, PACK * cols.start : PACK * cols.stop],
             )
 
-        def quantize_weight(name, cols):
-            quantize(w_codes[name], w_scales[name], w_bf16[name], cols)
+        def quantize_weight(name, slots):
+            quantize(w_codes[name], w_scales[name], w_bf16[name], slice(slots.start * P, slots.stop * P))
 
         def product(dst, name, t, codes, scales, start, stop):
             cols = slice(t * P, (t + 1) * P)
@@ -97,103 +107,111 @@ def tile_picked_expertpair_silu_p_kernel(
             )
 
         nc.vector.memset(table_scales[:].bitcast(I32), 0)
-        nc.sync.dma_start(task_sb[:], task)
-        load_mix(0)
         nc.sync.dma_start(offs_sb[:], offs)
+        nc.sync.dma_start(task_sb[:], task)
+        for t in range(PACK - 1):
+            load_mix(t)
+        load_weight("w2")
+        load_mix(PACK - 1)
         for q in range(P // QUADRANT):
             nc.scalar.dma_start(
                 out=table_scales[QUADRANT * q : QUADRANT * q + PACK, :].bitcast(I32),
                 in_=x_scales[0, PACK * q : PACK * (q + 1), :].bitcast(I32),
             )
-        load_mix(1)
-        load_mix(2)
-        load_weight("w2")
         nc.sync.dma_start(out=table_words[:].bitcast(I32), in_=x_words[0].rearrange("p n t -> p (n t)").bitcast(I32))
         load_weight("w1")
         load_weight("w4")
         load_weight("w3")
-        load_mix(PACK - 1)
 
-        for t in range(PACK - 1):
-            for cols in HALVES:
-                nc.vector.tensor_copy(share[t][:, cols], mix_sb[t][:].indirect(entries(task_sb, cols)))
-        x_codes = sbuf("x_codes", [P, S], U32)
+        def gather_shares(t):
+            for h, cols in enumerate(HALVES):
+                nc.vector.tensor_copy(share[h][:, t, :], mix_sb[t][:].indirect(entries(task_sb, cols)))
+
         x_bytes = sbuf("x_bytes", [P, S], U8)
+        for t in range(PACK - 1):
+            gather_shares(t)
         nc.vector.tensor_copy(x_bytes[:], table_scales[:].indirect(offs_sb[:]))
+        gather_shares(PACK - 1)
 
         z_bf16 = {name: sbuf("z_bf16_" + name, [P, PACK * S], BF16) for name in ("w2", "w1")}
+        z_codes = {"w1": sbuf("z_codes_w1", [P, S], U32)}
         z_scales = {name: sbuf("z_scales_" + name, [P, S], U8) for name in ("w2", "w1")}
+
+        def quantize_hidden(name, cols):
+            quantize(z_codes[name], z_scales[name], z_bf16[name], cols)
 
         def hidden(name, banks):
             for c in range(S // P):
                 cols = slice(c * P, (c + 1) * P)
                 bank = psum.tile([P, PACK, P], F32, name="hidden_%s_%d" % (name, c), tag=banks[c])
+                codes = x_codes[c // 2][:, c % 2 * P : (c % 2 + 1) * P]
                 for t in range(PACK):
-                    product(bank[:, t, :], name, t, x_codes[:, cols], x_bytes[:, cols], True, True)
+                    product(bank[:, t, :], name, t, codes, x_bytes[:, cols], True, True)
                 nc.scalar.activation(
                     z_bf16[name][:, PACK * cols.start : PACK * cols.stop].rearrange("p (n t) -> p n t", t=PACK),
                     bank[:].rearrange("p t n -> p n t"),
                     ACT.Silu,
                 )
 
-        round_on_scalar("w2", 0, P, 1.0)
-        quantize_weight("w2", ALL)
-        for cols in HALVES:
-            nc.vector.tensor_copy(x_codes[:, cols], table_words[:].indirect(entries(offs_sb, cols)))
+        round_on_scalar("w2", ALL_QUADS, ALL_SLOTS)
+        quantize_weight("w2", ALL_SLOTS)
+        x_codes = [reused("x_codes%d" % h, [P, S // 2], U32, RAW_OFFSET["w2"] + h * S * 2) for h in range(2)]
+        for codes, cols in zip(x_codes, HALVES):
+            nc.vector.tensor_copy(codes[:], table_words[:].indirect(entries(offs_sb, cols)))
         hidden("w2", ["A0", "A1", "A2", "A3"])
-        round_on_vector("w1", 0, P, 1.0)
-        quantize_weight("w1", ALL)
+        for slots in PAIRS:
+            round_on_vector("w1", ALL_QUADS, slots, 1.0)
+        for slots in PAIRS:
+            quantize_weight("w1", slots)
+        z_codes["w2"] = reused("z_codes_w2", [P, S], U32, RAW_OFFSET["w1"])
+        for cols in HALVES:
+            quantize_hidden("w2", cols)
         hidden("w1", ["B0", "B1", "B2", "B0"])
 
-        round_on_vector("w4", 0, P, 1.0)
-        z2_codes = sbuf("z2_codes", [P, S], U32, tag="w4_raw")
-        quantize(z2_codes, z_scales["w2"], z_bf16["w2"], ALL)
-        for cols in HALVES:
-            quantize_weight("w4", cols)
-        b_bank = [psum.tile([P, S], F32, name="b%d" % t, tag=bank) for t, bank in enumerate(("B3", "B1"))]
-        diff_bank = [psum.tile([P, S], F32, name="diff%d" % t, tag="A%d" % t) for t in range(PACK)]
-        for t in range(PACK):
-            product(diff_bank[t][:], "w4", t, z2_codes[:], z_scales["w2"][:], True, False)
-        for t in range(GPSIMD_SLOTS):
-            product(b_bank[t][:], "w4", t, z2_codes[:], z_scales["w2"][:], True, True)
+        for slots in PAIRS:
+            round_on_vector("w4", ALL_QUADS, slots, -1.0)
+        for slots in PAIRS:
+            quantize_weight("w4", slots)
+        round_on_vector("w3", ALL_QUADS, PAIRS[0], 1.0)
+        quantize_hidden("w1", HALVES[0])
+        quantize_weight("w3", PAIRS[0])
+        quantize_hidden("w1", HALVES[1])
+        round_on_vector("w3", slice(W3_ON_SCALAR, P), PAIRS[1], 1.0)
+        round_on_scalar("w3", slice(0, W3_ON_SCALAR), PAIRS[1])
+        quantize_weight("w3", PAIRS[1])
 
-        round_on_vector("w3", W3_ON_SCALAR, P, -1.0)
-        round_on_scalar("w3", 0, W3_ON_SCALAR, -1.0)
-        last_share = [sbuf("last_share0", [P, S // 2], F32)]
-        nc.vector.tensor_copy(last_share[0][:], mix_sb[PACK - 1][:].indirect(entries(task_sb, HALVES[0])))
-        z_codes = sbuf("z_codes", [P, S], U32)
-        quantize(z_codes, z_scales["w1"], z_bf16["w1"], ALL)
-        for slots in ((0,), (1,), (2, 3)):
-            quantize_weight("w3", slice(slots[0] * P, (slots[-1] + 1) * P))
-            for t in slots:
-                product(diff_bank[t][:], "w3", t, z_codes[:], z_scales["w1"][:], False, True)
-        last_share.append(sbuf("last_share1", [P, S // 2], F32, tag="z_bf16_w1"))
-        nc.vector.tensor_copy(last_share[1][:], mix_sb[PACK - 1][:].indirect(entries(task_sb, HALVES[1])))
+        units = [(slots, h) for slots in PAIRS for h in range(2)]
+        diff_bank = [psum.tile([P, 2, S // 2], F32, name="diff%d" % u, tag="A%d" % u) for u in range(len(units))]
+        b_bank = [psum.tile([P, 2, S // 2], F32, name="b%d" % u, tag=tag) for u, tag in enumerate(("B3", "B1", "B2", "B0"))]
 
-        scaled = [sbuf("scaled%d" % t, [P, S], F32) for t in range(PACK)]
-        b_sb = [sbuf("b_sb%d" % t, [P, S], F32) for t in range(GPSIMD_SLOTS)]
+        def passes(bank, name, z_name, u, start, stop):
+            slots, h = units[u]
+            codes, scales = z_codes[z_name][:, HALVES[h]], z_scales[z_name][:, HALVES[h]]
+            for i in range(2):
+                product(bank[:, i, :], name, slots.start + i, codes, scales, start and i == 0, stop and i == 1)
 
-        def scale(t, cols, q):
-            nc.vector.tensor_tensor(scaled[t][:, cols], diff_bank[t][:, cols], q, ALU.mult)
+        for u in range(len(units)):
+            passes(diff_bank[u], "w4", "w2", u, True, False)
+            passes(diff_bank[u], "w3", "w1", u, False, True)
+            passes(b_bank[u], "w4", "w2", u, True, True)
 
-        def finish(engine, queue, b, t, cols):
-            result = sbuf("result%d_%d" % (t, cols.start), [P, cols.stop - cols.start], F32)
-            engine.tensor_tensor(result[:], b[:, cols], scaled[t][:, cols], ALU.subtract)
-            queue.dma_start(out=out_rows[:, t, cols], in_=result[:])
+        scaled = [sbuf("scaled%d" % u, [P, 2, S // 2], F32) for u in range(len(units))]
+        b_sb = [sbuf("b_sb%d" % u, [P, 2, S // 2], F32) for u in range(2)]
 
-        for t in range(GPSIMD_SLOTS):
-            nc.scalar.copy(b_sb[t][:], b_bank[t][:])
-        for t in range(GPSIMD_SLOTS):
-            scale(t, ALL, share[t][:])
-            late = GPSIMD_SLOTS + t
-            b_bank.append(psum.tile([P, S], F32, name="b%d" % late, tag="A%d" % t))
-            product(b_bank[late][:], "w4", late, z2_codes[:], z_scales["w2"][:], True, True)
-        finish(nc.gpsimd, nc.scalar, b_sb[0], 0, ALL)
-        for cols in HALVES:
-            finish(nc.gpsimd, nc.scalar, b_sb[1], 1, cols)
-        scale(2, ALL, share[2][:])
-        scale(3, HALVES[0], last_share[0][:])
-        finish(nc.vector, nc.sync, b_bank[2], 2, ALL)
-        scale(3, HALVES[1], last_share[1][:])
-        for cols in HALVES:
-            finish(nc.vector, nc.sync, b_bank[3], 3, cols)
+        def finish(engine, queue, b, u, part):
+            slots, h = units[u]
+            result = sbuf("result%d_%d" % (u, part.start), [P, part.stop - part.start, S // 2], F32)
+            engine.tensor_tensor(result[:], scaled[u][:, part], b[:, part], ALU.subtract)
+            rows = slice(slots.start + part.start, slots.start + part.stop)
+            queue.dma_start(out=out_rows[:, rows, HALVES[h]], in_=result[:])
+
+        for u in range(2):
+            nc.scalar.copy(b_sb[u][:], b_bank[u][:])
+        for u, (slots, h) in enumerate(units):
+            nc.vector.tensor_tensor(scaled[u][:], diff_bank[u][:], share[h][:, slots, :], ALU.mult)
+        for u in range(2):
+            for i in range(2):
+                finish(nc.gpsimd, nc.scalar, b_sb[u], u, slice(i, i + 1))
+        finish(nc.vector, nc.sync, b_bank[2], 2, slice(0, 2))
+        for i in range(2):
+            finish(nc.vector, nc.sync, b_bank[3], 3, slice(i, i + 1))

@@ -24,8 +24,8 @@ ALL_QUADS = slice(0, P)
 ALL_SLOTS = slice(0, PACK)
 PAIRS = (slice(0, 2), slice(2, PACK))
 HALVES = (slice(0, S // 2), slice(S // 2, S))
-RAW_OFFSET = {"w2": 0, "w1": PACK * H * 4}
-W3_ON_SCALAR = 64
+RAW_OFFSET = {"w2": 0, "w1": PACK * H * 4, "w4": 2 * PACK * H * 4}
+W2_ON_SCALAR = 84
 
 
 def tile_picked_expertpair_silu_p_kernel(
@@ -53,7 +53,7 @@ def tile_picked_expertpair_silu_p_kernel(
         mix_rows = mix.rearrange("(p t) u -> p t u", t=PACK)
         out_rows = out.rearrange("(p t) j -> p t j", t=PACK)
         mix_sb = [sbuf("mix%d" % t, [P, U], F32) for t in range(PACK)]
-        share = [sbuf("share%d" % h, [P, PACK, S // 2], F32) for h in range(2)]
+        share = [sbuf("share%d" % h, [P, PACK - 1, S // 2], F32) for h in range(2)]
         weights = {"w1": w1, "w2": w2, "w3": w3, "w4": w4}
         w_raw, w_bf16, w_codes, w_scales = {}, {}, {}, {}
         for name in weights:
@@ -106,21 +106,23 @@ def tile_picked_expertpair_silu_p_kernel(
                 stop=stop,
             )
 
-        nc.vector.memset(table_scales[:].bitcast(I32), 0)
-        nc.sync.dma_start(offs_sb[:], offs)
+        nc.vector.memset(table_scales[:, : T // 2].bitcast(I32), 0)
+        nc.gpsimd.memset(table_scales[:, T // 2 :].bitcast(I32), 0)
+        load_mix(0)
         nc.sync.dma_start(task_sb[:], task)
-        for t in range(PACK - 1):
-            load_mix(t)
+        load_mix(1)
+        nc.sync.dma_start(offs_sb[:], offs)
         load_weight("w2")
-        load_mix(PACK - 1)
         for q in range(P // QUADRANT):
-            nc.scalar.dma_start(
+            nc.sync.dma_start(
                 out=table_scales[QUADRANT * q : QUADRANT * q + PACK, :].bitcast(I32),
                 in_=x_scales[0, PACK * q : PACK * (q + 1), :].bitcast(I32),
             )
         nc.sync.dma_start(out=table_words[:].bitcast(I32), in_=x_words[0].rearrange("p n t -> p (n t)").bitcast(I32))
+        load_mix(2)
         load_weight("w1")
         load_weight("w4")
+        load_mix(3)
         load_weight("w3")
 
         def gather_shares(t):
@@ -128,10 +130,9 @@ def tile_picked_expertpair_silu_p_kernel(
                 nc.vector.tensor_copy(share[h][:, t, :], mix_sb[t][:].indirect(entries(task_sb, cols)))
 
         x_bytes = sbuf("x_bytes", [P, S], U8)
-        for t in range(PACK - 1):
-            gather_shares(t)
+        gather_shares(0)
+        gather_shares(1)
         nc.vector.tensor_copy(x_bytes[:], table_scales[:].indirect(offs_sb[:]))
-        gather_shares(PACK - 1)
 
         z_bf16 = {name: sbuf("z_bf16_" + name, [P, PACK * S], BF16) for name in ("w2", "w1")}
         z_codes = {"w1": sbuf("z_codes_w1", [P, S], U32)}
@@ -153,11 +154,13 @@ def tile_picked_expertpair_silu_p_kernel(
                     ACT.Silu,
                 )
 
-        round_on_scalar("w2", ALL_QUADS, ALL_SLOTS)
+        round_on_scalar("w2", slice(0, W2_ON_SCALAR), ALL_SLOTS)
+        round_on_vector("w2", slice(W2_ON_SCALAR, P), ALL_SLOTS, 1.0)
         quantize_weight("w2", ALL_SLOTS)
         x_codes = [reused("x_codes%d" % h, [P, S // 2], U32, RAW_OFFSET["w2"] + h * S * 2) for h in range(2)]
         for codes, cols in zip(x_codes, HALVES):
             nc.vector.tensor_copy(codes[:], table_words[:].indirect(entries(offs_sb, cols)))
+        gather_shares(2)
         hidden("w2", ["A0", "A1", "A2", "A3"])
         for slots in PAIRS:
             round_on_vector("w1", ALL_QUADS, slots, 1.0)
@@ -172,12 +175,15 @@ def tile_picked_expertpair_silu_p_kernel(
             round_on_vector("w4", ALL_QUADS, slots, -1.0)
         for slots in PAIRS:
             quantize_weight("w4", slots)
-        round_on_vector("w3", ALL_QUADS, PAIRS[0], 1.0)
+        last_share = [reused("last_share0", [P, S // 2], F32, RAW_OFFSET["w4"])]
+        nc.vector.tensor_copy(last_share[0][:], mix_sb[PACK - 1][:].indirect(entries(task_sb, HALVES[0])))
         quantize_hidden("w1", HALVES[0])
-        quantize_weight("w3", PAIRS[0])
+        round_on_vector("w3", ALL_QUADS, PAIRS[0], 1.0)
+        round_on_scalar("w3", ALL_QUADS, PAIRS[1])
         quantize_hidden("w1", HALVES[1])
-        round_on_vector("w3", slice(W3_ON_SCALAR, P), PAIRS[1], 1.0)
-        round_on_scalar("w3", slice(0, W3_ON_SCALAR), PAIRS[1])
+        quantize_weight("w3", PAIRS[0])
+        last_share.append(sbuf("last_share1", [P, S // 2], F32, tag="z_bf16_w1"))
+        nc.vector.tensor_copy(last_share[1][:], mix_sb[PACK - 1][:].indirect(entries(task_sb, HALVES[1])))
         quantize_weight("w3", PAIRS[1])
 
         units = [(slots, h) for slots in PAIRS for h in range(2)]
@@ -190,7 +196,7 @@ def tile_picked_expertpair_silu_p_kernel(
             for i in range(2):
                 product(bank[:, i, :], name, slots.start + i, codes, scales, start and i == 0, stop and i == 1)
 
-        for u in range(len(units)):
+        for u in (0, 2, 1, 3):
             passes(diff_bank[u], "w4", "w2", u, True, False)
             passes(diff_bank[u], "w3", "w1", u, False, True)
             passes(b_bank[u], "w4", "w2", u, True, True)
@@ -205,13 +211,21 @@ def tile_picked_expertpair_silu_p_kernel(
             rows = slice(slots.start + part.start, slots.start + part.stop)
             queue.dma_start(out=out_rows[:, rows, HALVES[h]], in_=result[:])
 
+        def scale(u, part, q):
+            nc.vector.tensor_tensor(scaled[u][:, part], diff_bank[u][:, part], q, ALU.mult)
+
+        first, second, both = slice(0, 1), slice(1, 2), slice(0, 2)
         for u in range(2):
             nc.scalar.copy(b_sb[u][:], b_bank[u][:])
-        for u, (slots, h) in enumerate(units):
-            nc.vector.tensor_tensor(scaled[u][:], diff_bank[u][:], share[h][:, slots, :], ALU.mult)
+        scale(0, both, share[0][:, PAIRS[0]])
+        scale(2, first, share[0][:, 2:3])
+        scale(2, second, last_share[0][:].unsqueeze(1))
+        scale(1, both, share[1][:, PAIRS[0]])
+        finish(nc.vector, nc.sync, b_bank[2], 2, both)
+        scale(3, first, share[1][:, 2:3])
+        scale(3, second, last_share[1][:].unsqueeze(1))
         for u in range(2):
-            for i in range(2):
-                finish(nc.gpsimd, nc.scalar, b_sb[u], u, slice(i, i + 1))
-        finish(nc.vector, nc.sync, b_bank[2], 2, slice(0, 2))
-        for i in range(2):
-            finish(nc.vector, nc.sync, b_bank[3], 3, slice(i, i + 1))
+            for part in (first, second):
+                finish(nc.gpsimd, nc.scalar, b_sb[u], u, part)
+        for part in (first, second):
+            finish(nc.vector, nc.sync, b_bank[3], 3, part)

@@ -24,8 +24,9 @@ ALL_QUADS = slice(0, P)
 ALL_SLOTS = slice(0, PACK)
 PAIRS = (slice(0, 2), slice(2, PACK))
 HALVES = (slice(0, S // 2), slice(S // 2, S))
-RAW_OFFSET = {"w2": 0, "w1": PACK * H * 4, "w4": 2 * PACK * H * 4}
+RAW_OFFSET = {"w2": 0, "w1": PACK * H * 4, "w3": 2 * PACK * H * 4}
 W2_ON_SCALAR = 84
+W3_ON_SCALAR = 96
 
 
 def tile_picked_expertpair_silu_p_kernel(
@@ -113,17 +114,16 @@ def tile_picked_expertpair_silu_p_kernel(
         load_mix(1)
         nc.sync.dma_start(offs_sb[:], offs)
         load_weight("w2")
-        for q in range(P // QUADRANT):
+        for r in range(PACK):
             nc.sync.dma_start(
-                out=table_scales[QUADRANT * q : QUADRANT * q + PACK, :].bitcast(I32),
-                in_=x_scales[0, PACK * q : PACK * (q + 1), :].bitcast(I32),
+                out=table_scales[r:P:QUADRANT, :].bitcast(I32), in_=x_scales[0, r : PACK * PACK : PACK, :].bitcast(I32)
             )
         nc.sync.dma_start(out=table_words[:].bitcast(I32), in_=x_words[0].rearrange("p n t -> p (n t)").bitcast(I32))
         load_mix(2)
         load_weight("w1")
         load_weight("w4")
-        load_mix(3)
         load_weight("w3")
+        load_mix(3)
 
         def gather_shares(t):
             for h, cols in enumerate(HALVES):
@@ -175,16 +175,17 @@ def tile_picked_expertpair_silu_p_kernel(
             round_on_vector("w4", ALL_QUADS, slots, -1.0)
         for slots in PAIRS:
             quantize_weight("w4", slots)
-        last_share = [reused("last_share0", [P, S // 2], F32, RAW_OFFSET["w4"])]
-        nc.vector.tensor_copy(last_share[0][:], mix_sb[PACK - 1][:].indirect(entries(task_sb, HALVES[0])))
         quantize_hidden("w1", HALVES[0])
         round_on_vector("w3", ALL_QUADS, PAIRS[0], 1.0)
-        round_on_scalar("w3", ALL_QUADS, PAIRS[1])
-        quantize_hidden("w1", HALVES[1])
+        round_on_scalar("w3", slice(0, W3_ON_SCALAR), PAIRS[1])
+        last_share = [sbuf("last_share0", [P, S // 2], F32)]
+        nc.vector.tensor_copy(last_share[0][:], mix_sb[PACK - 1][:].indirect(entries(task_sb, HALVES[0])))
         quantize_weight("w3", PAIRS[0])
-        last_share.append(sbuf("last_share1", [P, S // 2], F32, tag="z_bf16_w1"))
-        nc.vector.tensor_copy(last_share[1][:], mix_sb[PACK - 1][:].indirect(entries(task_sb, HALVES[1])))
+        quantize_hidden("w1", HALVES[1])
+        round_on_vector("w3", slice(W3_ON_SCALAR, P), PAIRS[1], 1.0)
         quantize_weight("w3", PAIRS[1])
+        last_share.append(reused("last_share1", [P, S // 2], F32, RAW_OFFSET["w3"]))
+        nc.vector.tensor_copy(last_share[1][:], mix_sb[PACK - 1][:].indirect(entries(task_sb, HALVES[1])))
 
         units = [(slots, h) for slots in PAIRS for h in range(2)]
         diff_bank = [psum.tile([P, 2, S // 2], F32, name="diff%d" % u, tag="A%d" % u) for u in range(len(units))]

@@ -19,14 +19,8 @@ P = 128
 PACK = 4
 GROUP = 16
 QUADRANT = 32
-ALL = slice(0, S)
-ALL_QUADS = slice(0, P)
-ALL_SLOTS = slice(0, PACK)
 PAIRS = (slice(0, 2), slice(2, PACK))
 HALVES = (slice(0, S // 2), slice(S // 2, S))
-RAW_OFFSET = {"w2": 0, "w1": PACK * H * 4, "w3": 2 * PACK * H * 4}
-W2_ON_SCALAR = 84
-W3_ON_SCALAR = 96
 
 
 def tile_picked_expertpair_silu_p_kernel(
@@ -35,14 +29,10 @@ def tile_picked_expertpair_silu_p_kernel(
     nc = tc.nc
     with ExitStack() as ctx:
         keep = ctx.enter_context(tc.tile_pool(name="keep", bufs=1))
-        shared = ctx.enter_context(tc.tile_pool(name="shared", bufs=1))
         psum = ctx.enter_context(tc.psum_pool(name="psum", bufs=1))
 
         def sbuf(name, shape, dtype, tag=None):
             return keep.tile(shape, dtype, name=name, tag=tag or name, align_bytes=64)
-
-        def reused(name, shape, dtype, offset):
-            return shared.tile(shape, dtype, name=name, offset=offset, align_bytes=64)
 
         def entries(list_tile, cols):
             return list_tile[:, cols.start // GROUP : cols.stop // GROUP]
@@ -54,15 +44,15 @@ def tile_picked_expertpair_silu_p_kernel(
         mix_rows = mix.rearrange("(p t) u -> p t u", t=PACK)
         out_rows = out.rearrange("(p t) j -> p t j", t=PACK)
         mix_sb = [sbuf("mix%d" % t, [P, U], F32) for t in range(PACK)]
-        share = [sbuf("share%d" % h, [P, PACK - 1, S // 2], F32) for h in range(2)]
+        share = [sbuf("share%d" % h, [P, PACK, S // 2], F32) for h in range(2)]
         weights = {"w1": w1, "w2": w2, "w3": w3, "w4": w4}
+        pieces = {"w2": 1, "w1": 2, "w4": 2, "w3": 2}
         w_raw, w_bf16, w_codes, w_scales = {}, {}, {}, {}
         for name in weights:
-            if name in RAW_OFFSET:
-                w_raw[name] = reused(name + "_raw", [P, PACK, H], F32, RAW_OFFSET[name])
-            else:
-                w_raw[name] = sbuf(name + "_raw", [P, PACK, H], F32)
-            w_bf16[name] = sbuf(name + "_bf16", [P, PACK * H], BF16)
+            w_raw[name] = [
+                sbuf("%s_raw%d" % (name, c), [P, PACK, H // pieces[name]], F32) for c in range(pieces[name])
+            ]
+            w_bf16[name] = [sbuf("%s_bf16_%d" % (name, i), [P, 2 * PACK * P], BF16) for i in range(2)]
             w_codes[name] = sbuf(name + "_codes", [P, H], U32)
             w_scales[name] = sbuf(name + "_scales", [P, H], U8)
 
@@ -70,30 +60,31 @@ def tile_picked_expertpair_silu_p_kernel(
             nc.sync.dma_start(out=mix_sb[t][:], in_=mix_rows[:, t, :])
 
         def load_weight(name):
-            nc.sync.dma_start(out=w_raw[name][:], in_=weights[name].rearrange("(p j) c -> p j c", j=PACK))
+            width = H // pieces[name]
+            rows = weights[name].rearrange("(p j) c -> p j c", j=PACK)
+            for c in range(pieces[name]):
+                nc.sync.dma_start(out=w_raw[name][c][:], in_=rows[:, :, c * width : (c + 1) * width])
 
-        def rounding_views(name, quads, slots):
-            dst = w_bf16[name][:].rearrange("p (t m j) -> p m j t", t=PACK, j=PACK)[:, quads, :, slots]
-            src = w_raw[name][:].rearrange("p j (m t) -> p m j t", t=PACK)[:, quads, :, slots]
+        def rounding_views(name, c, i):
+            quads = P // pieces[name]
+            dst = w_bf16[name][i][:].rearrange("p (t m j) -> p m j t", t=2, j=PACK)[:, c * quads : (c + 1) * quads]
+            src = w_raw[name][c][:].rearrange("p j (m t) -> p m j t", t=PACK)[:, :, :, PAIRS[i]]
             return dst, src
 
-        def round_on_vector(name, quads, slots, sign):
-            dst, src = rounding_views(name, quads, slots)
+        def round_on_vector(name, c, i, sign):
+            dst, src = rounding_views(name, c, i)
             nc.vector.tensor_scalar(dst, src, sign, None, ALU.mult)
 
-        def round_on_scalar(name, quads, slots):
-            dst, src = rounding_views(name, quads, slots)
+        def round_on_scalar(name, c, i):
+            dst, src = rounding_views(name, c, i)
             nc.scalar.copy(dst, src)
 
-        def quantize(codes, scales, values, cols):
-            nc.vector.quantize_mx(
-                out=codes[:, cols].bitcast(FP8X4),
-                scales=scales[:, cols],
-                in_=values[:, PACK * cols.start : PACK * cols.stop],
-            )
+        def quantize(codes, scales, values):
+            nc.vector.quantize_mx(out=codes.bitcast(FP8X4), scales=scales, in_=values)
 
-        def quantize_weight(name, slots):
-            quantize(w_codes[name], w_scales[name], w_bf16[name], slice(slots.start * P, slots.stop * P))
+        def quantize_weight(name, i):
+            cols = slice(PAIRS[i].start * P, PAIRS[i].stop * P)
+            quantize(w_codes[name][:, cols], w_scales[name][:, cols], w_bf16[name][i][:])
 
         def product(dst, name, t, codes, scales, start, stop):
             cols = slice(t * P, (t + 1) * P)
@@ -112,34 +103,42 @@ def tile_picked_expertpair_silu_p_kernel(
         load_mix(0)
         nc.sync.dma_start(task_sb[:], task)
         load_mix(1)
-        nc.sync.dma_start(offs_sb[:], offs)
+        load_mix(2)
         load_weight("w2")
+        nc.sync.dma_start(offs_sb[:], offs)
+        load_mix(3)
         for r in range(PACK):
             nc.sync.dma_start(
                 out=table_scales[r:P:QUADRANT, :].bitcast(I32), in_=x_scales[0, r : PACK * PACK : PACK, :].bitcast(I32)
             )
         nc.sync.dma_start(out=table_words[:].bitcast(I32), in_=x_words[0].rearrange("p n t -> p (n t)").bitcast(I32))
-        load_mix(2)
         load_weight("w1")
         load_weight("w4")
         load_weight("w3")
-        load_mix(3)
 
         def gather_shares(t):
             for h, cols in enumerate(HALVES):
                 nc.vector.tensor_copy(share[h][:, t, :], mix_sb[t][:].indirect(entries(task_sb, cols)))
 
         x_bytes = sbuf("x_bytes", [P, S], U8)
-        gather_shares(0)
-        gather_shares(1)
+        x_codes = [sbuf("x_codes%d" % h, [P, S // 2], U32) for h in range(2)]
+        for t in range(PACK - 1):
+            gather_shares(t)
+        for i in range(2):
+            round_on_scalar("w2", 0, i)
+        gather_shares(PACK - 1)
         nc.vector.tensor_copy(x_bytes[:], table_scales[:].indirect(offs_sb[:]))
+        for i in range(2):
+            quantize_weight("w2", i)
+        for codes, cols in zip(x_codes, HALVES):
+            nc.vector.tensor_copy(codes[:], table_words[:].indirect(entries(offs_sb, cols)))
 
         z_bf16 = {name: sbuf("z_bf16_" + name, [P, PACK * S], BF16) for name in ("w2", "w1")}
         z_codes = {"w1": sbuf("z_codes_w1", [P, S], U32)}
         z_scales = {name: sbuf("z_scales_" + name, [P, S], U8) for name in ("w2", "w1")}
 
         def quantize_hidden(name, cols):
-            quantize(z_codes[name], z_scales[name], z_bf16[name], cols)
+            quantize(z_codes[name][:, cols], z_scales[name][:, cols], z_bf16[name][:, PACK * cols.start : PACK * cols.stop])
 
         def hidden(name, banks):
             for c in range(S // P):
@@ -154,42 +153,34 @@ def tile_picked_expertpair_silu_p_kernel(
                     ACT.Silu,
                 )
 
-        round_on_scalar("w2", slice(0, W2_ON_SCALAR), ALL_SLOTS)
-        round_on_vector("w2", slice(W2_ON_SCALAR, P), ALL_SLOTS, 1.0)
-        quantize_weight("w2", ALL_SLOTS)
-        x_codes = [reused("x_codes%d" % h, [P, S // 2], U32, RAW_OFFSET["w2"] + h * S * 2) for h in range(2)]
-        for codes, cols in zip(x_codes, HALVES):
-            nc.vector.tensor_copy(codes[:], table_words[:].indirect(entries(offs_sb, cols)))
-        gather_shares(2)
         hidden("w2", ["A0", "A1", "A2", "A3"])
-        for slots in PAIRS:
-            round_on_vector("w1", ALL_QUADS, slots, 1.0)
-        for slots in PAIRS:
-            quantize_weight("w1", slots)
-        z_codes["w2"] = reused("z_codes_w2", [P, S], U32, RAW_OFFSET["w1"])
-        for cols in HALVES:
-            quantize_hidden("w2", cols)
+        for c in range(2):
+            for i in range(2):
+                round_on_vector("w1", c, i, 1.0)
+        for i in range(2):
+            quantize_weight("w1", i)
         hidden("w1", ["B0", "B1", "B2", "B0"])
 
-        for slots in PAIRS:
-            round_on_vector("w4", ALL_QUADS, slots, -1.0)
-        for slots in PAIRS:
-            quantize_weight("w4", slots)
+        for i in range(2):
+            round_on_vector("w4", 0, i, -1.0)
+        z_codes["w2"] = sbuf("z_codes_w2", [P, S], U32, tag="w1_raw1")
+        quantize_hidden("w2", slice(0, S))
+        for i in range(2):
+            round_on_vector("w4", 1, i, -1.0)
+        for i in range(2):
+            quantize_weight("w4", i)
         quantize_hidden("w1", HALVES[0])
-        round_on_vector("w3", ALL_QUADS, PAIRS[0], 1.0)
-        round_on_scalar("w3", slice(0, W3_ON_SCALAR), PAIRS[1])
-        last_share = [sbuf("last_share0", [P, S // 2], F32)]
-        nc.vector.tensor_copy(last_share[0][:], mix_sb[PACK - 1][:].indirect(entries(task_sb, HALVES[0])))
-        quantize_weight("w3", PAIRS[0])
+        round_on_vector("w3", 0, 0, 1.0)
+        round_on_scalar("w3", 0, 1)
+        round_on_vector("w3", 1, 0, 1.0)
+        round_on_scalar("w3", 1, 1)
         quantize_hidden("w1", HALVES[1])
-        round_on_vector("w3", slice(W3_ON_SCALAR, P), PAIRS[1], 1.0)
-        quantize_weight("w3", PAIRS[1])
-        last_share.append(reused("last_share1", [P, S // 2], F32, RAW_OFFSET["w3"]))
-        nc.vector.tensor_copy(last_share[1][:], mix_sb[PACK - 1][:].indirect(entries(task_sb, HALVES[1])))
+        for i in range(2):
+            quantize_weight("w3", i)
 
         units = [(slots, h) for slots in PAIRS for h in range(2)]
         diff_bank = [psum.tile([P, 2, S // 2], F32, name="diff%d" % u, tag="A%d" % u) for u in range(len(units))]
-        b_bank = [psum.tile([P, 2, S // 2], F32, name="b%d" % u, tag=tag) for u, tag in enumerate(("B3", "B1", "B2", "B0"))]
+        b_bank = [psum.tile([P, 2, S // 2], F32, name="b%d" % u, tag=tag) for u, tag in enumerate(("B3", "B1", "B2"))]
 
         def passes(bank, name, z_name, u, start, stop):
             slots, h = units[u]
@@ -197,10 +188,11 @@ def tile_picked_expertpair_silu_p_kernel(
             for i in range(2):
                 product(bank[:, i, :], name, slots.start + i, codes, scales, start and i == 0, stop and i == 1)
 
-        for u in (0, 2, 1, 3):
+        for u in (0, 1, 2, 3):
             passes(diff_bank[u], "w4", "w2", u, True, False)
             passes(diff_bank[u], "w3", "w1", u, False, True)
-            passes(b_bank[u], "w4", "w2", u, True, True)
+            if u < 3:
+                passes(b_bank[u], "w4", "w2", u, True, True)
 
         scaled = [sbuf("scaled%d" % u, [P, 2, S // 2], F32) for u in range(len(units))]
         b_sb = [sbuf("b_sb%d" % u, [P, 2, S // 2], F32) for u in range(2)]
@@ -212,19 +204,25 @@ def tile_picked_expertpair_silu_p_kernel(
             rows = slice(slots.start + part.start, slots.start + part.stop)
             queue.dma_start(out=out_rows[:, rows, HALVES[h]], in_=result[:])
 
-        def scale(u, part, q):
-            nc.vector.tensor_tensor(scaled[u][:, part], diff_bank[u][:, part], q, ALU.mult)
+        def scale(u, part):
+            slots, h = units[u]
+            rows = slice(slots.start + part.start, slots.start + part.stop)
+            nc.vector.tensor_tensor(scaled[u][:, part], diff_bank[u][:, part], share[h][:, rows], ALU.mult)
 
         first, second, both = slice(0, 1), slice(1, 2), slice(0, 2)
         for u in range(2):
             nc.scalar.copy(b_sb[u][:], b_bank[u][:])
-        scale(0, both, share[0][:, PAIRS[0]])
-        scale(2, first, share[0][:, 2:3])
-        scale(2, second, last_share[0][:].unsqueeze(1))
-        scale(1, both, share[1][:, PAIRS[0]])
+        def late_b(u, tag):
+            b_bank.append(psum.tile([P, 2, S // 2], F32, name="b%d" % u, tag=tag))
+            passes(b_bank[u], "w4", "w2", u, True, True)
+
+        scale(0, both)
+        late_b(3, "A0")
+        scale(1, both)
+        scale(2, both)
+        scale(3, first)
         finish(nc.vector, nc.sync, b_bank[2], 2, both)
-        scale(3, first, share[1][:, 2:3])
-        scale(3, second, last_share[1][:].unsqueeze(1))
+        scale(3, second)
         for u in range(2):
             for part in (first, second):
                 finish(nc.gpsimd, nc.scalar, b_sb[u], u, part)

@@ -19,6 +19,10 @@ P = 128
 PACK = 4
 GROUP = 16
 QUADRANT = 32
+ALL = slice(0, S)
+ALL_QUADS = slice(0, P)
+SECOND_PAIR_ON_SCALAR = 84
+W3_OFFSET = PACK * H * 4
 PAIRS = (slice(0, 2), slice(2, PACK))
 HALVES = (slice(0, S // 2), slice(S // 2, S))
 
@@ -29,7 +33,11 @@ def tile_picked_expertpair_silu_p_kernel(
     nc = tc.nc
     with ExitStack() as ctx:
         keep = ctx.enter_context(tc.tile_pool(name="keep", bufs=1))
+        shared = ctx.enter_context(tc.tile_pool(name="shared", bufs=1))
         psum = ctx.enter_context(tc.psum_pool(name="psum", bufs=1))
+
+        def reused(name, shape, dtype, offset):
+            return shared.tile(shape, dtype, name=name, offset=offset, align_bytes=64)
 
         def sbuf(name, shape, dtype, tag=None):
             return keep.tile(shape, dtype, name=name, tag=tag or name, align_bytes=64)
@@ -44,54 +52,58 @@ def tile_picked_expertpair_silu_p_kernel(
         mix_rows = mix.rearrange("(p t) u -> p t u", t=PACK)
         out_rows = out.rearrange("(p t) j -> p t j", t=PACK)
         mix_sb = [sbuf("mix%d" % t, [P, U], F32) for t in range(PACK)]
-        share = [sbuf("share%d" % h, [P, PACK, S // 2], F32) for h in range(2)]
+        share = [[sbuf("share%d_%d" % (t, h), [P, S // 2], F32) for h in range(2)] for t in range(2)]
+        share.append(sbuf("share2", [P, S], F32))
+        share.append([sbuf("share3_0", [P, S // 2], F32)])
         weights = {"w1": w1, "w2": w2, "w3": w3, "w4": w4}
-        pieces = {"w2": 1, "w1": 2, "w4": 2, "w3": 2}
         w_raw, w_bf16, w_codes, w_scales = {}, {}, {}, {}
         for name in weights:
-            w_raw[name] = [
-                sbuf("%s_raw%d" % (name, c), [P, PACK, H // pieces[name]], F32) for c in range(pieces[name])
-            ]
+            if name == "w1":
+                w_raw[name] = reused("w1_raw", [P, PACK, H], F32, 0)
+            else:
+                w_raw[name] = sbuf(name + "_raw", [P, PACK, H], F32)
             w_bf16[name] = [sbuf("%s_bf16_%d" % (name, i), [P, 2 * PACK * P], BF16) for i in range(2)]
-            w_codes[name] = sbuf(name + "_codes", [P, H], U32)
-            w_scales[name] = sbuf(name + "_scales", [P, H], U8)
+            if name == "w3":
+                w_bf16[name][0] = reused("w3_first_pair", [P, 2 * PACK * P], BF16, W3_OFFSET)
+            w_codes[name] = [sbuf("%s_codes%d" % (name, i), [P, 2 * P], U32) for i in range(2)]
+            w_scales[name] = [sbuf("%s_scales%d" % (name, i), [P, 2 * P], U8) for i in range(2)]
 
         def load_mix(t):
             nc.sync.dma_start(out=mix_sb[t][:], in_=mix_rows[:, t, :])
 
         def load_weight(name):
-            width = H // pieces[name]
-            rows = weights[name].rearrange("(p j) c -> p j c", j=PACK)
-            for c in range(pieces[name]):
-                nc.sync.dma_start(out=w_raw[name][c][:], in_=rows[:, :, c * width : (c + 1) * width])
+            nc.sync.dma_start(out=w_raw[name][:], in_=weights[name].rearrange("(p j) c -> p j c", j=PACK))
 
-        def rounding_views(name, c, i):
-            quads = P // pieces[name]
-            dst = w_bf16[name][i][:].rearrange("p (t m j) -> p m j t", t=2, j=PACK)[:, c * quads : (c + 1) * quads]
-            src = w_raw[name][c][:].rearrange("p j (m t) -> p m j t", t=PACK)[:, :, :, PAIRS[i]]
+        def rounding_views(name, i, quads):
+            dst = w_bf16[name][i][:].rearrange("p (t m j) -> p m j t", t=2, j=PACK)[:, quads]
+            src = w_raw[name][:].rearrange("p j (m t) -> p m j t", t=PACK)[:, quads, :, PAIRS[i]]
             return dst, src
 
-        def round_on_vector(name, c, i, sign):
-            dst, src = rounding_views(name, c, i)
+        def round_on_vector(name, i, quads, sign):
+            dst, src = rounding_views(name, i, quads)
             nc.vector.tensor_scalar(dst, src, sign, None, ALU.mult)
 
-        def round_on_scalar(name, c, i):
-            dst, src = rounding_views(name, c, i)
+        def round_on_scalar(name, i, quads):
+            dst, src = rounding_views(name, i, quads)
             nc.scalar.copy(dst, src)
+
+        def round_shared(name, on_scalar):
+            round_on_vector(name, 0, ALL_QUADS, 1.0)
+            round_on_scalar(name, 1, slice(0, on_scalar))
+            round_on_vector(name, 1, slice(on_scalar, P), 1.0)
 
         def quantize(codes, scales, values):
             nc.vector.quantize_mx(out=codes.bitcast(FP8X4), scales=scales, in_=values)
 
         def quantize_weight(name, i):
-            cols = slice(PAIRS[i].start * P, PAIRS[i].stop * P)
-            quantize(w_codes[name][:, cols], w_scales[name][:, cols], w_bf16[name][i][:])
+            quantize(w_codes[name][i][:], w_scales[name][i][:], w_bf16[name][i][:])
 
         def product(dst, name, t, codes, scales, start, stop):
-            cols = slice(t * P, (t + 1) * P)
+            cols = slice(t % 2 * P, (t % 2 + 1) * P)
             nc.tensor.matmul_mx(
                 out=dst,
-                lhsT=w_codes[name][:, cols].bitcast(FP8X4),
-                lhsT_scale=w_scales[name][:, cols],
+                lhsT=w_codes[name][t // 2][:, cols].bitcast(FP8X4),
+                lhsT_scale=w_scales[name][t // 2][:, cols],
                 rhs=codes.bitcast(FP8X4),
                 rhs_scale=scales,
                 start=start,
@@ -103,128 +115,143 @@ def tile_picked_expertpair_silu_p_kernel(
         load_mix(0)
         nc.sync.dma_start(task_sb[:], task)
         load_mix(1)
-        load_mix(2)
-        load_weight("w2")
         nc.sync.dma_start(offs_sb[:], offs)
-        load_mix(3)
+        load_weight("w2")
         for r in range(PACK):
             nc.sync.dma_start(
                 out=table_scales[r:P:QUADRANT, :].bitcast(I32), in_=x_scales[0, r : PACK * PACK : PACK, :].bitcast(I32)
             )
         nc.sync.dma_start(out=table_words[:].bitcast(I32), in_=x_words[0].rearrange("p n t -> p (n t)").bitcast(I32))
+        load_mix(2)
         load_weight("w1")
         load_weight("w4")
         load_weight("w3")
+        load_mix(3)
 
-        def gather_shares(t):
-            for h, cols in enumerate(HALVES):
-                nc.vector.tensor_copy(share[h][:, t, :], mix_sb[t][:].indirect(entries(task_sb, cols)))
+        def share_view(t, cols):
+            if t == 2:
+                return share[t][:, cols]
+            return share[t][cols.start // (S // 2)][:]
+
+        def gather_share(t, h):
+            nc.vector.tensor_copy(share_view(t, HALVES[h]), mix_sb[t][:].indirect(entries(task_sb, HALVES[h])))
 
         x_bytes = sbuf("x_bytes", [P, S], U8)
         x_codes = [sbuf("x_codes%d" % h, [P, S // 2], U32) for h in range(2)]
-        for t in range(PACK - 1):
-            gather_shares(t)
-        for i in range(2):
-            round_on_scalar("w2", 0, i)
-        gather_shares(PACK - 1)
+
+        def gather_words(h):
+            nc.vector.tensor_copy(x_codes[h][:], table_words[:].indirect(entries(offs_sb, HALVES[h])))
+
+        for t in range(2):
+            for h in range(2):
+                gather_share(t, h)
+        round_on_scalar("w2", 1, ALL_QUADS)
+        round_on_vector("w2", 0, ALL_QUADS, 1.0)
         nc.vector.tensor_copy(x_bytes[:], table_scales[:].indirect(offs_sb[:]))
         for i in range(2):
             quantize_weight("w2", i)
-        for codes, cols in zip(x_codes, HALVES):
-            nc.vector.tensor_copy(codes[:], table_words[:].indirect(entries(offs_sb, cols)))
+        for h in range(2):
+            gather_words(h)
+        for h in range(2):
+            gather_share(2, h)
 
-        z_bf16 = {name: sbuf("z_bf16_" + name, [P, PACK * S], BF16) for name in ("w2", "w1")}
-        z_codes = {"w1": sbuf("z_codes_w1", [P, S], U32)}
-        z_scales = {name: sbuf("z_scales_" + name, [P, S], U8) for name in ("w2", "w1")}
+        z_bf16 = {name: [sbuf("z_bf16_%s_0" % name, [P, PACK * S // 2], BF16)] for name in ("w2", "w1")}
+        z_bf16["w1"].append(sbuf("z_bf16_w1_1", [P, PACK * S // 2], BF16))
+        z_codes = {"w1": [], "w2": []}
+        z_scales = {name: [sbuf("z_scales_%s_%d" % (name, h), [P, S // 2], U8) for h in range(2)] for name in z_codes}
 
-        def quantize_hidden(name, cols):
-            quantize(z_codes[name][:, cols], z_scales[name][:, cols], z_bf16[name][:, PACK * cols.start : PACK * cols.stop])
+        def quantize_hidden(name, h, codes):
+            z_codes[name].append(codes)
+            quantize(codes[:], z_scales[name][h][:], z_bf16[name][h][:])
 
-        def hidden(name, banks):
-            for c in range(S // P):
-                cols = slice(c * P, (c + 1) * P)
-                bank = psum.tile([P, PACK, P], F32, name="hidden_%s_%d" % (name, c), tag=banks[c])
-                codes = x_codes[c // 2][:, c % 2 * P : (c % 2 + 1) * P]
-                for t in range(PACK):
-                    product(bank[:, t, :], name, t, codes, x_bytes[:, cols], True, True)
-                nc.scalar.activation(
-                    z_bf16[name][:, PACK * cols.start : PACK * cols.stop].rearrange("p (n t) -> p n t", t=PACK),
-                    bank[:].rearrange("p t n -> p n t"),
-                    ACT.Silu,
-                )
+        def hidden(name, c, tag):
+            cols = slice(c * P, (c + 1) * P)
+            bank = psum.tile([P, PACK, P], F32, name="hidden_%s_%d" % (name, c), tag=tag)
+            codes = x_codes[c // 2][:, c % 2 * P : (c % 2 + 1) * P]
+            for t in range(PACK):
+                product(bank[:, t, :], name, t, codes, x_bytes[:, cols], True, True)
+            dst = z_bf16[name][c // 2][:, c % 2 * PACK * P : (c % 2 + 1) * PACK * P]
+            nc.scalar.activation(
+                dst.rearrange("p (n t) -> p n t", t=PACK), bank[:].rearrange("p t n -> p n t"), ACT.Silu
+            )
 
-        hidden("w2", ["A0", "A1", "A2", "A3"])
+        last = PACK - 1
         for c in range(2):
-            for i in range(2):
-                round_on_vector("w1", c, i, 1.0)
+            hidden("w2", c, "A%d" % c)
+        round_shared("w1", SECOND_PAIR_ON_SCALAR)
+        z_bf16["w2"].append(reused("z_bf16_w2_1", [P, PACK * S // 2], BF16, 0))
+        for c in range(2, PACK):
+            hidden("w2", c, "A%d" % (c - 2))
         for i in range(2):
             quantize_weight("w1", i)
-        hidden("w1", ["B0", "B1", "B2", "B0"])
-
+        quantize_hidden("w2", 0, reused("z_codes_w2_0", [P, S // 2], U32, PACK * S))
+        for c, tag in enumerate(("B0", "B1", "B2", "B0")):
+            hidden("w1", c, tag)
         for i in range(2):
-            round_on_vector("w4", 0, i, -1.0)
-        z_codes["w2"] = sbuf("z_codes_w2", [P, S], U32, tag="w1_raw1")
-        quantize_hidden("w2", slice(0, S))
-        for i in range(2):
-            round_on_vector("w4", 1, i, -1.0)
-        for i in range(2):
-            quantize_weight("w4", i)
-        quantize_hidden("w1", HALVES[0])
-        round_on_vector("w3", 0, 0, 1.0)
-        round_on_scalar("w3", 0, 1)
-        round_on_vector("w3", 1, 0, 1.0)
-        round_on_scalar("w3", 1, 1)
-        quantize_hidden("w1", HALVES[1])
+            round_on_vector("w4", i, ALL_QUADS, -1.0)
+        quantize_weight("w4", 0)
+        quantize_hidden("w2", 1, sbuf("z_codes_w2_1", [P, S // 2], U32, tag="w4_raw"))
+        quantize_weight("w4", 1)
+        quantize_hidden("w1", 0, sbuf("z_codes_w1_0", [P, S // 2], U32))
+        round_on_vector("w3", 0, ALL_QUADS, 1.0)
+        round_on_scalar("w3", 1, ALL_QUADS)
+        gather_share(last, 0)
         for i in range(2):
             quantize_weight("w3", i)
+        quantize_hidden("w1", 1, reused("z_codes_w1_1", [P, S // 2], U32, W3_OFFSET))
+        share[last].append(reused("share3_1", [P, S // 2], F32, W3_OFFSET + 2 * S))
 
-        units = [(slots, h) for slots in PAIRS for h in range(2)]
-        diff_bank = [psum.tile([P, 2, S // 2], F32, name="diff%d" % u, tag="A%d" % u) for u in range(len(units))]
-        b_bank = [psum.tile([P, 2, S // 2], F32, name="b%d" % u, tag=tag) for u, tag in enumerate(("B3", "B1", "B2"))]
+        units = [[(0, 0), (1, 0)], [(0, 1), (1, 1)], [(2, 0), (2, 1)], [(3, 0), (3, 1)]]
+        diff_bank = [psum.tile([P, S], F32, name="diff%d" % u, tag=tag) for u, tag in enumerate(("A0", "A1", "B0", "B2"))]
+        b_bank = [psum.tile([P, S], F32, name="b%d" % u, tag=tag) for u, tag in enumerate(("B3", "A2", "A3"))]
 
         def passes(bank, name, z_name, u, start, stop):
-            slots, h = units[u]
-            codes, scales = z_codes[z_name][:, HALVES[h]], z_scales[z_name][:, HALVES[h]]
-            for i in range(2):
-                product(bank[:, i, :], name, slots.start + i, codes, scales, start and i == 0, stop and i == 1)
+            for i, (t, h) in enumerate(units[u]):
+                product(bank[:, HALVES[i]], name, t, z_codes[z_name][h][:], z_scales[z_name][h][:],
+                        start and i == 0, stop and i == 1)
 
-        for u in (0, 1, 2, 3):
+        for u in range(len(units)):
             passes(diff_bank[u], "w4", "w2", u, True, False)
             passes(diff_bank[u], "w3", "w1", u, False, True)
-            if u < 3:
+            if u < last:
                 passes(b_bank[u], "w4", "w2", u, True, True)
 
-        scaled = [sbuf("scaled%d" % u, [P, 2, S // 2], F32) for u in range(len(units))]
-        b_sb = [sbuf("b_sb%d" % u, [P, 2, S // 2], F32) for u in range(2)]
-
-        def finish(engine, queue, b, u, part):
-            slots, h = units[u]
-            result = sbuf("result%d_%d" % (u, part.start), [P, part.stop - part.start, S // 2], F32)
-            engine.tensor_tensor(result[:], scaled[u][:, part], b[:, part], ALU.subtract)
-            rows = slice(slots.start + part.start, slots.start + part.stop)
-            queue.dma_start(out=out_rows[:, rows, HALVES[h]], in_=result[:])
-
-        def scale(u, part):
-            slots, h = units[u]
-            rows = slice(slots.start + part.start, slots.start + part.stop)
-            nc.vector.tensor_tensor(scaled[u][:, part], diff_bank[u][:, part], share[h][:, rows], ALU.mult)
-
-        first, second, both = slice(0, 1), slice(1, 2), slice(0, 2)
-        for u in range(2):
-            nc.scalar.copy(b_sb[u][:], b_bank[u][:])
         def late_b(u, tag):
-            b_bank.append(psum.tile([P, 2, S // 2], F32, name="b%d" % u, tag=tag))
+            b_bank.append(psum.tile([P, S], F32, name="b%d" % u, tag=tag))
             passes(b_bank[u], "w4", "w2", u, True, True)
 
-        scale(0, both)
-        late_b(3, "A0")
-        scale(1, both)
-        scale(2, both)
-        scale(3, first)
-        finish(nc.vector, nc.sync, b_bank[2], 2, both)
-        scale(3, second)
+        scaled = [sbuf("scaled%d" % u, [P, S], F32) for u in range(len(units))]
+        b_sb = [sbuf("b_sb%d" % u, [P, S], F32) for u in range(2)]
+
+        def place(u, part):
+            t, h = units[u][part.start // (S // 2)]
+            first = HALVES[h].start
+            return t, slice(first, first + part.stop - part.start)
+
+        def finish(engine, queue, b, u, part):
+            t, cols = place(u, part)
+            result = sbuf("result%d_%d" % (u, part.start), [P, part.stop - part.start], F32)
+            engine.tensor_tensor(result[:], scaled[u][:, part], b[:, part], ALU.subtract)
+            queue.dma_start(out=out_rows[:, t, cols], in_=result[:])
+
+        def scale(u, part):
+            t, cols = place(u, part)
+            nc.vector.tensor_tensor(scaled[u][:, part], diff_bank[u][:, part], share_view(t, cols), ALU.mult)
+
         for u in range(2):
-            for part in (first, second):
+            nc.scalar.copy(b_sb[u][:], b_bank[u][:])
+        scale(0, HALVES[0])
+        gather_share(last, 1)
+        scale(0, HALVES[1])
+        for part in HALVES:
+            scale(1, part)
+        late_b(last, "A1")
+        scale(2, ALL)
+        scale(last, HALVES[0])
+        finish(nc.vector, nc.sync, b_bank[2], 2, ALL)
+        scale(last, HALVES[1])
+        for u in range(2):
+            for part in HALVES:
                 finish(nc.gpsimd, nc.scalar, b_sb[u], u, part)
-        for part in (first, second):
-            finish(nc.vector, nc.sync, b_bank[3], 3, part)
+        for part in HALVES:
+            finish(nc.vector, nc.sync, b_bank[last], last, part)

@@ -210,7 +210,7 @@ def tile_picked_expertpair_silu_p_kernel(
                 product(bank[:, HALVES[i]], name, t, z_codes[z_name][h][:], z_scales[z_name][h][:],
                         start and i == 0, stop and i == 1)
 
-        for u in range(len(units)):
+        for u in (0, 2, 1, last):
             passes(diff_bank[u], "w4", "w2", u, True, False)
             passes(diff_bank[u], "w3", "w1", u, False, True)
             if u < last:
@@ -221,7 +221,8 @@ def tile_picked_expertpair_silu_p_kernel(
             passes(b_bank[u], "w4", "w2", u, True, True)
 
         scaled = [sbuf("scaled%d" % u, [P, S], F32) for u in range(len(units))]
-        b_sb = [sbuf("b_sb%d" % u, [P, S], F32) for u in range(2)]
+        b_both = sbuf("b_both", [P, 2, S], F32, tag="w3_raw")
+        b_sb = [b_both[:, u, :] for u in range(2)]
 
         def place(u, part):
             t, h = units[u][part.start // (S // 2)]
@@ -239,17 +240,17 @@ def tile_picked_expertpair_silu_p_kernel(
             nc.vector.tensor_tensor(scaled[u][:, part], diff_bank[u][:, part], share_view(t, cols), ALU.mult)
 
         for u in range(2):
-            nc.scalar.copy(b_sb[u][:], b_bank[u][:])
+            nc.scalar.copy(b_sb[u], b_bank[u][:])
         scale(0, HALVES[0])
         gather_share(last, 1)
         scale(0, HALVES[1])
-        for part in HALVES:
-            scale(1, part)
-        late_b(last, "A1")
+        late_b(last, "A0")
         scale(2, ALL)
-        scale(last, HALVES[0])
+        scale(1, HALVES[0])
         finish(nc.vector, nc.sync, b_bank[2], 2, ALL)
-        scale(last, HALVES[1])
+        scale(1, HALVES[1])
+        for part in HALVES:
+            scale(last, part)
         for u in range(2):
             for part in HALVES:
                 finish(nc.gpsimd, nc.scalar, b_sb[u], u, part)

@@ -199,7 +199,6 @@ def tile_picked_expertpair_silu_p_kernel(
         for i in range(2):
             quantize_weight("w3", i)
         quantize_hidden("w1", 1, reused("z_codes_w1_1", [P, S // 2], U32, W3_OFFSET))
-        share[last].append(reused("share3_1", [P, S // 2], F32, W3_OFFSET + 2 * S))
 
         units = [[(0, 0), (1, 0)], [(0, 1), (1, 1)], [(2, 0), (2, 1)], [(3, 0), (3, 1)]]
         diff_bank = [psum.tile([P, S], F32, name="diff%d" % u, tag=tag) for u, tag in enumerate(("A0", "A1", "B0", "B2"))]
@@ -241,14 +240,15 @@ def tile_picked_expertpair_silu_p_kernel(
 
         for u in range(2):
             nc.scalar.copy(b_sb[u], b_bank[u][:])
-        scale(0, HALVES[0])
-        gather_share(last, 1)
-        scale(0, HALVES[1])
+        for part in HALVES:
+            scale(0, part)
         late_b(last, "A0")
         scale(2, ALL)
         scale(1, HALVES[0])
         finish(nc.vector, nc.sync, b_bank[2], 2, ALL)
         scale(1, HALVES[1])
+        share[last].append(sbuf("share3_1", [P, S // 2], F32, tag="share2"))
+        gather_share(last, 1)
         for part in HALVES:
             scale(last, part)
         for u in range(2):

@@ -21,8 +21,10 @@ GROUP = 16
 QUADRANT = 32
 ALL = slice(0, S)
 ALL_QUADS = slice(0, P)
-SECOND_PAIR_ON_SCALAR = 84
-W3_OFFSET = PACK * H * 4
+SECOND_PAIR_ON_SCALAR = 40
+RAW_OFFSET = {"w1": 0, "w3": PACK * H * 4}
+W3_ON_SCALAR = 96
+W2_ON_VECTOR = 80
 PAIRS = (slice(0, 2), slice(2, PACK))
 HALVES = (slice(0, S // 2), slice(S // 2, S))
 
@@ -58,13 +60,11 @@ def tile_picked_expertpair_silu_p_kernel(
         weights = {"w1": w1, "w2": w2, "w3": w3, "w4": w4}
         w_raw, w_bf16, w_codes, w_scales = {}, {}, {}, {}
         for name in weights:
-            if name == "w1":
-                w_raw[name] = reused("w1_raw", [P, PACK, H], F32, 0)
+            if name in RAW_OFFSET:
+                w_raw[name] = reused(name + "_raw", [P, PACK, H], F32, RAW_OFFSET[name])
             else:
                 w_raw[name] = sbuf(name + "_raw", [P, PACK, H], F32)
             w_bf16[name] = [sbuf("%s_bf16_%d" % (name, i), [P, 2 * PACK * P], BF16) for i in range(2)]
-            if name == "w3":
-                w_bf16[name][0] = reused("w3_first_pair", [P, 2 * PACK * P], BF16, W3_OFFSET)
             w_codes[name] = [sbuf("%s_codes%d" % (name, i), [P, 2 * P], U32) for i in range(2)]
             w_scales[name] = [sbuf("%s_scales%d" % (name, i), [P, 2 * P], U8) for i in range(2)]
 
@@ -145,10 +145,11 @@ def tile_picked_expertpair_silu_p_kernel(
         for t in range(2):
             for h in range(2):
                 gather_share(t, h)
+        round_on_vector("w2", 0, slice(0, W2_ON_VECTOR), 1.0)
         round_on_scalar("w2", 1, ALL_QUADS)
-        round_on_vector("w2", 0, ALL_QUADS, 1.0)
+        round_on_scalar("w2", 0, slice(W2_ON_VECTOR, P))
         nc.vector.tensor_copy(x_bytes[:], table_scales[:].indirect(offs_sb[:]))
-        for i in range(2):
+        for i in (1, 0):
             quantize_weight("w2", i)
         for h in range(2):
             gather_words(h)
@@ -193,12 +194,11 @@ def tile_picked_expertpair_silu_p_kernel(
         quantize_hidden("w2", 1, sbuf("z_codes_w2_1", [P, S // 2], U32, tag="w4_raw"))
         quantize_weight("w4", 1)
         quantize_hidden("w1", 0, sbuf("z_codes_w1_0", [P, S // 2], U32))
-        round_on_vector("w3", 0, ALL_QUADS, 1.0)
-        round_on_scalar("w3", 1, ALL_QUADS)
+        round_shared("w3", W3_ON_SCALAR)
         gather_share(last, 0)
         for i in range(2):
             quantize_weight("w3", i)
-        quantize_hidden("w1", 1, reused("z_codes_w1_1", [P, S // 2], U32, W3_OFFSET))
+        quantize_hidden("w1", 1, reused("z_codes_w1_1", [P, S // 2], U32, RAW_OFFSET["w3"] + 8 * S))
 
         units = [[(0, 0), (1, 0)], [(0, 1), (1, 1)], [(2, 0), (2, 1)], [(3, 0), (3, 1)]]
         diff_bank = [psum.tile([P, S], F32, name="diff%d" % u, tag=tag) for u, tag in enumerate(("A0", "A1", "B0", "B2"))]
@@ -220,7 +220,7 @@ def tile_picked_expertpair_silu_p_kernel(
             passes(b_bank[u], "w4", "w2", u, True, True)
 
         scaled = [sbuf("scaled%d" % u, [P, S], F32) for u in range(len(units))]
-        b_both = sbuf("b_both", [P, 2, S], F32, tag="w3_raw")
+        b_both = reused("b_both", [P, 2, S], F32, RAW_OFFSET["w3"])
         b_sb = [b_both[:, u, :] for u in range(2)]
 
         def place(u, part):

@@ -19,14 +19,13 @@ P = 128
 PACK = 4
 GROUP = 16
 QUADRANT = 32
+RAW_BYTES = PACK * H * 4
 ALL = slice(0, S)
 ALL_QUADS = slice(0, P)
-SECOND_PAIR_ON_SCALAR = 40
-RAW_OFFSET = {"w1": 0, "w3": PACK * H * 4}
-W3_ON_SCALAR = 96
-W2_ON_VECTOR = 80
 PAIRS = (slice(0, 2), slice(2, PACK))
 HALVES = (slice(0, S // 2), slice(S // 2, S))
+W2_ON_VECTOR = 40
+W1_ON_SCALAR = 48
 
 
 def tile_picked_expertpair_silu_p_kernel(
@@ -38,15 +37,16 @@ def tile_picked_expertpair_silu_p_kernel(
         shared = ctx.enter_context(tc.tile_pool(name="shared", bufs=1))
         psum = ctx.enter_context(tc.psum_pool(name="psum", bufs=1))
 
-        def reused(name, shape, dtype, offset):
-            return shared.tile(shape, dtype, name=name, offset=offset, align_bytes=64)
-
-        def sbuf(name, shape, dtype, tag=None):
-            return keep.tile(shape, dtype, name=name, tag=tag or name, align_bytes=64)
+        def sbuf(name, shape, dtype, at=None):
+            if at is None:
+                return keep.tile(shape, dtype, name=name, tag=name, align_bytes=64)
+            return shared.tile(shape, dtype, name=name, offset=at, align_bytes=64)
 
         def entries(list_tile, cols):
             return list_tile[:, cols.start // GROUP : cols.stop // GROUP]
 
+        weights = {"w1": w1, "w2": w2, "w3": w3, "w4": w4}
+        raw_at = {name: i * RAW_BYTES for i, name in enumerate(weights)}
         task_sb = sbuf("task_sb", [P, S // GROUP], U16)
         offs_sb = sbuf("offs_sb", [P, S // GROUP], U16)
         table_words = sbuf("table_words", [P, T], U32)
@@ -54,19 +54,10 @@ def tile_picked_expertpair_silu_p_kernel(
         mix_rows = mix.rearrange("(p t) u -> p t u", t=PACK)
         out_rows = out.rearrange("(p t) j -> p t j", t=PACK)
         mix_sb = [sbuf("mix%d" % t, [P, U], F32) for t in range(PACK)]
-        share = [[sbuf("share%d_%d" % (t, h), [P, S // 2], F32) for h in range(2)] for t in range(2)]
-        share.append(sbuf("share2", [P, S], F32))
-        share.append([sbuf("share3_0", [P, S // 2], F32)])
-        weights = {"w1": w1, "w2": w2, "w3": w3, "w4": w4}
-        w_raw, w_bf16, w_codes, w_scales = {}, {}, {}, {}
-        for name in weights:
-            if name in RAW_OFFSET:
-                w_raw[name] = reused(name + "_raw", [P, PACK, H], F32, RAW_OFFSET[name])
-            else:
-                w_raw[name] = sbuf(name + "_raw", [P, PACK, H], F32)
-            w_bf16[name] = [sbuf("%s_bf16_%d" % (name, i), [P, 2 * PACK * P], BF16) for i in range(2)]
-            w_codes[name] = [sbuf("%s_codes%d" % (name, i), [P, 2 * P], U32) for i in range(2)]
-            w_scales[name] = [sbuf("%s_scales%d" % (name, i), [P, 2 * P], U8) for i in range(2)]
+        w_raw = {name: sbuf(name + "_raw", [P, PACK, H], F32, raw_at[name]) for name in weights}
+        w_bf16 = {name: [sbuf("%s_bf16_%d" % (name, i), [P, 2 * PACK * P], BF16) for i in range(2)] for name in weights}
+        w_codes = {name: [sbuf("%s_codes%d" % (name, i), [P, 2 * P], U32) for i in range(2)] for name in weights}
+        w_scales = {name: [sbuf("%s_scales%d" % (name, i), [P, 2 * P], U8) for i in range(2)] for name in weights}
 
         def load_mix(t):
             nc.sync.dma_start(out=mix_sb[t][:], in_=mix_rows[:, t, :])
@@ -74,23 +65,30 @@ def tile_picked_expertpair_silu_p_kernel(
         def load_weight(name):
             nc.sync.dma_start(out=w_raw[name][:], in_=weights[name].rearrange("(p j) c -> p j c", j=PACK))
 
+        def load_scale_rows():
+            for r in range(PACK):
+                nc.sync.dma_start(
+                    out=table_scales[r:P:QUADRANT, :].bitcast(I32),
+                    in_=x_scales[0, r : PACK * PACK : PACK, :].bitcast(I32),
+                )
+
+        def load_words():
+            nc.sync.dma_start(
+                out=table_words[:].bitcast(I32), in_=x_words[0].rearrange("p n t -> p (n t)").bitcast(I32)
+            )
+
         def rounding_views(name, i, quads):
             dst = w_bf16[name][i][:].rearrange("p (t m j) -> p m j t", t=2, j=PACK)[:, quads]
             src = w_raw[name][:].rearrange("p j (m t) -> p m j t", t=PACK)[:, quads, :, PAIRS[i]]
             return dst, src
 
-        def round_on_vector(name, i, quads, sign):
+        def round_on_vector(name, i, quads):
             dst, src = rounding_views(name, i, quads)
-            nc.vector.tensor_scalar(dst, src, sign, None, ALU.mult)
+            nc.vector.tensor_scalar(dst, src, -1.0 if name == "w4" else 1.0, None, ALU.mult)
 
         def round_on_scalar(name, i, quads):
             dst, src = rounding_views(name, i, quads)
             nc.scalar.copy(dst, src)
-
-        def round_shared(name, on_scalar):
-            round_on_vector(name, 0, ALL_QUADS, 1.0)
-            round_on_scalar(name, 1, slice(0, on_scalar))
-            round_on_vector(name, 1, slice(on_scalar, P), 1.0)
 
         def quantize(codes, scales, values):
             nc.vector.quantize_mx(out=codes.bitcast(FP8X4), scales=scales, in_=values)
@@ -110,149 +108,142 @@ def tile_picked_expertpair_silu_p_kernel(
                 stop=stop,
             )
 
-        nc.vector.memset(table_scales[:, : T // 2].bitcast(I32), 0)
-        nc.gpsimd.memset(table_scales[:, T // 2 :].bitcast(I32), 0)
-        load_mix(0)
-        nc.sync.dma_start(task_sb[:], task)
-        load_mix(1)
-        nc.sync.dma_start(offs_sb[:], offs)
-        load_weight("w2")
-        for r in range(PACK):
-            nc.sync.dma_start(
-                out=table_scales[r:P:QUADRANT, :].bitcast(I32), in_=x_scales[0, r : PACK * PACK : PACK, :].bitcast(I32)
-            )
-        nc.sync.dma_start(out=table_words[:].bitcast(I32), in_=x_words[0].rearrange("p n t -> p (n t)").bitcast(I32))
-        load_mix(2)
-        load_weight("w1")
-        load_weight("w4")
-        load_weight("w3")
-        load_mix(3)
+        def shares_on_vector(dst, t, cols):
+            nc.vector.tensor_copy(dst, mix_sb[t][:].indirect(entries(task_sb, cols)))
 
-        def share_view(t, cols):
-            if t == 2:
-                return share[t][:, cols]
-            return share[t][cols.start // (S // 2)][:]
-
-        def gather_share(t, h):
-            nc.vector.tensor_copy(share_view(t, HALVES[h]), mix_sb[t][:].indirect(entries(task_sb, HALVES[h])))
+        def shares_on_scalar(dst, t, cols):
+            nc.scalar.activation(dst, mix_sb[t][:].indirect(entries(task_sb, cols)), ACT.Copy)
 
         x_bytes = sbuf("x_bytes", [P, S], U8)
-        x_codes = [sbuf("x_codes%d" % h, [P, S // 2], U32) for h in range(2)]
+        x_codes = [sbuf("x_codes%d" % c, [P, P], U32) for c in range(PACK)]
 
-        def gather_words(h):
-            nc.vector.tensor_copy(x_codes[h][:], table_words[:].indirect(entries(offs_sb, HALVES[h])))
+        def gather_bytes():
+            nc.vector.tensor_copy(x_bytes[:], table_scales[:].indirect(offs_sb[:]))
 
-        for t in range(2):
-            for h in range(2):
-                gather_share(t, h)
-        round_on_vector("w2", 0, slice(0, W2_ON_VECTOR), 1.0)
-        round_on_scalar("w2", 1, ALL_QUADS)
-        round_on_scalar("w2", 0, slice(W2_ON_VECTOR, P))
-        nc.vector.tensor_copy(x_bytes[:], table_scales[:].indirect(offs_sb[:]))
-        for i in (1, 0):
-            quantize_weight("w2", i)
-        for h in range(2):
-            gather_words(h)
-        for h in range(2):
-            gather_share(2, h)
-
-        z_bf16 = {name: [sbuf("z_bf16_%s_0" % name, [P, PACK * S // 2], BF16)] for name in ("w2", "w1")}
-        z_bf16["w1"].append(sbuf("z_bf16_w1_1", [P, PACK * S // 2], BF16))
-        z_codes = {"w1": [], "w2": []}
-        z_scales = {name: [sbuf("z_scales_%s_%d" % (name, h), [P, S // 2], U8) for h in range(2)] for name in z_codes}
-
-        def quantize_hidden(name, h, codes):
-            z_codes[name].append(codes)
-            quantize(codes[:], z_scales[name][h][:], z_bf16[name][h][:])
-
-        def hidden(name, c, tag):
+        def gather_words(c):
             cols = slice(c * P, (c + 1) * P)
-            bank = psum.tile([P, PACK, P], F32, name="hidden_%s_%d" % (name, c), tag=tag)
-            codes = x_codes[c // 2][:, c % 2 * P : (c % 2 + 1) * P]
+            nc.vector.tensor_copy(x_codes[c][:], table_words[:].indirect(entries(offs_sb, cols)))
+
+        def bank(name, tag):
+            return psum.tile([P, S], F32, name=name, tag=tag)
+
+        def hidden(name, c, tag, dst):
+            cols = slice(c * P, (c + 1) * P)
+            acc = bank("hidden_%s_%d" % (name, c), tag)
             for t in range(PACK):
-                product(bank[:, t, :], name, t, codes, x_bytes[:, cols], True, True)
-            dst = z_bf16[name][c // 2][:, c % 2 * PACK * P : (c % 2 + 1) * PACK * P]
+                product(acc[:, t * P : (t + 1) * P], name, t, x_codes[c][:], x_bytes[:, cols], True, True)
+            part = dst[:, c % 2 * PACK * P : (c % 2 + 1) * PACK * P]
             nc.scalar.activation(
-                dst.rearrange("p (n t) -> p n t", t=PACK), bank[:].rearrange("p t n -> p n t"), ACT.Silu
+                part.rearrange("p (n t) -> p n t", t=PACK), acc[:].rearrange("p (t n) -> p n t", t=PACK), ACT.Silu
             )
 
-        last = PACK - 1
+        nc.vector.memset(table_scales[:, : T // 2].bitcast(I32), 0)
+        nc.gpsimd.memset(table_scales[:, T // 2 :].bitcast(I32), 0)
+        nc.sync.dma_start(out=mix_sb[0][0:P:2, :], in_=mix_rows[0:P:2, 0, :])
+        nc.sync.dma_start(task_sb[:], task)
+        nc.sync.dma_start(out=mix_sb[0][1:P:2, :], in_=mix_rows[1:P:2, 0, :])
+        nc.sync.dma_start(offs_sb[:], offs)
+        load_weight("w2")
+        load_scale_rows()
+        load_words()
+        load_mix(1)
+        for name in ("w1", "w4", "w3"):
+            load_weight(name)
+        load_mix(2)
+        load_mix(3)
+
+        share = [sbuf("share%d" % t, [P, S], F32) for t in range(PACK)]
+        for half in HALVES:
+            shares_on_vector(share[0][:, half], 0, half)
+        round_on_vector("w2", 0, slice(0, W2_ON_VECTOR))
+        round_on_scalar("w2", 1, ALL_QUADS)
+        round_on_scalar("w2", 0, slice(W2_ON_VECTOR, P))
+        gather_bytes()
+        for i in (1, 0):
+            quantize_weight("w2", i)
+        for c in range(PACK):
+            gather_words(c)
+        for half in HALVES:
+            shares_on_vector(share[1][:, half], 1, half)
+
+        half_bytes = PACK * S
+        z2_bf16 = [sbuf("z2_bf16_0", [P, PACK * S // 2], BF16)]
         for c in range(2):
-            hidden("w2", c, "A%d" % c)
-        round_shared("w1", SECOND_PAIR_ON_SCALAR)
-        z_bf16["w2"].append(reused("z_bf16_w2_1", [P, PACK * S // 2], BF16, 0))
+            hidden("w2", c, "A%d" % c, z2_bf16[0])
+        round_on_vector("w1", 0, ALL_QUADS)
+        round_on_scalar("w1", 1, slice(0, W1_ON_SCALAR))
+        round_on_vector("w1", 1, slice(W1_ON_SCALAR, P))
+        z2_bf16.append(sbuf("z2_bf16_1", [P, PACK * S // 2], BF16, raw_at["w1"]))
         for c in range(2, PACK):
-            hidden("w2", c, "A%d" % (c - 2))
+            hidden("w2", c, "A%d" % (c % 2), z2_bf16[1])
         for i in range(2):
             quantize_weight("w1", i)
-        quantize_hidden("w2", 0, reused("z_codes_w2_0", [P, S // 2], U32, PACK * S))
-        for c, tag in enumerate(("B0", "B1", "B2", "B0")):
-            hidden("w1", c, tag)
-        for i in range(2):
-            round_on_vector("w4", i, ALL_QUADS, -1.0)
+        z2_codes = sbuf("z2_codes", [P, S], U32, raw_at["w1"] + half_bytes)
+        z2_scales = sbuf("z2_scales", [P, S], U8)
+        quantize(z2_codes[:, HALVES[0]], z2_scales[:, HALVES[0]], z2_bf16[0][:])
+        z_bf16 = [sbuf("z_bf16_%d" % h, [P, PACK * S // 2], BF16) for h in range(2)]
+        for c in range(PACK):
+            hidden("w1", c, "B%d" % (c % 2), z_bf16[c // 2])
+        quantize(z2_codes[:, HALVES[1]], z2_scales[:, HALVES[1]], z2_bf16[1][:])
+        round_on_vector("w4", 0, ALL_QUADS)
+        round_on_vector("w4", 1, slice(0, P // 2))
         quantize_weight("w4", 0)
-        quantize_hidden("w2", 1, sbuf("z_codes_w2_1", [P, S // 2], U32, tag="w4_raw"))
+        round_on_vector("w4", 1, slice(P // 2, P))
+        z_codes = sbuf("z_codes", [P, S], U32)
+        z_scales = sbuf("z_scales", [P, S], U8)
+        quantize(z_codes[:, HALVES[0]], z_scales[:, HALVES[0]], z_bf16[0][:])
         quantize_weight("w4", 1)
-        quantize_hidden("w1", 0, sbuf("z_codes_w1_0", [P, S // 2], U32))
-        round_shared("w3", W3_ON_SCALAR)
-        gather_share(last, 0)
+        round_on_vector("w3", 0, ALL_QUADS)
+        round_on_scalar("w3", 1, ALL_QUADS)
+        quantize(z_codes[:, HALVES[1]], z_scales[:, HALVES[1]], z_bf16[1][:])
         for i in range(2):
             quantize_weight("w3", i)
-        quantize_hidden("w1", 1, reused("z_codes_w1_1", [P, S // 2], U32, RAW_OFFSET["w3"] + 8 * S))
 
-        units = [[(0, 0), (1, 0)], [(0, 1), (1, 1)], [(2, 0), (2, 1)], [(3, 0), (3, 1)]]
-        diff_bank = [psum.tile([P, S], F32, name="diff%d" % u, tag=tag) for u, tag in enumerate(("A0", "A1", "B0", "B2"))]
-        b_bank = [psum.tile([P, S], F32, name="b%d" % u, tag=tag) for u, tag in enumerate(("B3", "A2", "A3"))]
+        diff = [bank("diff%d" % t, tag) for t, tag in enumerate(("A0", "A1", "B2", "B3"))]
+        minus_b = []
 
-        def passes(bank, name, z_name, u, start, stop):
-            for i, (t, h) in enumerate(units[u]):
-                product(bank[:, HALVES[i]], name, t, z_codes[z_name][h][:], z_scales[z_name][h][:],
-                        start and i == 0, stop and i == 1)
+        def second_alone(t, tag):
+            minus_b.append(bank("minus_b%d" % t, tag))
+            product(minus_b[t][:], "w4", t, z2_codes[:], z2_scales[:], True, True)
 
-        for u in (0, 2, 1, last):
-            passes(diff_bank[u], "w4", "w2", u, True, False)
-            passes(diff_bank[u], "w3", "w1", u, False, True)
-            if u < last:
-                passes(b_bank[u], "w4", "w2", u, True, True)
+        for t in range(2):
+            product(diff[t][:], "w4", t, z2_codes[:], z2_scales[:], True, False)
+        for t in range(2):
+            second_alone(t, "A%d" % (2 + t))
+        for t in range(2, PACK):
+            product(diff[t][:], "w4", t, z2_codes[:], z2_scales[:], True, False)
+        for t in range(PACK):
+            product(diff[t][:], "w3", t, z_codes[:], z_scales[:], False, True)
 
-        def late_b(u, tag):
-            b_bank.append(psum.tile([P, S], F32, name="b%d" % u, tag=tag))
-            passes(b_bank[u], "w4", "w2", u, True, True)
+        b1_sb = sbuf("b1_sb", [P, S], F32, raw_at["w3"])
+        b2_sb = sbuf("b2_sb", [P, S // 2], F32, raw_at["w3"] + 4 * S)
+        shares_on_scalar(share[2][:, HALVES[0]], 2, HALVES[0])
+        nc.scalar.copy(b1_sb[:], minus_b[1][:])
+        second_alone(2, "A3")
+        shares_on_scalar(share[2][:, HALVES[1]], 2, HALVES[1])
+        shares_on_scalar(share[3][:, HALVES[0]], 3, HALVES[0])
+        nc.scalar.copy(b2_sb[:], minus_b[2][:, HALVES[0]])
+        shares_on_scalar(share[3][:, HALVES[1]], 3, HALVES[1])
 
-        scaled = [sbuf("scaled%d" % u, [P, S], F32) for u in range(len(units))]
-        b_both = reused("b_both", [P, 2, S], F32, RAW_OFFSET["w3"])
-        b_sb = [b_both[:, u, :] for u in range(2)]
+        scaled = [sbuf("scaled%d" % t, [P, S], F32) for t in range(PACK)]
 
-        def place(u, part):
-            t, h = units[u][part.start // (S // 2)]
-            first = HALVES[h].start
-            return t, slice(first, first + part.stop - part.start)
+        def scale(t, cols):
+            nc.vector.tensor_tensor(scaled[t][:, cols], diff[t][:, cols], share[t][:, cols], ALU.mult)
 
-        def finish(engine, queue, b, u, part):
-            t, cols = place(u, part)
-            result = sbuf("result%d_%d" % (u, part.start), [P, part.stop - part.start], F32)
-            engine.tensor_tensor(result[:], scaled[u][:, part], b[:, part], ALU.subtract)
-            queue.dma_start(out=out_rows[:, t, cols], in_=result[:])
+        def finish(engine, b, t, cols):
+            result = sbuf("result%d_%d" % (t, cols.start), [P, cols.stop - cols.start], F32)
+            engine.tensor_tensor(result[:], scaled[t][:, cols], b[:, cols], ALU.subtract)
+            nc.sync.dma_start(out=out_rows[:, t, cols], in_=result[:])
 
-        def scale(u, part):
-            t, cols = place(u, part)
-            nc.vector.tensor_tensor(scaled[u][:, part], diff_bank[u][:, part], share_view(t, cols), ALU.mult)
-
-        for u in range(2):
-            nc.scalar.copy(b_sb[u], b_bank[u][:])
-        for part in HALVES:
-            scale(0, part)
-        late_b(last, "A0")
+        scale(0, ALL)
+        second_alone(3, "A0")
+        scale(1, ALL)
+        finish(nc.vector, minus_b[0], 0, ALL)
+        finish(nc.gpsimd, b1_sb, 1, ALL)
         scale(2, ALL)
-        scale(1, HALVES[0])
-        finish(nc.vector, nc.sync, b_bank[2], 2, ALL)
-        scale(1, HALVES[1])
-        share[last].append(sbuf("share3_1", [P, S // 2], F32, tag="share2"))
-        gather_share(last, 1)
-        for part in HALVES:
-            scale(last, part)
-        for u in range(2):
-            for part in HALVES:
-                finish(nc.gpsimd, nc.scalar, b_sb[u], u, part)
-        for part in HALVES:
-            finish(nc.vector, nc.sync, b_bank[last], last, part)
+        scale(3, HALVES[0])
+        finish(nc.vector, minus_b[2], 2, HALVES[1])
+        finish(nc.gpsimd, b2_sb, 2, HALVES[0])
+        scale(3, HALVES[1])
+        for half in HALVES:
+            finish(nc.vector, minus_b[3], 3, half)

@@ -24,8 +24,8 @@ ALL = slice(0, S)
 ALL_QUADS = slice(0, P)
 PAIRS = (slice(0, 2), slice(2, PACK))
 HALVES = (slice(0, S // 2), slice(S // 2, S))
-W2_ON_VECTOR = 40
-W1_ON_SCALAR = 48
+W2_ON_VECTOR = 64
+W3_ON_SCALAR = 96
 
 
 def tile_picked_expertpair_silu_p_kernel(
@@ -139,22 +139,23 @@ def tile_picked_expertpair_silu_p_kernel(
 
         nc.vector.memset(table_scales[:, : T // 2].bitcast(I32), 0)
         nc.gpsimd.memset(table_scales[:, T // 2 :].bitcast(I32), 0)
-        nc.sync.dma_start(out=mix_sb[0][0:P:2, :], in_=mix_rows[0:P:2, 0, :])
+        load_mix(0)
         nc.sync.dma_start(task_sb[:], task)
-        nc.sync.dma_start(out=mix_sb[0][1:P:2, :], in_=mix_rows[1:P:2, 0, :])
+        load_mix(1)
         nc.sync.dma_start(offs_sb[:], offs)
         load_weight("w2")
         load_scale_rows()
         load_words()
-        load_mix(1)
+        load_mix(2)
         for name in ("w1", "w4", "w3"):
             load_weight(name)
-        load_mix(2)
         load_mix(3)
 
-        share = [sbuf("share%d" % t, [P, S], F32) for t in range(PACK)]
-        for half in HALVES:
-            shares_on_vector(share[0][:, half], 0, half)
+        first_shares = sbuf("first_shares", [P, 2, S], F32)
+        share = [first_shares[:, 0, :], first_shares[:, 1, :], sbuf("share2", [P, S], F32), sbuf("share3", [P, S], F32)]
+        for t in range(2):
+            for half in HALVES:
+                shares_on_vector(share[t][:, half], t, half)
         round_on_vector("w2", 0, slice(0, W2_ON_VECTOR))
         round_on_scalar("w2", 1, ALL_QUADS)
         round_on_scalar("w2", 0, slice(W2_ON_VECTOR, P))
@@ -164,86 +165,105 @@ def tile_picked_expertpair_silu_p_kernel(
         for c in range(PACK):
             gather_words(c)
         for half in HALVES:
-            shares_on_vector(share[1][:, half], 1, half)
+            shares_on_vector(share[2][:, half], 2, half)
 
-        half_bytes = PACK * S
-        z2_bf16 = [sbuf("z2_bf16_0", [P, PACK * S // 2], BF16)]
-        for c in range(2):
-            hidden("w2", c, "A%d" % c, z2_bf16[0])
-        round_on_vector("w1", 0, ALL_QUADS)
-        round_on_scalar("w1", 1, slice(0, W1_ON_SCALAR))
-        round_on_vector("w1", 1, slice(W1_ON_SCALAR, P))
-        z2_bf16.append(sbuf("z2_bf16_1", [P, PACK * S // 2], BF16, raw_at["w1"]))
-        for c in range(2, PACK):
-            hidden("w2", c, "A%d" % (c % 2), z2_bf16[1])
+        z2_bf16 = sbuf("z2_bf16", [P, PACK * S], BF16)
+        for c in range(PACK):
+            hidden("w2", c, "A%d" % (c % 2), z2_bf16[:, c // 2 * 2 * S : (c // 2 + 1) * 2 * S])
+        for i in range(2):
+            round_on_vector("w1", i, ALL_QUADS)
         for i in range(2):
             quantize_weight("w1", i)
-        z2_codes = sbuf("z2_codes", [P, S], U32, raw_at["w1"] + half_bytes)
+        z2_codes = sbuf("z2_codes", [P, S], U32, raw_at["w1"])
         z2_scales = sbuf("z2_scales", [P, S], U8)
-        quantize(z2_codes[:, HALVES[0]], z2_scales[:, HALVES[0]], z2_bf16[0][:])
+        quantize(z2_codes[:], z2_scales[:], z2_bf16[:])
         z_bf16 = [sbuf("z_bf16_%d" % h, [P, PACK * S // 2], BF16) for h in range(2)]
         for c in range(PACK):
-            hidden("w1", c, "B%d" % (c % 2), z_bf16[c // 2])
-        quantize(z2_codes[:, HALVES[1]], z2_scales[:, HALVES[1]], z2_bf16[1][:])
+            hidden("w1", c, "B%d" % (c % 3), z_bf16[c // 2])
         round_on_vector("w4", 0, ALL_QUADS)
         round_on_vector("w4", 1, slice(0, P // 2))
         quantize_weight("w4", 0)
         round_on_vector("w4", 1, slice(P // 2, P))
-        z_codes = sbuf("z_codes", [P, S], U32)
-        z_scales = sbuf("z_scales", [P, S], U8)
-        quantize(z_codes[:, HALVES[0]], z_scales[:, HALVES[0]], z_bf16[0][:])
+        z_codes = [sbuf("z_codes0", [P, S // 2], U32)]
+        z_scales = [sbuf("z_scales%d" % h, [P, S // 2], U8) for h in range(2)]
+        quantize(z_codes[0][:], z_scales[0][:], z_bf16[0][:])
         quantize_weight("w4", 1)
         round_on_vector("w3", 0, ALL_QUADS)
-        round_on_scalar("w3", 1, ALL_QUADS)
-        quantize(z_codes[:, HALVES[1]], z_scales[:, HALVES[1]], z_bf16[1][:])
+        round_on_scalar("w3", 1, slice(0, W3_ON_SCALAR))
+        round_on_vector("w3", 1, slice(W3_ON_SCALAR, P))
         for i in range(2):
             quantize_weight("w3", i)
+        z_codes.append(sbuf("z_codes1", [P, S // 2], U32, raw_at["w3"] + 8 * S))
+        quantize(z_codes[1][:], z_scales[1][:], z_bf16[1][:])
 
-        diff = [bank("diff%d" % t, tag) for t, tag in enumerate(("A0", "A1", "B2", "B3"))]
-        minus_b = []
+        units = [[(0, 0), (1, 0)], [(0, 1), (1, 1)], [(2, 0), (2, 1)], [(3, 0), (3, 1)]]
+        diff = [bank("diff%d" % u, tag) for u, tag in enumerate(("A0", "A1", "B3", "B1"))]
+        minus_b = {}
 
-        def second_alone(t, tag):
-            minus_b.append(bank("minus_b%d" % t, tag))
-            product(minus_b[t][:], "w4", t, z2_codes[:], z2_scales[:], True, True)
+        def second_net(acc, u, stop):
+            if u < 2:
+                for t in range(2):
+                    product(acc[:, HALVES[t]], "w4", t, z2_codes[:, HALVES[u]], z2_scales[:, HALVES[u]],
+                            t == 0, stop and t == 1)
+            else:
+                product(acc[:], "w4", u, z2_codes[:], z2_scales[:], True, stop)
 
-        for t in range(2):
-            product(diff[t][:], "w4", t, z2_codes[:], z2_scales[:], True, False)
-        for t in range(2):
-            second_alone(t, "A%d" % (2 + t))
-        for t in range(2, PACK):
-            product(diff[t][:], "w4", t, z2_codes[:], z2_scales[:], True, False)
-        for t in range(PACK):
-            product(diff[t][:], "w3", t, z_codes[:], z_scales[:], False, True)
+        def second_alone(u, tag):
+            minus_b[u] = bank("minus_b%d" % u, tag)
+            second_net(minus_b[u], u, True)
 
-        b1_sb = sbuf("b1_sb", [P, S], F32, raw_at["w3"])
+        def first_net(u):
+            for i, (t, h) in enumerate(units[u]):
+                product(diff[u][:, HALVES[i]], "w3", t, z_codes[h][:], z_scales[h][:], False, i == 1)
+
+        for u in range(2):
+            second_net(diff[u], u, False)
+        for u in range(2):
+            second_alone(u, "A%d" % (2 + u))
+        for u in range(2, PACK):
+            second_net(diff[u], u, False)
+        second_alone(2, "B2")
+        for u in range(PACK):
+            first_net(u)
+
+        b0_sb = sbuf("b0_sb", [P, S], F32, raw_at["w3"])
         b2_sb = sbuf("b2_sb", [P, S // 2], F32, raw_at["w3"] + 4 * S)
-        shares_on_scalar(share[2][:, HALVES[0]], 2, HALVES[0])
-        nc.scalar.copy(b1_sb[:], minus_b[1][:])
-        second_alone(2, "A3")
-        shares_on_scalar(share[2][:, HALVES[1]], 2, HALVES[1])
+        nc.scalar.copy(b0_sb[:], minus_b[0][:])
         shares_on_scalar(share[3][:, HALVES[0]], 3, HALVES[0])
         nc.scalar.copy(b2_sb[:], minus_b[2][:, HALVES[0]])
         shares_on_scalar(share[3][:, HALVES[1]], 3, HALVES[1])
 
-        scaled = [sbuf("scaled%d" % t, [P, S], F32) for t in range(PACK)]
+        scaled = [sbuf("scaled%d" % u, [P, S], F32) for u in range(PACK)]
 
-        def scale(t, cols):
-            nc.vector.tensor_tensor(scaled[t][:, cols], diff[t][:, cols], share[t][:, cols], ALU.mult)
+        def scale(u, cols):
+            if u < 2:
+                nc.vector.tensor_tensor(
+                    scaled[u][:].rearrange("p (t j) -> p t j", t=2),
+                    diff[u][:].rearrange("p (t j) -> p t j", t=2),
+                    first_shares[:, :, HALVES[u]],
+                    ALU.mult,
+                )
+            else:
+                nc.vector.tensor_tensor(scaled[u][:, cols], diff[u][:, cols], share[u][:, cols], ALU.mult)
 
-        def finish(engine, b, t, cols):
-            result = sbuf("result%d_%d" % (t, cols.start), [P, cols.stop - cols.start], F32)
-            engine.tensor_tensor(result[:], scaled[t][:, cols], b[:, cols], ALU.subtract)
-            nc.sync.dma_start(out=out_rows[:, t, cols], in_=result[:])
+        def finish(engine, b, u, i):
+            t, h = units[u][i]
+            result = sbuf("result%d_%d" % (u, i), [P, S // 2], F32)
+            engine.tensor_tensor(result[:], scaled[u][:, HALVES[i]], b[:, HALVES[i]], ALU.subtract)
+            nc.sync.dma_start(out=out_rows[:, t, HALVES[h]], in_=result[:])
 
         scale(0, ALL)
         second_alone(3, "A0")
+        finish(nc.gpsimd, b0_sb, 0, 0)
         scale(1, ALL)
-        finish(nc.vector, minus_b[0], 0, ALL)
-        finish(nc.gpsimd, b1_sb, 1, ALL)
-        scale(2, ALL)
+        scale(2, HALVES[0])
+        finish(nc.vector, minus_b[1], 1, 0)
+        finish(nc.vector, minus_b[1], 1, 1)
+        finish(nc.gpsimd, b0_sb, 0, 1)
+        scale(2, HALVES[1])
         scale(3, HALVES[0])
-        finish(nc.vector, minus_b[2], 2, HALVES[1])
-        finish(nc.gpsimd, b2_sb, 2, HALVES[0])
+        finish(nc.vector, minus_b[2], 2, 1)
+        finish(nc.gpsimd, b2_sb, 2, 0)
         scale(3, HALVES[1])
-        for half in HALVES:
-            finish(nc.vector, minus_b[3], 3, half)
+        for i in range(2):
+            finish(nc.vector, minus_b[3], 3, i)

@@ -24,7 +24,7 @@ ALL = slice(0, S)
 ALL_QUADS = slice(0, P)
 PAIRS = (slice(0, 2), slice(2, PACK))
 HALVES = (slice(0, S // 2), slice(S // 2, S))
-W2_ON_VECTOR = 64
+W2_ON_VECTOR = 48
 W3_ON_SCALAR = 96
 
 
@@ -139,23 +139,24 @@ def tile_picked_expertpair_silu_p_kernel(
 
         nc.vector.memset(table_scales[:, : T // 2].bitcast(I32), 0)
         nc.gpsimd.memset(table_scales[:, T // 2 :].bitcast(I32), 0)
-        load_mix(0)
+        nc.sync.dma_start(out=mix_sb[0][0:P:2, :], in_=mix_rows[0:P:2, 0, :])
         nc.sync.dma_start(task_sb[:], task)
-        load_mix(1)
+        nc.sync.dma_start(out=mix_sb[0][1:P:2, :], in_=mix_rows[1:P:2, 0, :])
         nc.sync.dma_start(offs_sb[:], offs)
         load_weight("w2")
         load_scale_rows()
         load_words()
+        load_mix(1)
+        load_weight("w1")
         load_mix(2)
-        for name in ("w1", "w4", "w3"):
+        for name in ("w4", "w3"):
             load_weight(name)
         load_mix(3)
 
         first_shares = sbuf("first_shares", [P, 2, S], F32)
         share = [first_shares[:, 0, :], first_shares[:, 1, :], sbuf("share2", [P, S], F32), sbuf("share3", [P, S], F32)]
-        for t in range(2):
-            for half in HALVES:
-                shares_on_vector(share[t][:, half], t, half)
+        for half in HALVES:
+            shares_on_vector(share[0][:, half], 0, half)
         round_on_vector("w2", 0, slice(0, W2_ON_VECTOR))
         round_on_scalar("w2", 1, ALL_QUADS)
         round_on_scalar("w2", 0, slice(W2_ON_VECTOR, P))
@@ -165,11 +166,13 @@ def tile_picked_expertpair_silu_p_kernel(
         for c in range(PACK):
             gather_words(c)
         for half in HALVES:
-            shares_on_vector(share[2][:, half], 2, half)
+            shares_on_vector(share[1][:, half], 1, half)
 
         z2_bf16 = sbuf("z2_bf16", [P, PACK * S], BF16)
         for c in range(PACK):
             hidden("w2", c, "A%d" % (c % 2), z2_bf16[:, c // 2 * 2 * S : (c // 2 + 1) * 2 * S])
+        for half in HALVES:
+            shares_on_scalar(share[2][:, half], 2, half)
         for i in range(2):
             round_on_vector("w1", i, ALL_QUADS)
         for i in range(2):
@@ -239,12 +242,12 @@ def tile_picked_expertpair_silu_p_kernel(
             if u < 2:
                 nc.vector.tensor_tensor(
                     scaled[u][:].rearrange("p (t j) -> p t j", t=2),
-                    diff[u][:].rearrange("p (t j) -> p t j", t=2),
                     first_shares[:, :, HALVES[u]],
+                    diff[u][:].rearrange("p (t j) -> p t j", t=2),
                     ALU.mult,
                 )
             else:
-                nc.vector.tensor_tensor(scaled[u][:, cols], diff[u][:, cols], share[u][:, cols], ALU.mult)
+                nc.vector.tensor_tensor(scaled[u][:, cols], share[u][:, cols], diff[u][:, cols], ALU.mult)
 
         def finish(engine, b, u, i):
             t, h = units[u][i]

@@ -25,7 +25,8 @@ ALL_QUADS = slice(0, P)
 PAIRS = (slice(0, 2), slice(2, PACK))
 HALVES = (slice(0, S // 2), slice(S // 2, S))
 W2_ON_VECTOR = 48
-W3_ON_SCALAR = 96
+W3_ON_SCALAR = 48
+W4_ON_SCALAR = 40
 
 
 def tile_picked_expertpair_silu_p_kernel(
@@ -53,10 +54,15 @@ def tile_picked_expertpair_silu_p_kernel(
         table_scales = sbuf("table_scales", [P, T], U8)
         mix_rows = mix.rearrange("(p t) u -> p t u", t=PACK)
         out_rows = out.rearrange("(p t) j -> p t j", t=PACK)
-        mix_sb = [sbuf("mix%d" % t, [P, U], F32) for t in range(PACK)]
+        mix_at = [(PACK + 1) * RAW_BYTES + t * U * 4 for t in range(PACK)]
+        mix_sb = [sbuf("mix%d" % t, [P, U], F32, mix_at[t]) for t in range(PACK)]
         w_raw = {name: sbuf(name + "_raw", [P, PACK, H], F32, raw_at[name]) for name in weights}
         w_bf16 = {name: [sbuf("%s_bf16_%d" % (name, i), [P, 2 * PACK * P], BF16) for i in range(2)] for name in weights}
-        w_codes = {name: [sbuf("%s_codes%d" % (name, i), [P, 2 * P], U32) for i in range(2)] for name in weights}
+        codes_at = {name: PACK * RAW_BYTES + i * PACK * P * 4 for i, name in enumerate(weights)}
+        w_codes = {
+            name: [sbuf("%s_codes%d" % (name, i), [P, 2 * P], U32, codes_at[name] + i * 2 * P * 4) for i in range(2)]
+            for name in weights
+        }
         w_scales = {name: [sbuf("%s_scales%d" % (name, i), [P, 2 * P], U8) for i in range(2)] for name in weights}
 
         def load_mix(t):
@@ -88,7 +94,10 @@ def tile_picked_expertpair_silu_p_kernel(
 
         def round_on_scalar(name, i, quads):
             dst, src = rounding_views(name, i, quads)
-            nc.scalar.copy(dst, src)
+            if name == "w4":
+                nc.scalar.mul(dst, src, -1.0)
+            else:
+                nc.scalar.copy(dst, src)
 
         def quantize(codes, scales, values):
             nc.vector.quantize_mx(out=codes.bitcast(FP8X4), scales=scales, in_=values)
@@ -108,19 +117,22 @@ def tile_picked_expertpair_silu_p_kernel(
                 stop=stop,
             )
 
-        def shares_on_vector(dst, t, cols):
-            nc.vector.tensor_copy(dst, mix_sb[t][:].indirect(entries(task_sb, cols)))
+        def shares_on_vector(t, h, at=None):
+            share[t, h] = sbuf("share%d_%d" % (t, h), [P, S // 2], F32, at)
+            nc.vector.tensor_copy(share[t, h][:], mix_sb[t][:].indirect(entries(task_sb, HALVES[h])))
 
-        def shares_on_scalar(dst, t, cols):
-            nc.scalar.activation(dst, mix_sb[t][:].indirect(entries(task_sb, cols)), ACT.Copy)
+        def shares_on_scalar(t, h, at=None):
+            share[t, h] = sbuf("share%d_%d" % (t, h), [P, S // 2], F32, at)
+            nc.scalar.activation(share[t, h][:], mix_sb[t][:].indirect(entries(task_sb, HALVES[h])), ACT.Copy)
 
         x_bytes = sbuf("x_bytes", [P, S], U8)
-        x_codes = [sbuf("x_codes%d" % c, [P, P], U32) for c in range(PACK)]
+        x_codes = {}
 
         def gather_bytes():
             nc.vector.tensor_copy(x_bytes[:], table_scales[:].indirect(offs_sb[:]))
 
-        def gather_words(c):
+        def gather_words(c, at=None):
+            x_codes[c] = sbuf("x_codes%d" % c, [P, P], U32, at)
             cols = slice(c * P, (c + 1) * P)
             nc.vector.tensor_copy(x_codes[c][:], table_words[:].indirect(entries(offs_sb, cols)))
 
@@ -148,15 +160,14 @@ def tile_picked_expertpair_silu_p_kernel(
         load_words()
         load_mix(1)
         load_weight("w1")
-        load_mix(2)
         for name in ("w4", "w3"):
             load_weight(name)
+        load_mix(2)
         load_mix(3)
 
-        first_shares = sbuf("first_shares", [P, 2, S], F32)
-        share = [first_shares[:, 0, :], first_shares[:, 1, :], sbuf("share2", [P, S], F32), sbuf("share3", [P, S], F32)]
-        for half in HALVES:
-            shares_on_vector(share[0][:, half], 0, half)
+        share = {}
+        for h in range(2):
+            shares_on_vector(0, h)
         round_on_vector("w2", 0, slice(0, W2_ON_VECTOR))
         round_on_scalar("w2", 1, ALL_QUADS)
         round_on_scalar("w2", 0, slice(W2_ON_VECTOR, P))
@@ -165,14 +176,12 @@ def tile_picked_expertpair_silu_p_kernel(
             quantize_weight("w2", i)
         for c in range(PACK):
             gather_words(c)
-        for half in HALVES:
-            shares_on_vector(share[1][:, half], 1, half)
+        for h in range(2):
+            shares_on_vector(1, h)
 
         z2_bf16 = sbuf("z2_bf16", [P, PACK * S], BF16)
         for c in range(PACK):
             hidden("w2", c, "A%d" % (c % 2), z2_bf16[:, c // 2 * 2 * S : (c // 2 + 1) * 2 * S])
-        for half in HALVES:
-            shares_on_scalar(share[2][:, half], 2, half)
         for i in range(2):
             round_on_vector("w1", i, ALL_QUADS)
         for i in range(2):
@@ -180,13 +189,15 @@ def tile_picked_expertpair_silu_p_kernel(
         z2_codes = sbuf("z2_codes", [P, S], U32, raw_at["w1"])
         z2_scales = sbuf("z2_scales", [P, S], U8)
         quantize(z2_codes[:], z2_scales[:], z2_bf16[:])
+        round_on_scalar("w4", 1, slice(0, W4_ON_SCALAR))
         z_bf16 = [sbuf("z_bf16_%d" % h, [P, PACK * S // 2], BF16) for h in range(2)]
         for c in range(PACK):
-            hidden("w1", c, "B%d" % (c % 3), z_bf16[c // 2])
+            hidden("w1", c, "B%d" % c, z_bf16[c // 2])
+        w4_cut = (W4_ON_SCALAR + P) // 2
         round_on_vector("w4", 0, ALL_QUADS)
-        round_on_vector("w4", 1, slice(0, P // 2))
+        round_on_vector("w4", 1, slice(W4_ON_SCALAR, w4_cut))
         quantize_weight("w4", 0)
-        round_on_vector("w4", 1, slice(P // 2, P))
+        round_on_vector("w4", 1, slice(w4_cut, P))
         z_codes = [sbuf("z_codes0", [P, S // 2], U32)]
         z_scales = [sbuf("z_scales%d" % h, [P, S // 2], U8) for h in range(2)]
         quantize(z_codes[0][:], z_scales[0][:], z_bf16[0][:])
@@ -200,73 +211,64 @@ def tile_picked_expertpair_silu_p_kernel(
         quantize(z_codes[1][:], z_scales[1][:], z_bf16[1][:])
 
         units = [[(0, 0), (1, 0)], [(0, 1), (1, 1)], [(2, 0), (2, 1)], [(3, 0), (3, 1)]]
-        diff = [bank("diff%d" % u, tag) for u, tag in enumerate(("A0", "A1", "B3", "B1"))]
+        diff = [bank("diff%d" % u, tag) for u, tag in enumerate(("A0", "A1", "B0", "B1"))]
         minus_b = {}
 
-        def second_net(acc, u, stop):
+        def second_net(u):
             if u < 2:
                 for t in range(2):
-                    product(acc[:, HALVES[t]], "w4", t, z2_codes[:, HALVES[u]], z2_scales[:, HALVES[u]],
-                            t == 0, stop and t == 1)
+                    product(diff[u][:, HALVES[t]], "w4", t, z2_codes[:, HALVES[u]], z2_scales[:, HALVES[u]],
+                            t == 0, False)
             else:
-                product(acc[:], "w4", u, z2_codes[:], z2_scales[:], True, stop)
+                product(diff[u][:], "w4", u, z2_codes[:], z2_scales[:], True, False)
 
-        def second_alone(u, tag):
-            minus_b[u] = bank("minus_b%d" % u, tag)
-            second_net(minus_b[u], u, True)
+        def second_alone(t, tag):
+            minus_b[t] = bank("minus_b%d" % t, tag)
+            product(minus_b[t][:], "w4", t, z2_codes[:], z2_scales[:], True, True)
 
         def first_net(u):
             for i, (t, h) in enumerate(units[u]):
                 product(diff[u][:, HALVES[i]], "w3", t, z_codes[h][:], z_scales[h][:], False, i == 1)
 
         for u in range(2):
-            second_net(diff[u], u, False)
-        for u in range(2):
-            second_alone(u, "A%d" % (2 + u))
+            second_net(u)
+        second_alone(1, "A2")
+        second_alone(0, "A3")
         for u in range(2, PACK):
-            second_net(diff[u], u, False)
-        second_alone(2, "B2")
+            second_net(u)
         for u in range(PACK):
             first_net(u)
 
-        b0_sb = sbuf("b0_sb", [P, S], F32, raw_at["w3"])
-        b2_sb = sbuf("b2_sb", [P, S // 2], F32, raw_at["w3"] + 4 * S)
-        nc.scalar.copy(b0_sb[:], minus_b[0][:])
-        shares_on_scalar(share[3][:, HALVES[0]], 3, HALVES[0])
-        nc.scalar.copy(b2_sb[:], minus_b[2][:, HALVES[0]])
-        shares_on_scalar(share[3][:, HALVES[1]], 3, HALVES[1])
+        b1_sb = sbuf("b1_sb", [P, S], F32, raw_at["w3"])
+        b2_sb = sbuf("b2_sb", [P, S], F32, raw_at["w3"] + 4 * S)
+        nc.scalar.copy(b1_sb[:], minus_b[1][:])
+        for h in range(2):
+            shares_on_scalar(2, h)
 
-        scaled = [sbuf("scaled%d" % u, [P, S], F32) for u in range(PACK)]
+        scaled = [sbuf("scaled%d" % t, [P, S], F32) for t in range(PACK)]
 
-        def scale(u, cols):
-            if u < 2:
-                nc.vector.tensor_tensor(
-                    scaled[u][:].rearrange("p (t j) -> p t j", t=2),
-                    first_shares[:, :, HALVES[u]],
-                    diff[u][:].rearrange("p (t j) -> p t j", t=2),
-                    ALU.mult,
-                )
-            else:
-                nc.vector.tensor_tensor(scaled[u][:, cols], share[u][:, cols], diff[u][:, cols], ALU.mult)
+        def scale(u, i):
+            t, h = units[u][i]
+            nc.vector.tensor_tensor(scaled[t][:, HALVES[h]], share[t, h][:], diff[u][:, HALVES[i]], ALU.mult)
 
         def finish(engine, b, u, i):
             t, h = units[u][i]
-            result = sbuf("result%d_%d" % (u, i), [P, S // 2], F32)
-            engine.tensor_tensor(result[:], scaled[u][:, HALVES[i]], b[:, HALVES[i]], ALU.subtract)
+            result = sbuf("result%d_%d" % (t, h), [P, S // 2], F32)
+            engine.tensor_tensor(result[:], scaled[t][:, HALVES[h]], b[:, HALVES[h]], ALU.subtract)
             nc.sync.dma_start(out=out_rows[:, t, HALVES[h]], in_=result[:])
 
-        scale(0, ALL)
-        second_alone(3, "A0")
-        finish(nc.gpsimd, b0_sb, 0, 0)
-        scale(1, ALL)
-        scale(2, HALVES[0])
-        finish(nc.vector, minus_b[1], 1, 0)
-        finish(nc.vector, minus_b[1], 1, 1)
-        finish(nc.gpsimd, b0_sb, 0, 1)
-        scale(2, HALVES[1])
-        scale(3, HALVES[0])
-        finish(nc.vector, minus_b[2], 2, 1)
-        finish(nc.gpsimd, b2_sb, 2, 0)
-        scale(3, HALVES[1])
-        for i in range(2):
-            finish(nc.vector, minus_b[3], 3, i)
+        on_gpsimd = {0: b1_sb, 1: b1_sb, 2: b2_sb}
+        for u in range(PACK):
+            for i in range(2):
+                scale(u, i)
+            if u < 2:
+                second_alone(2 + u, "A%d" % u)
+            if u == 0:
+                shares_on_scalar(3, 0)
+                nc.scalar.copy(b2_sb[:, HALVES[1]], minus_b[2][:, HALVES[1]])
+                shares_on_scalar(3, 1)
+            finish(nc.vector, minus_b[units[u][0][0]], u, 0)
+            if u in on_gpsimd:
+                finish(nc.gpsimd, on_gpsimd[u], u, 1)
+            else:
+                finish(nc.vector, minus_b[u], u, 1)

@@ -24,9 +24,6 @@ ALL = slice(0, S)
 ALL_QUADS = slice(0, P)
 PAIRS = (slice(0, 2), slice(2, PACK))
 HALVES = (slice(0, S // 2), slice(S // 2, S))
-W2_ON_VECTOR = 48
-W3_ON_SCALAR = 48
-W4_ON_SCALAR = 40
 
 
 def tile_picked_expertpair_silu_p_kernel(
@@ -51,13 +48,21 @@ def tile_picked_expertpair_silu_p_kernel(
         task_sb = sbuf("task_sb", [P, S // GROUP], U16)
         offs_sb = sbuf("offs_sb", [P, S // GROUP], U16)
         table_words = sbuf("table_words", [P, T], U32)
+        scale_rows = sbuf("scale_rows", [P, T], U8)
         table_scales = sbuf("table_scales", [P, T], U8)
         mix_rows = mix.rearrange("(p t) u -> p t u", t=PACK)
         out_rows = out.rearrange("(p t) j -> p t j", t=PACK)
         mix_at = [(PACK + 1) * RAW_BYTES + t * U * 4 for t in range(PACK)]
         mix_sb = [sbuf("mix%d" % t, [P, U], F32, mix_at[t]) for t in range(PACK)]
         w_raw = {name: sbuf(name + "_raw", [P, PACK, H], F32, raw_at[name]) for name in weights}
-        w_bf16 = {name: [sbuf("%s_bf16_%d" % (name, i), [P, 2 * PACK * P], BF16) for i in range(2)] for name in weights}
+        w3_pair0_at = (PACK + 2) * RAW_BYTES
+        w_bf16 = {
+            name: [
+                sbuf("%s_bf16_%d" % (name, i), [P, 2 * PACK * P], BF16, w3_pair0_at if (name, i) == ("w3", 0) else None)
+                for i in range(2)
+            ]
+            for name in weights
+        }
         codes_at = {name: PACK * RAW_BYTES + i * PACK * P * 4 for i, name in enumerate(weights)}
         w_codes = {
             name: [sbuf("%s_codes%d" % (name, i), [P, 2 * P], U32, codes_at[name] + i * 2 * P * 4) for i in range(2)]
@@ -74,9 +79,14 @@ def tile_picked_expertpair_silu_p_kernel(
         def load_scale_rows():
             for r in range(PACK):
                 nc.sync.dma_start(
-                    out=table_scales[r:P:QUADRANT, :].bitcast(I32),
+                    out=scale_rows[r:P:QUADRANT, :].bitcast(I32),
                     in_=x_scales[0, r : PACK * PACK : PACK, :].bitcast(I32),
                 )
+
+        def move_scale_rows():
+            for q in range(PACK):
+                rows = slice(q * QUADRANT, q * QUADRANT + PACK)
+                nc.vector.tensor_copy(table_scales[rows, :].bitcast(I32), scale_rows[rows, :].bitcast(I32))
 
         def load_words():
             nc.sync.dma_start(
@@ -91,13 +101,6 @@ def tile_picked_expertpair_silu_p_kernel(
         def round_on_vector(name, i, quads):
             dst, src = rounding_views(name, i, quads)
             nc.vector.tensor_scalar(dst, src, -1.0 if name == "w4" else 1.0, None, ALU.mult)
-
-        def round_on_scalar(name, i, quads):
-            dst, src = rounding_views(name, i, quads)
-            if name == "w4":
-                nc.scalar.mul(dst, src, -1.0)
-            else:
-                nc.scalar.copy(dst, src)
 
         def quantize(codes, scales, values):
             nc.vector.quantize_mx(out=codes.bitcast(FP8X4), scales=scales, in_=values)
@@ -149,66 +152,54 @@ def tile_picked_expertpair_silu_p_kernel(
                 part.rearrange("p (n t) -> p n t", t=PACK), acc[:].rearrange("p (t n) -> p n t", t=PACK), ACT.Silu
             )
 
-        nc.vector.memset(table_scales[:, : T // 2].bitcast(I32), 0)
-        nc.gpsimd.memset(table_scales[:, T // 2 :].bitcast(I32), 0)
-        nc.sync.dma_start(out=mix_sb[0][0:P:2, :], in_=mix_rows[0:P:2, 0, :])
-        nc.sync.dma_start(task_sb[:], task)
-        nc.sync.dma_start(out=mix_sb[0][1:P:2, :], in_=mix_rows[1:P:2, 0, :])
         nc.sync.dma_start(offs_sb[:], offs)
-        load_weight("w2")
         load_scale_rows()
+        load_weight("w2")
         load_words()
-        load_mix(1)
-        load_weight("w1")
-        for name in ("w4", "w3"):
+        nc.sync.dma_start(task_sb[:], task)
+        load_mix(0)
+        for name in ("w1", "w4", "w3"):
             load_weight(name)
-        load_mix(2)
-        load_mix(3)
+        for t in range(1, PACK):
+            load_mix(t)
+
+        def round_and_quantize(name):
+            for i in range(2):
+                round_on_vector(name, i, ALL_QUADS)
+            for i in range(2):
+                quantize_weight(name, i)
 
         share = {}
-        for h in range(2):
-            shares_on_vector(0, h)
-        round_on_vector("w2", 0, slice(0, W2_ON_VECTOR))
-        round_on_scalar("w2", 1, ALL_QUADS)
-        round_on_scalar("w2", 0, slice(W2_ON_VECTOR, P))
+        nc.vector.memset(table_scales[:].bitcast(I32), 0)
+        move_scale_rows()
         gather_bytes()
-        for i in (1, 0):
-            quantize_weight("w2", i)
+        round_and_quantize("w2")
         for c in range(PACK):
             gather_words(c)
         for h in range(2):
-            shares_on_vector(1, h)
+            shares_on_vector(0, h)
 
         z2_bf16 = sbuf("z2_bf16", [P, PACK * S], BF16)
         for c in range(PACK):
             hidden("w2", c, "A%d" % (c % 2), z2_bf16[:, c // 2 * 2 * S : (c // 2 + 1) * 2 * S])
-        for i in range(2):
-            round_on_vector("w1", i, ALL_QUADS)
-        for i in range(2):
-            quantize_weight("w1", i)
+        round_and_quantize("w1")
         z2_codes = sbuf("z2_codes", [P, S], U32, raw_at["w1"])
         z2_scales = sbuf("z2_scales", [P, S], U8)
         quantize(z2_codes[:], z2_scales[:], z2_bf16[:])
-        round_on_scalar("w4", 1, slice(0, W4_ON_SCALAR))
         z_bf16 = [sbuf("z_bf16_%d" % h, [P, PACK * S // 2], BF16) for h in range(2)]
         for c in range(PACK):
             hidden("w1", c, "B%d" % c, z_bf16[c // 2])
-        w4_cut = (W4_ON_SCALAR + P) // 2
-        round_on_vector("w4", 0, ALL_QUADS)
-        round_on_vector("w4", 1, slice(W4_ON_SCALAR, w4_cut))
-        quantize_weight("w4", 0)
-        round_on_vector("w4", 1, slice(w4_cut, P))
+        round_and_quantize("w4")
         z_codes = [sbuf("z_codes0", [P, S // 2], U32)]
         z_scales = [sbuf("z_scales%d" % h, [P, S // 2], U8) for h in range(2)]
         quantize(z_codes[0][:], z_scales[0][:], z_bf16[0][:])
-        quantize_weight("w4", 1)
         round_on_vector("w3", 0, ALL_QUADS)
-        round_on_scalar("w3", 1, slice(0, W3_ON_SCALAR))
-        round_on_vector("w3", 1, slice(W3_ON_SCALAR, P))
-        for i in range(2):
-            quantize_weight("w3", i)
-        z_codes.append(sbuf("z_codes1", [P, S // 2], U32, raw_at["w3"] + 8 * S))
+        round_on_vector("w3", 1, slice(0, P // 2))
+        quantize_weight("w3", 0)
+        round_on_vector("w3", 1, slice(P // 2, P))
+        z_codes.append(sbuf("z_codes1", [P, S // 2], U32, w3_pair0_at))
         quantize(z_codes[1][:], z_scales[1][:], z_bf16[1][:])
+        quantize_weight("w3", 1)
 
         units = [[(0, 0), (1, 0)], [(0, 1), (1, 1)], [(2, 0), (2, 1)], [(3, 0), (3, 1)]]
         diff = [bank("diff%d" % u, tag) for u, tag in enumerate(("A0", "A1", "B0", "B1"))]
@@ -236,14 +227,25 @@ def tile_picked_expertpair_silu_p_kernel(
         second_alone(0, "A3")
         for u in range(2, PACK):
             second_net(u)
+        for t in range(2, PACK):
+            second_alone(t, "B%d" % t)
         for u in range(PACK):
             first_net(u)
 
-        b1_sb = sbuf("b1_sb", [P, S], F32, raw_at["w3"])
-        b2_sb = sbuf("b2_sb", [P, S], F32, raw_at["w3"] + 4 * S)
-        nc.scalar.copy(b1_sb[:], minus_b[1][:])
+        on_gpsimd = [(1, 0), (1, 1), (2, 1)]
+        b_sb = {}
+
+        def copy_b(t, h):
+            b_sb[t, h] = sbuf("b%d_%d" % (t, h), [P, S // 2], F32)
+            nc.scalar.copy(b_sb[t, h][:], minus_b[t][:, HALVES[h]])
+
         for h in range(2):
-            shares_on_scalar(2, h)
+            copy_b(1, h)
+            shares_on_scalar(1, h)
+        copy_b(2, 1)
+        for t in range(2, PACK):
+            for h in range(2):
+                shares_on_scalar(t, h)
 
         scaled = [sbuf("scaled%d" % t, [P, S], F32) for t in range(PACK)]
 
@@ -251,24 +253,16 @@ def tile_picked_expertpair_silu_p_kernel(
             t, h = units[u][i]
             nc.vector.tensor_tensor(scaled[t][:, HALVES[h]], share[t, h][:], diff[u][:, HALVES[i]], ALU.mult)
 
-        def finish(engine, b, u, i):
-            t, h = units[u][i]
+        def finish(t, h):
             result = sbuf("result%d_%d" % (t, h), [P, S // 2], F32)
-            engine.tensor_tensor(result[:], scaled[t][:, HALVES[h]], b[:, HALVES[h]], ALU.subtract)
+            if (t, h) in on_gpsimd:
+                nc.gpsimd.tensor_tensor(result[:], scaled[t][:, HALVES[h]], b_sb[t, h][:], ALU.subtract)
+            else:
+                nc.vector.tensor_tensor(result[:], scaled[t][:, HALVES[h]], minus_b[t][:, HALVES[h]], ALU.subtract)
             nc.sync.dma_start(out=out_rows[:, t, HALVES[h]], in_=result[:])
 
-        on_gpsimd = {0: b1_sb, 1: b1_sb, 2: b2_sb}
         for u in range(PACK):
             for i in range(2):
                 scale(u, i)
-            if u < 2:
-                second_alone(2 + u, "A%d" % u)
-            if u == 0:
-                shares_on_scalar(3, 0)
-                nc.scalar.copy(b2_sb[:, HALVES[1]], minus_b[2][:, HALVES[1]])
-                shares_on_scalar(3, 1)
-            finish(nc.vector, minus_b[units[u][0][0]], u, 0)
-            if u in on_gpsimd:
-                finish(nc.gpsimd, on_gpsimd[u], u, 1)
-            else:
-                finish(nc.vector, minus_b[u], u, 1)
+            for t, h in units[u]:
+                finish(t, h)

@@ -24,6 +24,7 @@ ALL = slice(0, S)
 ALL_QUADS = slice(0, P)
 PAIRS = (slice(0, 2), slice(2, PACK))
 HALVES = (slice(0, S // 2), slice(S // 2, S))
+W3_ON_SCALAR = 40
 
 
 def tile_picked_expertpair_silu_p_kernel(
@@ -63,7 +64,8 @@ def tile_picked_expertpair_silu_p_kernel(
             ]
             for name in weights
         }
-        codes_at = {name: PACK * RAW_BYTES + i * PACK * P * 4 for i, name in enumerate(weights)}
+        codes_at = {name: PACK * RAW_BYTES + i * PACK * P * 4 for i, name in enumerate(("w1", "w3", "w4"))}
+        codes_at["w2"] = (PACK + 3) * RAW_BYTES
         w_codes = {
             name: [sbuf("%s_codes%d" % (name, i), [P, 2 * P], U32, codes_at[name] + i * 2 * P * 4) for i in range(2)]
             for name in weights
@@ -102,6 +104,10 @@ def tile_picked_expertpair_silu_p_kernel(
             dst, src = rounding_views(name, i, quads)
             nc.vector.tensor_scalar(dst, src, -1.0 if name == "w4" else 1.0, None, ALU.mult)
 
+        def round_on_scalar(name, i, quads):
+            dst, src = rounding_views(name, i, quads)
+            nc.scalar.copy(dst, src)
+
         def quantize(codes, scales, values):
             nc.vector.quantize_mx(out=codes.bitcast(FP8X4), scales=scales, in_=values)
 
@@ -120,13 +126,13 @@ def tile_picked_expertpair_silu_p_kernel(
                 stop=stop,
             )
 
-        def shares_on_vector(t, h, at=None):
-            share[t, h] = sbuf("share%d_%d" % (t, h), [P, S // 2], F32, at)
-            nc.vector.tensor_copy(share[t, h][:], mix_sb[t][:].indirect(entries(task_sb, HALVES[h])))
+        def shares_on_vector(t, cols):
+            dst = share[t, cols.start * 2 // S][:, cols.start % (S // 2) : (cols.stop - 1) % (S // 2) + 1]
+            nc.vector.tensor_copy(dst, mix_sb[t][:].indirect(entries(task_sb, cols)))
 
-        def shares_on_scalar(t, h, at=None):
-            share[t, h] = sbuf("share%d_%d" % (t, h), [P, S // 2], F32, at)
-            nc.scalar.activation(share[t, h][:], mix_sb[t][:].indirect(entries(task_sb, HALVES[h])), ACT.Copy)
+        def shares_on_scalar(t, cols):
+            dst = share[t, cols.start * 2 // S][:, cols.start % (S // 2) : (cols.stop - 1) % (S // 2) + 1]
+            nc.scalar.activation(dst, mix_sb[t][:].indirect(entries(task_sb, cols)), ACT.Copy)
 
         x_bytes = sbuf("x_bytes", [P, S], U8)
         x_codes = {}
@@ -152,13 +158,14 @@ def tile_picked_expertpair_silu_p_kernel(
                 part.rearrange("p (n t) -> p n t", t=PACK), acc[:].rearrange("p (t n) -> p n t", t=PACK), ACT.Silu
             )
 
-        nc.sync.dma_start(offs_sb[:], offs)
         load_scale_rows()
+        nc.sync.dma_start(offs_sb[:], offs)
         load_weight("w2")
         load_words()
         nc.sync.dma_start(task_sb[:], task)
+        load_weight("w1")
         load_mix(0)
-        for name in ("w1", "w4", "w3"):
+        for name in ("w4", "w3"):
             load_weight(name)
         for t in range(1, PACK):
             load_mix(t)
@@ -169,41 +176,63 @@ def tile_picked_expertpair_silu_p_kernel(
             for i in range(2):
                 quantize_weight(name, i)
 
-        share = {}
+        share = {
+            (t, h): sbuf(
+                "share%d_%d" % (t, h), [P, S // 2], F32, codes_at["w2"] + (2 * h + 1) * P * 4 if t == 0 else None
+            )
+            for t in range(PACK)
+            for h in range(2)
+        }
         nc.vector.memset(table_scales[:].bitcast(I32), 0)
         move_scale_rows()
         gather_bytes()
         round_and_quantize("w2")
         for c in range(PACK):
             gather_words(c)
-        for h in range(2):
-            shares_on_vector(0, h)
 
         z2_bf16 = sbuf("z2_bf16", [P, PACK * S], BF16)
         for c in range(PACK):
             hidden("w2", c, "A%d" % (c % 2), z2_bf16[:, c // 2 * 2 * S : (c // 2 + 1) * 2 * S])
         round_and_quantize("w1")
+        shares_on_vector(0, slice(0, P))
         z2_codes = sbuf("z2_codes", [P, S], U32, raw_at["w1"])
         z2_scales = sbuf("z2_scales", [P, S], U8)
         quantize(z2_codes[:], z2_scales[:], z2_bf16[:])
+        shares_on_scalar(0, slice(P, 2 * P))
+        shares_on_scalar(0, HALVES[1])
         z_bf16 = [sbuf("z_bf16_%d" % h, [P, PACK * S // 2], BF16) for h in range(2)]
         for c in range(PACK):
-            hidden("w1", c, "B%d" % c, z_bf16[c // 2])
-        round_and_quantize("w4")
+            hidden("w1", c, "B%d" % (c % 3), z_bf16[c // 2])
+        round_on_vector("w4", 0, ALL_QUADS)
+        round_on_vector("w4", 1, slice(0, P // 2))
+        quantize_weight("w4", 0)
+        round_on_vector("w4", 1, slice(P // 2, P))
         z_codes = [sbuf("z_codes0", [P, S // 2], U32)]
         z_scales = [sbuf("z_scales%d" % h, [P, S // 2], U8) for h in range(2)]
         quantize(z_codes[0][:], z_scales[0][:], z_bf16[0][:])
+        quantize_weight("w4", 1)
+
+        minus_b = {}
+
+        def second_alone(t, tag):
+            minus_b[t] = bank("minus_b%d" % t, tag)
+            product(minus_b[t][:], "w4", t, z2_codes[:], z2_scales[:], True, True)
+
+        second_alone(1, "A2")
+        b1_sb = sbuf("b1_sb", [P, S], F32)
+        nc.scalar.copy(b1_sb[:], minus_b[1][:])
+        w3_cut = (W3_ON_SCALAR + P) // 2
+        round_on_scalar("w3", 1, slice(0, W3_ON_SCALAR))
         round_on_vector("w3", 0, ALL_QUADS)
-        round_on_vector("w3", 1, slice(0, P // 2))
+        round_on_vector("w3", 1, slice(W3_ON_SCALAR, w3_cut))
         quantize_weight("w3", 0)
-        round_on_vector("w3", 1, slice(P // 2, P))
+        round_on_vector("w3", 1, slice(w3_cut, P))
         z_codes.append(sbuf("z_codes1", [P, S // 2], U32, w3_pair0_at))
         quantize(z_codes[1][:], z_scales[1][:], z_bf16[1][:])
         quantize_weight("w3", 1)
 
         units = [[(0, 0), (1, 0)], [(0, 1), (1, 1)], [(2, 0), (2, 1)], [(3, 0), (3, 1)]]
-        diff = [bank("diff%d" % u, tag) for u, tag in enumerate(("A0", "A1", "B0", "B1"))]
-        minus_b = {}
+        diff = [bank("diff%d" % u, tag) for u, tag in enumerate(("A0", "A1", "B1", "B2"))]
 
         def second_net(u):
             if u < 2:
@@ -213,39 +242,27 @@ def tile_picked_expertpair_silu_p_kernel(
             else:
                 product(diff[u][:], "w4", u, z2_codes[:], z2_scales[:], True, False)
 
-        def second_alone(t, tag):
-            minus_b[t] = bank("minus_b%d" % t, tag)
-            product(minus_b[t][:], "w4", t, z2_codes[:], z2_scales[:], True, True)
-
         def first_net(u):
             for i, (t, h) in enumerate(units[u]):
                 product(diff[u][:, HALVES[i]], "w3", t, z_codes[h][:], z_scales[h][:], False, i == 1)
 
         for u in range(2):
             second_net(u)
-        second_alone(1, "A2")
         second_alone(0, "A3")
+        second_alone(2, "B3")
         for u in range(2, PACK):
             second_net(u)
-        for t in range(2, PACK):
-            second_alone(t, "B%d" % t)
         for u in range(PACK):
             first_net(u)
 
-        on_gpsimd = [(1, 0), (1, 1), (2, 1)]
-        b_sb = {}
-
-        def copy_b(t, h):
-            b_sb[t, h] = sbuf("b%d_%d" % (t, h), [P, S // 2], F32)
-            nc.scalar.copy(b_sb[t, h][:], minus_b[t][:, HALVES[h]])
-
+        b2_sb = sbuf("b2_sb", [P, S // 2], F32)
+        on_gpsimd = {(1, 0): b1_sb[:, HALVES[0]], (1, 1): b1_sb[:, HALVES[1]], (2, 1): b2_sb[:]}
         for h in range(2):
-            copy_b(1, h)
-            shares_on_scalar(1, h)
-        copy_b(2, 1)
+            shares_on_scalar(1, HALVES[h])
+        nc.scalar.copy(b2_sb[:], minus_b[2][:, HALVES[1]])
         for t in range(2, PACK):
             for h in range(2):
-                shares_on_scalar(t, h)
+                shares_on_scalar(t, HALVES[h])
 
         scaled = [sbuf("scaled%d" % t, [P, S], F32) for t in range(PACK)]
 
@@ -256,7 +273,7 @@ def tile_picked_expertpair_silu_p_kernel(
         def finish(t, h):
             result = sbuf("result%d_%d" % (t, h), [P, S // 2], F32)
             if (t, h) in on_gpsimd:
-                nc.gpsimd.tensor_tensor(result[:], scaled[t][:, HALVES[h]], b_sb[t, h][:], ALU.subtract)
+                nc.gpsimd.tensor_tensor(result[:], scaled[t][:, HALVES[h]], on_gpsimd[t, h], ALU.subtract)
             else:
                 nc.vector.tensor_tensor(result[:], scaled[t][:, HALVES[h]], minus_b[t][:, HALVES[h]], ALU.subtract)
             nc.sync.dma_start(out=out_rows[:, t, HALVES[h]], in_=result[:])
@@ -264,5 +281,7 @@ def tile_picked_expertpair_silu_p_kernel(
         for u in range(PACK):
             for i in range(2):
                 scale(u, i)
+            if u == 0:
+                second_alone(3, "A0")
             for t, h in units[u]:
                 finish(t, h)

@@ -24,7 +24,6 @@ ALL = slice(0, S)
 ALL_QUADS = slice(0, P)
 PAIRS = (slice(0, 2), slice(2, PACK))
 HALVES = (slice(0, S // 2), slice(S // 2, S))
-W3_ON_SCALAR = 40
 
 
 def tile_picked_expertpair_silu_p_kernel(
@@ -45,15 +44,16 @@ def tile_picked_expertpair_silu_p_kernel(
             return list_tile[:, cols.start // GROUP : cols.stop // GROUP]
 
         weights = {"w1": w1, "w2": w2, "w3": w3, "w4": w4}
-        raw_at = {name: i * RAW_BYTES for i, name in enumerate(weights)}
+        raw_at = {"w2": RAW_BYTES, "w4": 64, "w3": 2 * RAW_BYTES - 64, "w1": (PACK + 5) * RAW_BYTES + 64}
         task_sb = sbuf("task_sb", [P, S // GROUP], U16)
         offs_sb = sbuf("offs_sb", [P, S // GROUP], U16)
         table_words = sbuf("table_words", [P, T], U32)
+        table_at = (PACK + 4) * RAW_BYTES + 2 * RAW_BYTES
         scale_rows = sbuf("scale_rows", [P, T], U8)
-        table_scales = sbuf("table_scales", [P, T], U8)
+        table_scales = sbuf("table_scales", [P, T], U8, table_at)
         mix_rows = mix.rearrange("(p t) u -> p t u", t=PACK)
         out_rows = out.rearrange("(p t) j -> p t j", t=PACK)
-        mix_at = [(PACK + 1) * RAW_BYTES + t * U * 4 for t in range(PACK)]
+        mix_at = [table_at + T - 64] + [RAW_BYTES + 64 + t * U * 4 for t in range(PACK - 1)]
         mix_sb = [sbuf("mix%d" % t, [P, U], F32, mix_at[t]) for t in range(PACK)]
         w_raw = {name: sbuf(name + "_raw", [P, PACK, H], F32, raw_at[name]) for name in weights}
         w3_pair0_at = (PACK + 2) * RAW_BYTES
@@ -79,16 +79,10 @@ def tile_picked_expertpair_silu_p_kernel(
             nc.sync.dma_start(out=w_raw[name][:], in_=weights[name].rearrange("(p j) c -> p j c", j=PACK))
 
         def load_scale_rows():
-            for r in range(PACK):
-                nc.sync.dma_start(
-                    out=scale_rows[r:P:QUADRANT, :].bitcast(I32),
-                    in_=x_scales[0, r : PACK * PACK : PACK, :].bitcast(I32),
-                )
+            nc.sync.dma_start(out=scale_rows[:GROUP, :].bitcast(I32), in_=x_scales[0].bitcast(I32))
 
         def move_scale_rows():
-            for q in range(PACK):
-                rows = slice(q * QUADRANT, q * QUADRANT + PACK)
-                nc.vector.tensor_copy(table_scales[rows, :].bitcast(I32), scale_rows[rows, :].bitcast(I32))
+            nc.vector.tensor_copy(table_scales[:GROUP, :].bitcast(I32), scale_rows[:GROUP, :].bitcast(I32))
 
         def load_words():
             nc.sync.dma_start(
@@ -103,10 +97,6 @@ def tile_picked_expertpair_silu_p_kernel(
         def round_on_vector(name, i, quads):
             dst, src = rounding_views(name, i, quads)
             nc.vector.tensor_scalar(dst, src, -1.0 if name == "w4" else 1.0, None, ALU.mult)
-
-        def round_on_scalar(name, i, quads):
-            dst, src = rounding_views(name, i, quads)
-            nc.scalar.copy(dst, src)
 
         def quantize(codes, scales, values):
             nc.vector.quantize_mx(out=codes.bitcast(FP8X4), scales=scales, in_=values)
@@ -138,7 +128,14 @@ def tile_picked_expertpair_silu_p_kernel(
         x_codes = {}
 
         def gather_bytes():
-            nc.vector.tensor_copy(x_bytes[:], table_scales[:].indirect(offs_sb[:]))
+            picked = sbuf("picked_bytes", [P, S], U8)
+            nc.vector.tensor_copy(picked[:], table_scales[:].indirect(offs_sb[:]))
+            nc.vector.tensor_copy(x_bytes[:PACK, :].bitcast(I32), picked[:PACK, :].bitcast(I32))
+            for q in range(1, PACK):
+                nc.sync.dma_start(
+                    out=x_bytes[q * QUADRANT : q * QUADRANT + PACK, :].bitcast(I32),
+                    in_=picked[q * PACK : (q + 1) * PACK, :].bitcast(I32),
+                )
 
         def gather_words(c, at=None):
             x_codes[c] = sbuf("x_codes%d" % c, [P, P], U32, at)
@@ -158,23 +155,28 @@ def tile_picked_expertpair_silu_p_kernel(
                 part.rearrange("p (n t) -> p n t", t=PACK), acc[:].rearrange("p (t n) -> p n t", t=PACK), ACT.Silu
             )
 
+        def round_and_quantize(name):
+            for i in range(2):
+                round_on_vector(name, i, ALL_QUADS)
+            for i in range(2):
+                quantize_weight(name, i)
+
         load_scale_rows()
         nc.sync.dma_start(offs_sb[:], offs)
+        nc.sync.dma_start(task_sb[:], task)
         load_weight("w2")
         load_words()
-        nc.sync.dma_start(task_sb[:], task)
+        nc.vector.memset(table_scales[:].bitcast(I32), 0)
+        nc.vector.memset(x_bytes[:].bitcast(I32), 0)
+        move_scale_rows()
+        gather_bytes()
+        round_and_quantize("w2")
         load_weight("w1")
         load_mix(0)
         for name in ("w4", "w3"):
             load_weight(name)
         for t in range(1, PACK):
             load_mix(t)
-
-        def round_and_quantize(name):
-            for i in range(2):
-                round_on_vector(name, i, ALL_QUADS)
-            for i in range(2):
-                quantize_weight(name, i)
 
         share = {
             (t, h): sbuf(
@@ -183,16 +185,12 @@ def tile_picked_expertpair_silu_p_kernel(
             for t in range(PACK)
             for h in range(2)
         }
-        nc.vector.memset(table_scales[:].bitcast(I32), 0)
-        move_scale_rows()
-        gather_bytes()
-        round_and_quantize("w2")
         for c in range(PACK):
             gather_words(c)
 
         z2_bf16 = sbuf("z2_bf16", [P, PACK * S], BF16)
         for c in range(PACK):
-            hidden("w2", c, "A%d" % (c % 2), z2_bf16[:, c // 2 * 2 * S : (c // 2 + 1) * 2 * S])
+            hidden("w2", c, "A%d" % (c % 3), z2_bf16[:, c // 2 * 2 * S : (c // 2 + 1) * 2 * S])
         round_and_quantize("w1")
         shares_on_vector(0, slice(0, P))
         z2_codes = sbuf("z2_codes", [P, S], U32, raw_at["w1"])
@@ -221,12 +219,10 @@ def tile_picked_expertpair_silu_p_kernel(
         second_alone(1, "A2")
         b1_sb = sbuf("b1_sb", [P, S], F32)
         nc.scalar.copy(b1_sb[:], minus_b[1][:])
-        w3_cut = (W3_ON_SCALAR + P) // 2
-        round_on_scalar("w3", 1, slice(0, W3_ON_SCALAR))
         round_on_vector("w3", 0, ALL_QUADS)
-        round_on_vector("w3", 1, slice(W3_ON_SCALAR, w3_cut))
+        round_on_vector("w3", 1, slice(0, P // 2))
         quantize_weight("w3", 0)
-        round_on_vector("w3", 1, slice(w3_cut, P))
+        round_on_vector("w3", 1, slice(P // 2, P))
         z_codes.append(sbuf("z_codes1", [P, S // 2], U32, w3_pair0_at))
         quantize(z_codes[1][:], z_scales[1][:], z_bf16[1][:])
         quantize_weight("w3", 1)
@@ -257,10 +253,8 @@ def tile_picked_expertpair_silu_p_kernel(
 
         b2_sb = sbuf("b2_sb", [P, S // 2], F32)
         on_gpsimd = {(1, 0): b1_sb[:, HALVES[0]], (1, 1): b1_sb[:, HALVES[1]], (2, 1): b2_sb[:]}
-        for h in range(2):
-            shares_on_scalar(1, HALVES[h])
         nc.scalar.copy(b2_sb[:], minus_b[2][:, HALVES[1]])
-        for t in range(2, PACK):
+        for t in range(1, PACK):
             for h in range(2):
                 shares_on_scalar(t, HALVES[h])
 

@@ -56,10 +56,10 @@ def tile_picked_expertpair_silu_p_kernel(
         mix_at = [table_at + T - 64] + [RAW_BYTES + 64 + t * U * 4 for t in range(PACK - 1)]
         mix_sb = [sbuf("mix%d" % t, [P, U], F32, mix_at[t]) for t in range(PACK)]
         w_raw = {name: sbuf(name + "_raw", [P, PACK, H], F32, raw_at[name]) for name in weights}
-        w3_pair0_at = (PACK + 2) * RAW_BYTES
+        w3_bf16_at = [(PACK + 2) * RAW_BYTES + i * 4 * PACK * P for i in range(2)]
         w_bf16 = {
             name: [
-                sbuf("%s_bf16_%d" % (name, i), [P, 2 * PACK * P], BF16, w3_pair0_at if (name, i) == ("w3", 0) else None)
+                sbuf("%s_bf16_%d" % (name, i), [P, 2 * PACK * P], BF16, w3_bf16_at[i] if name == "w3" else None)
                 for i in range(2)
             ]
             for name in weights
@@ -150,9 +150,8 @@ def tile_picked_expertpair_silu_p_kernel(
             acc = bank("hidden_%s_%d" % (name, c), tag)
             for t in range(PACK):
                 product(acc[:, t * P : (t + 1) * P], name, t, x_codes[c][:], x_bytes[:, cols], True, True)
-            part = dst[:, c % 2 * PACK * P : (c % 2 + 1) * PACK * P]
             nc.scalar.activation(
-                part.rearrange("p (n t) -> p n t", t=PACK), acc[:].rearrange("p (t n) -> p n t", t=PACK), ACT.Silu
+                dst.rearrange("p (n t) -> p n t", t=PACK), acc[:].rearrange("p (t n) -> p n t", t=PACK), ACT.Silu
             )
 
         def round_and_quantize(name):
@@ -190,7 +189,7 @@ def tile_picked_expertpair_silu_p_kernel(
 
         z2_bf16 = sbuf("z2_bf16", [P, PACK * S], BF16)
         for c in range(PACK):
-            hidden("w2", c, "A%d" % (c % 3), z2_bf16[:, c // 2 * 2 * S : (c // 2 + 1) * 2 * S])
+            hidden("w2", c, "A%d" % (c % 3), z2_bf16[:, c * PACK * P : (c + 1) * PACK * P])
         round_and_quantize("w1")
         shares_on_vector(0, slice(0, P))
         z2_codes = sbuf("z2_codes", [P, S], U32, raw_at["w1"])
@@ -198,17 +197,25 @@ def tile_picked_expertpair_silu_p_kernel(
         quantize(z2_codes[:], z2_scales[:], z2_bf16[:])
         shares_on_scalar(0, slice(P, 2 * P))
         shares_on_scalar(0, HALVES[1])
-        z_bf16 = [sbuf("z_bf16_%d" % h, [P, PACK * S // 2], BF16) for h in range(2)]
+        z_bf16 = sbuf("z_bf16", [P, PACK * S], BF16)
         for c in range(PACK):
-            hidden("w1", c, "B%d" % (c % 3), z_bf16[c // 2])
+            hidden("w1", c, "B%d" % (c % 3), z_bf16[:, c * PACK * P : (c + 1) * PACK * P])
+        z_parts = {}
+
+        def quantize_z(cols, at=None):
+            width = cols.stop - cols.start
+            codes = sbuf("z_codes%d" % cols.start, [P, width], U32, at)
+            scales = sbuf("z_scales%d" % cols.start, [P, width], U8)
+            quantize(codes[:], scales[:], z_bf16[:, PACK * cols.start : PACK * cols.stop])
+            z_parts[cols.start, cols.stop] = codes, scales
+
         round_on_vector("w4", 0, ALL_QUADS)
         round_on_vector("w4", 1, slice(0, P // 2))
         quantize_weight("w4", 0)
         round_on_vector("w4", 1, slice(P // 2, P))
-        z_codes = [sbuf("z_codes0", [P, S // 2], U32)]
-        z_scales = [sbuf("z_scales%d" % h, [P, S // 2], U8) for h in range(2)]
-        quantize(z_codes[0][:], z_scales[0][:], z_bf16[0][:])
+        quantize_z(HALVES[0])
         quantize_weight("w4", 1)
+        quantize_z(slice(2 * P, 3 * P))
 
         minus_b = {}
 
@@ -221,48 +228,53 @@ def tile_picked_expertpair_silu_p_kernel(
         nc.scalar.copy(b1_sb[:], minus_b[1][:])
         round_on_vector("w3", 0, ALL_QUADS)
         round_on_vector("w3", 1, slice(0, P // 2))
-        quantize_weight("w3", 0)
+        for t in range(2):
+            quantize(
+                w_codes["w3"][0][:, t * P : (t + 1) * P],
+                w_scales["w3"][0][:, t * P : (t + 1) * P],
+                w_bf16["w3"][0][:, t * PACK * P : (t + 1) * PACK * P],
+            )
         round_on_vector("w3", 1, slice(P // 2, P))
-        z_codes.append(sbuf("z_codes1", [P, S // 2], U32, w3_pair0_at))
-        quantize(z_codes[1][:], z_scales[1][:], z_bf16[1][:])
+        quantize_z(slice(3 * P, S), w3_bf16_at[0])
         quantize_weight("w3", 1)
 
-        units = [[(0, 0), (1, 0)], [(0, 1), (1, 1)], [(2, 0), (2, 1)], [(3, 0), (3, 1)]]
-        diff = [bank("diff%d" % u, tag) for u, tag in enumerate(("A0", "A1", "B1", "B2"))]
+        groups = [[(0, 0)], [(1, 0)], [(0, 1), (1, 1)], [(2, 0), (2, 1)], [(3, 0), (3, 1)]]
+        diff = {}
+        for group, tag in zip(groups, ("A0", "B0", "A1", "B1", "B2")):
+            acc = bank("diff_" + tag, tag)
+            for i, piece in enumerate(group):
+                diff[piece] = acc[:, HALVES[i]]
 
-        def second_net(u):
-            if u < 2:
-                for t in range(2):
-                    product(diff[u][:, HALVES[t]], "w4", t, z2_codes[:, HALVES[u]], z2_scales[:, HALVES[u]],
-                            t == 0, False)
-            else:
-                product(diff[u][:], "w4", u, z2_codes[:], z2_scales[:], True, False)
+        def second_net(group):
+            for i, (t, h) in enumerate(group):
+                product(diff[t, h], "w4", t, z2_codes[:, HALVES[h]], z2_scales[:, HALVES[h]], i == 0, False)
 
-        def first_net(u):
-            for i, (t, h) in enumerate(units[u]):
-                product(diff[u][:, HALVES[i]], "w3", t, z_codes[h][:], z_scales[h][:], False, i == 1)
+        def first_net(group):
+            for t, h in group:
+                for (lo, hi), (codes, scales) in z_parts.items():
+                    if lo * 2 // S == h:
+                        cols = slice(lo - HALVES[h].start, hi - HALVES[h].start)
+                        last = (t, h) == group[-1] and hi == HALVES[h].stop
+                        product(diff[t, h][:, cols], "w3", t, codes[:], scales[:], False, last)
 
-        for u in range(2):
-            second_net(u)
+        second_net(groups[0])
+        second_net(groups[2])
         second_alone(0, "A3")
         second_alone(2, "B3")
-        for u in range(2, PACK):
-            second_net(u)
-        for u in range(PACK):
-            first_net(u)
+        for g in (3, 4, 1):
+            second_net(groups[g])
+        for group in groups:
+            first_net(group)
 
-        b2_sb = sbuf("b2_sb", [P, S // 2], F32)
-        on_gpsimd = {(1, 0): b1_sb[:, HALVES[0]], (1, 1): b1_sb[:, HALVES[1]], (2, 1): b2_sb[:]}
-        nc.scalar.copy(b2_sb[:], minus_b[2][:, HALVES[1]])
+        on_gpsimd = {(1, 0): b1_sb[:, HALVES[0]], (1, 1): b1_sb[:, HALVES[1]]}
         for t in range(1, PACK):
             for h in range(2):
                 shares_on_scalar(t, HALVES[h])
 
-        scaled = [sbuf("scaled%d" % t, [P, S], F32) for t in range(PACK)]
+        scaled = [sbuf("scaled%d" % t, [P, S], F32, w3_bf16_at[1] if t == 1 else None) for t in range(PACK)]
 
-        def scale(u, i):
-            t, h = units[u][i]
-            nc.vector.tensor_tensor(scaled[t][:, HALVES[h]], share[t, h][:], diff[u][:, HALVES[i]], ALU.mult)
+        def scale(t, h):
+            nc.vector.tensor_tensor(scaled[t][:, HALVES[h]], share[t, h][:], diff[t, h], ALU.mult)
 
         def finish(t, h):
             result = sbuf("result%d_%d" % (t, h), [P, S // 2], F32)
@@ -272,10 +284,10 @@ def tile_picked_expertpair_silu_p_kernel(
                 nc.vector.tensor_tensor(result[:], scaled[t][:, HALVES[h]], minus_b[t][:, HALVES[h]], ALU.subtract)
             nc.sync.dma_start(out=out_rows[:, t, HALVES[h]], in_=result[:])
 
-        for u in range(PACK):
-            for i in range(2):
-                scale(u, i)
-            if u == 0:
+        for unit in [groups[0] + groups[1]] + groups[2:]:
+            for t, h in unit:
+                scale(t, h)
+            if unit[0] == (0, 0):
                 second_alone(3, "A0")
-            for t, h in units[u]:
+            for t, h in unit:
                 finish(t, h)

@@ -49,17 +49,16 @@ def tile_picked_expertpair_silu_p_kernel(
         offs_sb = sbuf("offs_sb", [P, S // GROUP], U16)
         table_words = sbuf("table_words", [P, T], U32)
         table_at = (PACK + 4) * RAW_BYTES + 2 * RAW_BYTES
-        scale_rows = sbuf("scale_rows", [P, T], U8)
         table_scales = sbuf("table_scales", [P, T], U8, table_at)
         mix_rows = mix.rearrange("(p t) u -> p t u", t=PACK)
         out_rows = out.rearrange("(p t) j -> p t j", t=PACK)
         mix_at = [table_at + T - 64] + [RAW_BYTES + 64 + t * U * 4 for t in range(PACK - 1)]
         mix_sb = [sbuf("mix%d" % t, [P, U], F32, mix_at[t]) for t in range(PACK)]
         w_raw = {name: sbuf(name + "_raw", [P, PACK, H], F32, raw_at[name]) for name in weights}
-        w3_bf16_at = [(PACK + 2) * RAW_BYTES + i * 4 * PACK * P for i in range(2)]
+        w3_pair0_at = (PACK + 2) * RAW_BYTES
         w_bf16 = {
             name: [
-                sbuf("%s_bf16_%d" % (name, i), [P, 2 * PACK * P], BF16, w3_bf16_at[i] if name == "w3" else None)
+                sbuf("%s_bf16_%d" % (name, i), [P, 2 * PACK * P], BF16, w3_pair0_at if (name, i) == ("w3", 0) else None)
                 for i in range(2)
             ]
             for name in weights
@@ -79,10 +78,7 @@ def tile_picked_expertpair_silu_p_kernel(
             nc.sync.dma_start(out=w_raw[name][:], in_=weights[name].rearrange("(p j) c -> p j c", j=PACK))
 
         def load_scale_rows():
-            nc.sync.dma_start(out=scale_rows[:GROUP, :].bitcast(I32), in_=x_scales[0].bitcast(I32))
-
-        def move_scale_rows():
-            nc.vector.tensor_copy(table_scales[:GROUP, :].bitcast(I32), scale_rows[:GROUP, :].bitcast(I32))
+            nc.sync.dma_start(out=table_scales[GROUP:QUADRANT, :].bitcast(I32), in_=x_scales[0].bitcast(I32))
 
         def load_words():
             nc.sync.dma_start(
@@ -130,11 +126,10 @@ def tile_picked_expertpair_silu_p_kernel(
         def gather_bytes():
             picked = sbuf("picked_bytes", [P, S], U8)
             nc.vector.tensor_copy(picked[:], table_scales[:].indirect(offs_sb[:]))
-            nc.vector.tensor_copy(x_bytes[:PACK, :].bitcast(I32), picked[:PACK, :].bitcast(I32))
-            for q in range(1, PACK):
+            for q in range(PACK):
                 nc.sync.dma_start(
                     out=x_bytes[q * QUADRANT : q * QUADRANT + PACK, :].bitcast(I32),
-                    in_=picked[q * PACK : (q + 1) * PACK, :].bitcast(I32),
+                    in_=picked[GROUP + q * PACK : GROUP + (q + 1) * PACK, :].bitcast(I32),
                 )
 
         def gather_words(c, at=None):
@@ -165,9 +160,9 @@ def tile_picked_expertpair_silu_p_kernel(
         nc.sync.dma_start(task_sb[:], task)
         load_weight("w2")
         load_words()
-        nc.vector.memset(table_scales[:].bitcast(I32), 0)
+        for rows in (slice(0, GROUP), slice(QUADRANT, 2 * QUADRANT), slice(2 * QUADRANT, P)):
+            nc.vector.memset(table_scales[rows, :].bitcast(I32), 0)
         nc.vector.memset(x_bytes[:].bitcast(I32), 0)
-        move_scale_rows()
         gather_bytes()
         round_and_quantize("w2")
         load_weight("w1")
@@ -235,18 +230,16 @@ def tile_picked_expertpair_silu_p_kernel(
                 w_bf16["w3"][0][:, t * PACK * P : (t + 1) * PACK * P],
             )
         round_on_vector("w3", 1, slice(P // 2, P))
-        quantize_z(slice(3 * P, S), w3_bf16_at[0])
+        quantize_z(slice(3 * P, S), w3_pair0_at)
         quantize_weight("w3", 1)
 
         groups = [[(0, 0)], [(1, 0)], [(0, 1), (1, 1)], [(2, 0), (2, 1)], [(3, 0), (3, 1)]]
         diff = {}
-        for group, tag in zip(groups, ("A0", "B0", "A1", "B1", "B2")):
-            acc = bank("diff_" + tag, tag)
-            for i, piece in enumerate(group):
-                diff[piece] = acc[:, HALVES[i]]
 
-        def second_net(group):
+        def second_net(group, tag):
+            acc = bank("diff%d_%d" % group[0], tag)
             for i, (t, h) in enumerate(group):
+                diff[t, h] = acc[:, HALVES[i]]
                 product(diff[t, h], "w4", t, z2_codes[:, HALVES[h]], z2_scales[:, HALVES[h]], i == 0, False)
 
         def first_net(group):
@@ -257,13 +250,12 @@ def tile_picked_expertpair_silu_p_kernel(
                         last = (t, h) == group[-1] and hi == HALVES[h].stop
                         product(diff[t, h][:, cols], "w3", t, codes[:], scales[:], False, last)
 
-        second_net(groups[0])
-        second_net(groups[2])
+        second_net(groups[0], "A0")
+        second_net(groups[2], "A1")
         second_alone(0, "A3")
-        second_alone(2, "B3")
-        for g in (3, 4, 1):
-            second_net(groups[g])
-        for group in groups:
+        second_net(groups[3], "B1")
+        second_net(groups[1], "B0")
+        for group in groups[:4]:
             first_net(group)
 
         on_gpsimd = {(1, 0): b1_sb[:, HALVES[0]], (1, 1): b1_sb[:, HALVES[1]]}
@@ -271,7 +263,7 @@ def tile_picked_expertpair_silu_p_kernel(
             for h in range(2):
                 shares_on_scalar(t, HALVES[h])
 
-        scaled = [sbuf("scaled%d" % t, [P, S], F32, w3_bf16_at[1] if t == 1 else None) for t in range(PACK)]
+        scaled = [sbuf("scaled%d" % t, [P, S], F32) for t in range(PACK)]
 
         def scale(t, h):
             nc.vector.tensor_tensor(scaled[t][:, HALVES[h]], share[t, h][:], diff[t, h], ALU.mult)
@@ -284,10 +276,14 @@ def tile_picked_expertpair_silu_p_kernel(
                 nc.vector.tensor_tensor(result[:], scaled[t][:, HALVES[h]], minus_b[t][:, HALVES[h]], ALU.subtract)
             nc.sync.dma_start(out=out_rows[:, t, HALVES[h]], in_=result[:])
 
-        for unit in [groups[0] + groups[1]] + groups[2:]:
+        for u, unit in enumerate([groups[0] + groups[1]] + groups[2:]):
             for t, h in unit:
                 scale(t, h)
-            if unit[0] == (0, 0):
-                second_alone(3, "A0")
+            if u == 0:
+                second_alone(2, "A0")
+                second_net(groups[4], "B0")
+                first_net(groups[4])
+            if u == 1:
+                second_alone(3, "A1")
             for t, h in unit:
                 finish(t, h)

from contextlib import ExitStack

import concourse.mybir as mybir

K, T, S, N, H, U = 512, 2048, 512, 512, 512, 512
FLOPS = 2 * (2 * K * H * S + 2 * H * N * S)

F32 = mybir.dt.float32
BF16 = mybir.dt.bfloat16
I32 = mybir.dt.int32
U32 = mybir.dt.uint32
U16 = mybir.dt.uint16
U8 = mybir.dt.uint8
FP8X4 = mybir.dt.float8_e4m3fn_x4
ACT = mybir.ActivationFunctionType
ALU = mybir.AluOpType

P = 128
PACK = 4
GROUP = 16
QUADRANT = 32
RAW_BYTES = PACK * H * 4
ALL = slice(0, S)
ALL_QUADS = slice(0, P)
PAIRS = (slice(0, 2), slice(2, PACK))
HALVES = (slice(0, S // 2), slice(S // 2, S))


def tile_picked_expertpair_silu_p_kernel(
    tc, x_words, x_scales, w1, w2, w3, w4, mix, offs, task, out
):
    nc = tc.nc
    with ExitStack() as ctx:
        keep = ctx.enter_context(tc.tile_pool(name="keep", bufs=1))
        shared = ctx.enter_context(tc.tile_pool(name="shared", bufs=1))
        psum = ctx.enter_context(tc.psum_pool(name="psum", bufs=1))

        def sbuf(name, shape, dtype, at=None):
            if at is None:
                return keep.tile(shape, dtype, name=name, tag=name, align_bytes=64)
            return shared.tile(shape, dtype, name=name, offset=at, align_bytes=64)

        def entries(list_tile, cols):
            return list_tile[:, cols.start // GROUP : cols.stop // GROUP]

        weights = {"w1": w1, "w2": w2, "w3": w3, "w4": w4}
        raw_at = {"w2": RAW_BYTES, "w4": 64, "w3": 2 * RAW_BYTES - 64, "w1": (PACK + 5) * RAW_BYTES + 64}
        task_sb = sbuf("task_sb", [P, S // GROUP], U16)
        offs_sb = sbuf("offs_sb", [P, S // GROUP], U16)
        table_words = sbuf("table_words", [P, T], U32)
        table_at = (PACK + 4) * RAW_BYTES + 2 * RAW_BYTES
        table_scales = sbuf("table_scales", [P, T], U8, table_at)
        mix_rows = mix.rearrange("(p t) u -> p t u", t=PACK)
        out_rows = out.rearrange("(p t) j -> p t j", t=PACK)
        mix_at = [table_at + T - 64] + [RAW_BYTES + 64 + t * U * 4 for t in range(PACK - 1)]
        mix_sb = [sbuf("mix%d" % t, [P, U], F32, mix_at[t]) for t in range(PACK)]
        w_raw = {name: sbuf(name + "_raw", [P, PACK, H], F32, raw_at[name]) for name in weights}
        w3_pair0_at = (PACK + 2) * RAW_BYTES
        w_bf16 = {
            name: [
                sbuf("%s_bf16_%d" % (name, i), [P, 2 * PACK * P], BF16, w3_pair0_at if (name, i) == ("w3", 0) else None)
                for i in range(2)
            ]
            for name in weights
        }
        codes_at = {name: PACK * RAW_BYTES + i * PACK * P * 4 for i, name in enumerate(("w1", "w3", "w4"))}
        codes_at["w2"] = (PACK + 3) * RAW_BYTES
        w_codes = {
            name: [sbuf("%s_codes%d" % (name, i), [P, 2 * P], U32, codes_at[name] + i * 2 * P * 4) for i in range(2)]
            for name in weights
        }
        w_scales = {name: [sbuf("%s_scales%d" % (name, i), [P, 2 * P], U8) for i in range(2)] for name in weights}

        def load_mix(t):
            nc.sync.dma_start(out=mix_sb[t][:], in_=mix_rows[:, t, :])

        def load_weight(name):
            nc.sync.dma_start(out=w_raw[name][:], in_=weights[name].rearrange("(p j) c -> p j c", j=PACK))

        def load_scale_rows():
            nc.sync.dma_start(out=table_scales[GROUP:QUADRANT, :].bitcast(I32), in_=x_scales[0].bitcast(I32))

        def load_words():
            nc.sync.dma_start(
                out=table_words[:].bitcast(I32), in_=x_words[0].rearrange("p n t -> p (n t)").bitcast(I32)
            )

        def rounding_views(name, i, quads):
            dst = w_bf16[name][i][:].rearrange("p (t m j) -> p m j t", t=2, j=PACK)[:, quads]
            src = w_raw[name][:].rearrange("p j (m t) -> p m j t", t=PACK)[:, quads, :, PAIRS[i]]
            return dst, src

        def round_on_vector(name, i, quads):
            dst, src = rounding_views(name, i, quads)
            nc.vector.tensor_scalar(dst, src, -1.0 if name == "w4" else 1.0, None, ALU.mult)

        def quantize(codes, scales, values):
            nc.vector.quantize_mx(out=codes.bitcast(FP8X4), scales=scales, in_=values)

        def quantize_weight(name, i):
            quantize(w_codes[name][i][:], w_scales[name][i][:], w_bf16[name][i][:])

        def product(dst, name, t, codes, scales, start, stop):
            cols = slice(t % 2 * P, (t % 2 + 1) * P)
            nc.tensor.matmul_mx(
                out=dst,
                lhsT=w_codes[name][t // 2][:, cols].bitcast(FP8X4),
                lhsT_scale=w_scales[name][t // 2][:, cols],
                rhs=codes.bitcast(FP8X4),
                rhs_scale=scales,
                start=start,
                stop=stop,
            )

        def shares_on_vector(t, cols):
            dst = share[t, cols.start * 2 // S][:, cols.start % (S // 2) : (cols.stop - 1) % (S // 2) + 1]
            nc.vector.tensor_copy(dst, mix_sb[t][:].indirect(entries(task_sb, cols)))

        def shares_on_scalar(t, cols):
            dst = share[t, cols.start * 2 // S][:, cols.start % (S // 2) : (cols.stop - 1) % (S // 2) + 1]
            nc.scalar.activation(dst, mix_sb[t][:].indirect(entries(task_sb, cols)), ACT.Copy)

        x_bytes = sbuf("x_bytes", [P, S], U8)
        x_codes = {}

        def gather_bytes():
            picked = sbuf("picked_bytes", [P, S], U8)
            nc.vector.tensor_copy(picked[:], table_scales[:].indirect(offs_sb[:]))
            for q in range(PACK):
                nc.sync.dma_start(
                    out=x_bytes[q * QUADRANT : q * QUADRANT + PACK, :].bitcast(I32),
                    in_=picked[GROUP + q * PACK : GROUP + (q + 1) * PACK, :].bitcast(I32),
                )

        def gather_words(c, at=None):
            x_codes[c] = sbuf("x_codes%d" % c, [P, P], U32, at)
            cols = slice(c * P, (c + 1) * P)
            nc.vector.tensor_copy(x_codes[c][:], table_words[:].indirect(entries(offs_sb, cols)))

        def bank(name, tag):
            return psum.tile([P, S], F32, name=name, tag=tag)

        def hidden(name, c, tag, dst):
            cols = slice(c * P, (c + 1) * P)
            acc = bank("hidden_%s_%d" % (name, c), tag)
            for t in range(PACK):
                product(acc[:, t * P : (t + 1) * P], name, t, x_codes[c][:], x_bytes[:, cols], True, True)
            nc.scalar.activation(
                dst.rearrange("p (n t) -> p n t", t=PACK), acc[:].rearrange("p (t n) -> p n t", t=PACK), ACT.Silu
            )

        def round_and_quantize(name):
            for i in range(2):
                round_on_vector(name, i, ALL_QUADS)
            for i in range(2):
                quantize_weight(name, i)

        load_scale_rows()
        nc.sync.dma_start(offs_sb[:], offs)
        nc.sync.dma_start(task_sb[:], task)
        load_weight("w2")
        load_words()
        for rows in (slice(0, GROUP), slice(QUADRANT, 2 * QUADRANT), slice(2 * QUADRANT, P)):
            nc.vector.memset(table_scales[rows, :].bitcast(I32), 0)
        nc.vector.memset(x_bytes[:].bitcast(I32), 0)
        gather_bytes()
        round_and_quantize("w2")
        load_weight("w1")
        load_mix(0)
        for name in ("w4", "w3"):
            load_weight(name)
        for t in range(1, PACK):
            load_mix(t)

        share = {
            (t, h): sbuf(
                "share%d_%d" % (t, h), [P, S // 2], F32, codes_at["w2"] + (2 * h + 1) * P * 4 if t == 0 else None
            )
            for t in range(PACK)
            for h in range(2)
        }
        for c in range(PACK):
            gather_words(c)

        z2_bf16 = sbuf("z2_bf16", [P, PACK * S], BF16)
        for c in range(PACK):
            hidden("w2", c, "A%d" % (c % 3), z2_bf16[:, c * PACK * P : (c + 1) * PACK * P])
        round_and_quantize("w1")
        shares_on_vector(0, slice(0, P))
        z2_codes = sbuf("z2_codes", [P, S], U32, raw_at["w1"])
        z2_scales = sbuf("z2_scales", [P, S], U8)
        quantize(z2_codes[:], z2_scales[:], z2_bf16[:])
        shares_on_scalar(0, slice(P, 2 * P))
        shares_on_scalar(0, HALVES[1])
        z_bf16 = sbuf("z_bf16", [P, PACK * S], BF16)
        for c in range(PACK):
            hidden("w1", c, "B%d" % (c % 3), z_bf16[:, c * PACK * P : (c + 1) * PACK * P])
        z_parts = {}

        def quantize_z(cols, at=None):
            width = cols.stop - cols.start
            codes = sbuf("z_codes%d" % cols.start, [P, width], U32, at)
            scales = sbuf("z_scales%d" % cols.start, [P, width], U8)
            quantize(codes[:], scales[:], z_bf16[:, PACK * cols.start : PACK * cols.stop])
            z_parts[cols.start, cols.stop] = codes, scales

        round_on_vector("w4", 0, ALL_QUADS)
        round_on_vector("w4", 1, slice(0, P // 2))
        quantize_weight("w4", 0)
        round_on_vector("w4", 1, slice(P // 2, P))
        quantize_z(HALVES[0])
        quantize_weight("w4", 1)
        quantize_z(slice(2 * P, 3 * P))

        minus_b = {}

        def second_alone(t, tag):
            minus_b[t] = bank("minus_b%d" % t, tag)
            product(minus_b[t][:], "w4", t, z2_codes[:], z2_scales[:], True, True)

        second_alone(1, "A2")
        b1_sb = sbuf("b1_sb", [P, S], F32)
        nc.scalar.copy(b1_sb[:], minus_b[1][:])
        round_on_vector("w3", 0, ALL_QUADS)
        round_on_vector("w3", 1, slice(0, P // 2))
        for t in range(2):
            quantize(
                w_codes["w3"][0][:, t * P : (t + 1) * P],
                w_scales["w3"][0][:, t * P : (t + 1) * P],
                w_bf16["w3"][0][:, t * PACK * P : (t + 1) * PACK * P],
            )
        round_on_vector("w3", 1, slice(P // 2, P))
        quantize_z(slice(3 * P, S), w3_pair0_at)
        quantize_weight("w3", 1)

        groups = [[(0, 0)], [(1, 0)], [(0, 1), (1, 1)], [(2, 0), (2, 1)], [(3, 0), (3, 1)]]
        diff = {}

        def second_net(group, tag):
            acc = bank("diff%d_%d" % group[0], tag)
            for i, (t, h) in enumerate(group):
                diff[t, h] = acc[:, HALVES[i]]
                product(diff[t, h], "w4", t, z2_codes[:, HALVES[h]], z2_scales[:, HALVES[h]], i == 0, False)

        def first_net(group):
            for t, h in group:
                for (lo, hi), (codes, scales) in z_parts.items():
                    if lo * 2 // S == h:
                        cols = slice(lo - HALVES[h].start, hi - HALVES[h].start)
                        last = (t, h) == group[-1] and hi == HALVES[h].stop
                        product(diff[t, h][:, cols], "w3", t, codes[:], scales[:], False, last)

        second_net(groups[0], "A0")
        second_net(groups[2], "A1")
        second_alone(0, "A3")
        second_net(groups[3], "B1")
        second_net(groups[1], "B0")
        for group in groups[:4]:
            first_net(group)

        on_gpsimd = {(1, 0): b1_sb[:, HALVES[0]], (1, 1): b1_sb[:, HALVES[1]]}
        for t in range(1, PACK):
            for h in range(2):
                shares_on_scalar(t, HALVES[h])

        scaled = [sbuf("scaled%d" % t, [P, S], F32) for t in range(PACK)]

        def scale(t, h):
            nc.vector.tensor_tensor(scaled[t][:, HALVES[h]], share[t, h][:], diff[t, h], ALU.mult)

        def finish(t, h):
            result = sbuf("result%d_%d" % (t, h), [P, S // 2], F32)
            if (t, h) in on_gpsimd:
                nc.gpsimd.tensor_tensor(result[:], scaled[t][:, HALVES[h]], on_gpsimd[t, h], ALU.subtract)
            else:
                nc.vector.tensor_tensor(result[:], scaled[t][:, HALVES[h]], minus_b[t][:, HALVES[h]], ALU.subtract)
            nc.sync.dma_start(out=out_rows[:, t, HALVES[h]], in_=result[:])

        for u, unit in enumerate([groups[0] + groups[1]] + groups[2:]):
            for t, h in unit:
                scale(t, h)
            if u == 0:
                second_alone(2, "A0")
                second_net(groups[4], "B0")
                first_net(groups[4])
            if u == 1:
                second_alone(3, "A1")
            for t, h in unit:
                finish(t, h)
